import numpy as np
import ml_dtypes


def mxq(x, axis, fmt="e4m3"):
    dtype, down = {"e4m3": (ml_dtypes.float8_e4m3fn, 7), "e5m2": (ml_dtypes.float8_e5m2, 14)}[fmt]
    v = np.moveaxis(np.asarray(x, np.float32).astype(ml_dtypes.bfloat16).astype(np.float64), axis, -1)
    blocks = v.reshape(v.shape[:-1] + (-1, 32))
    amax = np.abs(blocks).max(-1, keepdims=True)
    byte = np.maximum(np.where(amax > 0, np.frexp(amax)[1] - 1 + 127, 0) - down, 1)
    scale = np.exp2(byte - 127.0)
    codes = (blocks / scale).astype(np.float32).astype(dtype).astype(np.float64)
    return np.moveaxis((codes * scale).reshape(v.shape), -1, axis)


WIDE = False


def mx_kscale(k):
    if not WIDE:
        return np.ones(k)
    levels = np.array([10, -10, 5, -5, 0])
    if k % 512:
        return np.exp2(np.random.permutation(np.resize(levels, k // 32))).repeat(32)
    a = np.empty((k // 512, 16))
    for p in range(k // 512):
        a[p, :8] = np.random.permutation(np.resize(levels, 8))
        for g in range(8):
            far = levels[np.abs(levels - a[p, g]) >= 10]
            a[p, g + 8] = far[np.random.randint(len(far))]
    return np.exp2(a.ravel()).repeat(32)


def f64(x):
    return np.asarray(x).astype(np.float64)


def striped(idx):
    return np.tile(idx.reshape(-1, 16).T, (8, 1)).astype(np.uint16)


def unstriped(offs):
    return offs[:16].T.reshape(-1).astype(np.int64)


E2M1 = np.array([0.0, 0.5, 1.0, 1.5, 2.0, 3.0, 4.0, 6.0, -0.0, -0.5, -1.0, -1.5, -2.0, -3.0, -4.0, -6.0])


def pack_weight(w, fmt):
    k, n = w.shape
    w = f64(np.asarray(w, np.float32).astype(ml_dtypes.bfloat16)).reshape(k // 32, 32, n)
    amax = np.abs(w).max(1)
    if fmt == "e4m3":
        byte = np.frexp(amax)[1] - 1 + 127 - 7
    else:
        mant, ex = np.frexp(amax / 6.0)
        byte = np.where(mant > 0.5, ex, ex - 1) + 127
    byte = np.clip(np.where(amax > 0, byte, 1), 1, 254)
    scaled = (w * np.exp2(127.0 - byte)[:, None, :]).reshape(k, n).astype(np.float32)
    by_word = np.ascontiguousarray(scaled.reshape(k // 512, 128, 4, n).transpose(0, 1, 3, 2))
    if fmt == "e4m3":
        words = by_word.astype(ml_dtypes.float8_e4m3fn).view(np.uint8)
    else:
        c = by_word.astype(ml_dtypes.float4_e2m1fn).view(np.uint8) & 0xF
        words = (c[..., 0::2] | (c[..., 1::2] << 4)).reshape(k // 512, 128, 2 * n)
    return np.ascontiguousarray(words), np.ascontiguousarray(byte.astype(np.uint8).reshape(k // 512, 16, n))


def unpack_weight(words, scales, fmt):
    g, _, n = scales.shape
    words = np.ascontiguousarray(words).reshape(g, 128, n, -1)
    if fmt == "e4m3":
        vals = words.view(ml_dtypes.float8_e4m3fn).astype(np.float64)
    else:
        nib = np.empty((g, 128, n, 4), np.uint8)
        nib[..., 0::2] = words & 0xF
        nib[..., 1::2] = words >> 4
        vals = E2M1[nib]
    vals = vals * np.repeat(np.exp2(scales.astype(np.float64) - 127.0), 8, axis=1)[..., None]
    return vals.transpose(0, 1, 3, 2).reshape(g * 512, n)


def gelu(v):
    return 0.5 * v * (1.0 + np.tanh(np.sqrt(2.0 / np.pi) * (v + 0.044715 * v**3)))


K, H, T, S, P = 1536, 1024, 2048, 1024, 512


def setup_inputs():
    n = np.random.standard_normal
    s = mx_kscale(K)[:, None]
    u = mx_kscale(H)[:, None]
    tab_words, tab_scales = pack_weight(n((K, T)) * s, "e4m3")
    w1_words, w1_scales = pack_weight(n((K, H)) / np.sqrt(K) / s, "e2m1")
    wt_words, wt_scales = pack_weight(1.5 * n((H, H)) / np.sqrt(H) / u, "e4m3")
    return {
        "tab_words": tab_words, "tab_scales": tab_scales,
        "offs": striped(np.random.permutation(T)[:S]),
        "pos1": striped(np.random.permutation(S)[:P]),
        "pos2": striped(np.random.permutation(S)[:P]),
        "w1_words": w1_words, "w1_scales": w1_scales,
        "gain": (np.exp(0.2 * n(H)) * u[:, 0]).astype(np.float32),
        "wg": (1.5 * n((H, H)) / np.sqrt(H) / u).astype(np.float32),
        "wt_words": wt_words, "wt_scales": wt_scales,
    }


def reference(tab_words, tab_scales, offs, pos1, pos2, w1_words, w1_scales,
              gain, wg, wt_words, wt_scales):
    v = unpack_weight(tab_words, tab_scales, "e4m3")[:, unstriped(offs)]
    w1 = unpack_weight(w1_words, w1_scales, "e2m1")
    wt = unpack_weight(wt_words, wt_scales, "e4m3")
    h = w1.T @ v
    lead = h[:, unstriped(pos1)]
    follow = h[:, unstriped(pos2)]
    act = 0.5 * lead * (1.0 + np.tanh(np.sqrt(2.0 / np.pi) * (lead + 0.044715 * lead ** 3)))
    x = mxq(f64(gain)[:, None] * act, 0, "e4m3")
    gate = 1.0 / (1.0 + np.exp(-(mxq(f64(wg), 0, "e4m3").T @ x)))
    answer = np.tanh(wt.T @ x)
    return follow + gate * (answer - follow)

@@ -1,0 +1,308 @@
+from contextlib import ExitStack
+
+import concourse.mybir as mybir
+from concourse.masks import make_identity
+
+K, H, T, S, M = 1536, 1024, 2048, 1024, 512
+P = 128
+BANK = 512
+PASSES_1 = K // 512
+PASSES_2 = H // 512
+ROW_TILES = H // P
+M_BLOCKS = M // P
+FLOPS = 2 * K * H * S + 2 * 2 * H * H * M
+
+F32 = mybir.dt.float32
+BF16 = mybir.dt.bfloat16
+I32 = mybir.dt.int32
+U32 = mybir.dt.uint32
+U16 = mybir.dt.uint16
+U8 = mybir.dt.uint8
+FP8X4 = mybir.dt.float8_e4m3fn_x4
+FP4X4 = mybir.dt.float4_e2m1fn_x4
+ACT = mybir.ActivationFunctionType
+ALU = mybir.AluOpType
+
+EARLY = 3
+CAST = "gpsimd"
+GAIN = "vector"
+GROUPS = [[0, 1], [2, 3], [4, 5], [6], [7]]
+
+
+def tile_list_fugue_imitation_gate_kernel(
+    tc, tab_words, tab_scales, offs, pos1, pos2, w1_words, w1_scales, gain, wg, wt_words, wt_scales, out
+):
+    nc = tc.nc
+    with ExitStack() as ctx:
+        keep = ctx.enter_context(tc.tile_pool(name="keep", bufs=1))
+        ring = ctx.enter_context(tc.tile_pool(name="ring", bufs=3))
+        psum = ctx.enter_context(tc.psum_pool(name="psum", bufs=1))
+
+        offs_sb = keep.tile([P, S // 16], U16, name="offs_sb")
+        pos1_sb = keep.tile([P, M // 16], U16, name="pos1_sb")
+        pos2_sb = keep.tile([P, M // 16], U16, name="pos2_sb")
+        tab_scale = keep.tile([P, T], U8, name="tab_scale", align_bytes=64)
+        w1_scale = keep.tile([P, PASSES_1, H], U8, name="w1_scale", align_bytes=64)
+        wt_scale = keep.tile([P, PASSES_2, H], U8, name="wt_scale", align_bytes=64)
+        v_scale = [keep.tile([P, S], U8, name=f"v_scale{a}", align_bytes=64) for a in range(PASSES_1)]
+        gain_rows = keep.tile([P, P], F32, name="gain_rows")
+        zero_col = keep.tile([P, 1], F32, name="zero_col")
+        zero_bias = keep.tile([P, 1], F32, name="zero_bias")
+        ident_f32 = keep.tile([P, P], F32, name="ident_f32")
+        ident_bf16 = keep.tile([P, P], BF16, name="ident_bf16")
+
+        nc.gpsimd.memset(tab_scale[:].bitcast(I32), 0)
+        nc.vector.memset(w1_scale[:].bitcast(I32), 0)
+        nc.vector.memset(zero_col[:], 0.0)
+        nc.vector.memset(gain_rows[:], 0.0)
+        for a in range(1, PASSES_1):
+            nc.vector.memset(v_scale[a][:].bitcast(I32), 0)
+        nc.vector.memset(wt_scale[:].bitcast(I32), 0)
+        nc.scalar.activation(zero_bias[:], zero_col[:], ACT.Gelu_apprx_tanh)
+
+        w1_i32 = w1_words.bitcast(I32)
+        w1_code = [keep.tile([P, PASSES_1, H], U8, name=f"w1_code{u}", align_bytes=64) for u in range(2)]
+        tab_code = [keep.tile([P, T], U32, name=f"tab_code{a}") for a in range(PASSES_1)]
+
+        def load_w1(u):
+            nc.sync.dma_start(
+                out=w1_code[u][:].bitcast(I32),
+                in_=w1_i32[:, :, 256 * u : 256 * (u + 1)].rearrange("a p c -> p a c"),
+            )
+
+        def load_tab(a):
+            nc.sync.dma_start(
+                out=tab_code[a][:].bitcast(I32),
+                in_=tab_words[a].rearrange("p t i -> p (t i)").bitcast(I32),
+            )
+
+        nc.sync.dma_start(offs_sb[:], offs)
+        for q in range(4):
+            nc.sync.dma_start(
+                out=tab_scale[32 * q : 32 * q + 4 * PASSES_1, :].bitcast(I32),
+                in_=tab_scales.bitcast(I32)[:, 4 * q : 4 * q + 4, :],
+            )
+        load_tab(0)
+        load_w1(0)
+        make_identity(nc, ident_f32[:])
+        for q in range(4):
+            nc.gpsimd.dma_start(
+                out=w1_scale[32 * q : 32 * q + 4, :, :].bitcast(I32),
+                in_=w1_scales.bitcast(I32)[:, 4 * q : 4 * q + 4, :].rearrange("a r c -> r a c"),
+            )
+        nc.gpsimd.dma_start(out=gain_rows[0:ROW_TILES, :], in_=gain.rearrange("(i p) -> i p", p=P))
+        make_identity(nc, ident_bf16[:])
+        load_tab(1)
+        load_tab(2)
+        load_w1(1)
+        nc.sync.dma_start(pos1_sb[:], pos1)
+        nc.sync.dma_start(pos2_sb[:], pos2)
+        chunks = [(b, u) for u in range(2) for b in range(PASSES_2)]
+        wg_raw = {}
+        for b, u in chunks:
+            wg_raw[b, u] = keep.tile([P, 4, BANK], F32, name=f"wg_raw{b}{u}")
+            nc.sync.dma_start(
+                out=wg_raw[b, u][:],
+                in_=wg[512 * b : 512 * (b + 1), BANK * u : BANK * (u + 1)].rearrange("(p j) n -> p j n", j=4),
+            )
+        wt_code = keep.tile([P, PASSES_2, H], U32, name="wt_code", align_bytes=64)
+        nc.sync.dma_start(
+            out=wt_code[:].bitcast(I32),
+            in_=wt_words.rearrange("a p c i -> p a (c i)").bitcast(I32),
+        )
+        for q in range(4):
+            nc.sync.dma_start(
+                out=wt_scale[32 * q : 32 * q + 4, :, :].bitcast(I32),
+                in_=wt_scales.bitcast(I32)[:, 4 * q : 4 * q + 4, :].rearrange("a r c -> r a c"),
+            )
+
+        gain_ps = psum.tile([P, BANK], F32, name="gain_ps", tag="turn", bufs=2)
+        nc.tensor.transpose(gain_ps[:, 0:P], gain_rows[:], ident_f32[:])
+        gain_col = keep.tile([P, ROW_TILES], F32, name="gain_col")
+        nc.scalar.copy(gain_col[:], gain_ps[:, 0:ROW_TILES])
+
+        nc.vector.tensor_copy(v_scale[0][:], tab_scale[:].indirect(offs_sb[:]))
+        for a in range(1, PASSES_1):
+            nc.scalar.dma_start(
+                out=v_scale[a][0:100, :].bitcast(I32), in_=v_scale[0][4 * a : 4 * a + 100, :].bitcast(I32)
+            )
+        v_code = [keep.tile([P, S], U32, name=f"v_code{a}", align_bytes=64) for a in range(PASSES_1)]
+        for a in range(PASSES_1 - 1):
+            nc.vector.tensor_copy(v_code[a][:], tab_code[a][:].indirect(offs_sb[:]))
+        for u in range(2):
+            nc.vector.tensor_copy(
+                v_code[-1][:, BANK * u : BANK * (u + 1)],
+                tab_code[-1][:].indirect(offs_sb[:, 32 * u : 32 * (u + 1)]),
+            )
+
+        def stage1_pass(acc, i, u, a):
+            cols = slice(BANK * u, BANK * (u + 1))
+            nc.tensor.matmul_mx(
+                out=acc[:],
+                lhsT=w1_code[i // 4][:, a, 256 * (i % 4) : 256 * (i % 4 + 1)].bitcast(FP4X4),
+                lhsT_scale=w1_scale[:, a, P * i : P * (i + 1)],
+                rhs=v_code[a][:, cols].bitcast(FP8X4),
+                rhs_scale=v_scale[a][:, cols],
+                start=(a == 0),
+                stop=(a == PASSES_1 - 1),
+            )
+
+        h = [keep.tile([P, S], F32, name=f"h{i}") for i in range(ROW_TILES)]
+        lead = keep.tile([P, ROW_TILES, M], F32, name="lead", tag="lead_follow")
+        x_rows = {}
+        x_turned = [keep.tile([P, M_BLOCKS, 2, P], F32, name=f"x_turned{b}") for b in range(PASSES_2)]
+        x_code = keep.tile([P, PASSES_2, M], U32, name="x_code", align_bytes=64)
+        x_scale = keep.tile([P, PASSES_2, M], U8, name="x_scale", align_bytes=64)
+        wg_code = {}
+        wg_scale = {}
+
+        def cast_wg(c):
+            b, u = chunks[c]
+            grouped = ring.tile([P, BANK, 4], BF16, name="wg_grouped", align_bytes=64)
+            for s in range(2):
+                cols = slice(256 * s, 256 * (s + 1))
+                src = wg_raw[b, u][:, :, cols].rearrange("p j n -> p n j")
+                if CAST == "gpsimd":
+                    nc.gpsimd.tensor_scalar(grouped[:, cols, :], src, 1.0, 0.0, ALU.mult, ALU.add)
+                else:
+                    nc.scalar.copy(grouped[:, cols, :], src)
+            wg_code[b, u] = keep.tile([P, BANK], U32, name=f"wg_code{b}{u}", align_bytes=64)
+            wg_scale[b, u] = keep.tile([P, BANK], U8, name=f"wg_scale{b}{u}", align_bytes=64)
+            nc.vector.quantize_mx(
+                out=wg_code[b, u][:].bitcast(FP8X4),
+                scales=wg_scale[b, u][:],
+                in_=grouped[:].rearrange("p n j -> p (n j)"),
+            )
+
+        def leader(i):
+            nc.vector.tensor_copy(lead[:, i, :], h[i][:].indirect(pos1_sb[:]))
+            act = ring.tile([P, M], F32, name="act")
+            nc.scalar.activation(act[:], lead[:, i, :], ACT.Gelu_apprx_tanh)
+            x_rows[i] = ring.tile([P, M], BF16, name="x_rows", bufs=4)
+            if GAIN == "vector":
+                nc.vector.tensor_scalar(x_rows[i][:], act[:], gain_col[:, i : i + 1], None, ALU.mult)
+            elif GAIN == "gpsimd":
+                nc.gpsimd.tensor_scalar(x_rows[i][:], act[:], gain_col[:, i : i + 1], 0.0, ALU.mult, ALU.add)
+            else:
+                nc.scalar.activation(x_rows[i][:], act[:], ACT.Copy, scale=gain_col[:, i : i + 1])
+
+        def turn_out(group):
+            n = len(group)
+            ps = psum.tile([P, M_BLOCKS, n, P], BF16, name="turn_out_ps", tag="turn", bufs=2)
+            for g, i in enumerate(group):
+                for mb in range(M_BLOCKS):
+                    nc.tensor.transpose(ps[:, mb, g, :], x_rows[i][:, P * mb : P * (mb + 1)], ident_bf16[:])
+            first = 32 * (group[0] % 4)
+            words = ps[:].rearrange("p mb g r -> p (mb g r)").bitcast(F32)
+            nc.scalar.copy(
+                x_turned[group[0] // 4][:, :, :, first : first + 32 * n],
+                words.rearrange("p (mb w u) -> p mb u w", mb=M_BLOCKS, u=2),
+            )
+
+        def turn_back(b, tag):
+            grouped = keep.tile([P, 4 * M], BF16, name=f"x_grouped{b}", tag=tag, align_bytes=64)
+            for half in range(2):
+                ps = psum.tile([P, 2, 2 * P], F32, name="turn_back_ps", tag="turn", bufs=2)
+                for mb in range(2):
+                    for u in range(2):
+                        nc.tensor.transpose(
+                            ps[:, u, P * mb : P * (mb + 1)], x_turned[b][:, 2 * half + mb, u, :], ident_f32[:]
+                        )
+                nc.scalar.copy(
+                    grouped[:].bitcast(F32)[:, BANK * half : BANK * (half + 1)].rearrange("p (m u) -> p m u", u=2),
+                    ps[:].rearrange("p u m -> p m u"),
+                )
+            nc.vector.quantize_mx(out=x_code[:, b, :].bitcast(FP8X4), scales=x_scale[:, b, :], in_=grouped[:])
+
+        acc = {}
+        for i in range(EARLY):
+            for u in range(2):
+                acc[i, u] = psum.tile([P, BANK], F32, name="acc", tag="acc", bufs=6)
+        for a in range(PASSES_1 - 1):
+            for i in range(EARLY):
+                for u in range(2):
+                    stage1_pass(acc[i, u], i, u, a)
+        for u in range(2):
+            for i in range(EARLY):
+                stage1_pass(acc[i, u], i, u, PASSES_1 - 1)
+                nc.scalar.copy(h[i][:, BANK * u : BANK * (u + 1)], acc[i, u][:])
+
+        ends = {g[-1]: g for g in GROUPS}
+        for i in range(ROW_TILES):
+            ahead = i + EARLY
+            if ahead < ROW_TILES:
+                for u in range(2):
+                    bank = psum.tile([P, BANK], F32, name="acc", tag="acc", bufs=6)
+                    for a in range(PASSES_1):
+                        stage1_pass(bank, ahead, u, a)
+                    nc.scalar.copy(h[ahead][:, BANK * u : BANK * (u + 1)], bank[:])
+            leader(i)
+            if i in ends:
+                turn_out(ends[i])
+            if i == 3:
+                turn_back(0, "x_grouped0")
+            if i % 2 == 1:
+                cast_wg(i // 2)
+
+        follow_a = keep.tile([P, 4, M], F32, name="follow_a", tag="lead_follow")
+        for i in range(4):
+            nc.vector.tensor_copy(follow_a[:, i, :], h[i][:].indirect(pos2_sb[:]))
+        turn_back(1, "x_follow")
+        follow_b = keep.tile([P, 4, M], F32, name="follow_b", tag="x_follow", align_bytes=64)
+        for i in range(4, ROW_TILES):
+            nc.vector.tensor_copy(follow_b[:, i - 4, :], h[i][:].indirect(pos2_sb[:]))
+
+        def follow(i):
+            return (follow_a if i < 4 else follow_b)[:, i % 4, :]
+
+        half_gate = {}
+        diff = {}
+        step = {}
+
+        def products(i):
+            u, cols = i // 4, slice(P * (i % 4), P * (i % 4 + 1))
+            a_ps = psum.tile([P, BANK], F32, name="acc", tag="acc", bufs=6)
+            for b in range(PASSES_2):
+                nc.tensor.matmul_mx(
+                    out=a_ps[:],
+                    lhsT=wt_code[:, b, P * i : P * (i + 1)].bitcast(FP8X4),
+                    lhsT_scale=wt_scale[:, b, P * i : P * (i + 1)],
+                    rhs=x_code[:, b, :].bitcast(FP8X4),
+                    rhs_scale=x_scale[:, b, :],
+                    start=(b == 0),
+                    stop=(b == PASSES_2 - 1),
+                )
+            g_ps = psum.tile([P, BANK], F32, name="acc", tag="acc", bufs=6)
+            for b in range(PASSES_2):
+                nc.tensor.matmul_mx(
+                    out=g_ps[:],
+                    lhsT=wg_code[b, u][:, cols].bitcast(FP8X4),
+                    lhsT_scale=wg_scale[b, u][:, cols],
+                    rhs=x_code[:, b, :].bitcast(FP8X4),
+                    rhs_scale=x_scale[:, b, :],
+                    start=(b == 0),
+                    stop=(b == PASSES_2 - 1),
+                )
+            answer = ring.tile([P, M], F32, name="answer")
+            nc.scalar.activation(answer[:], a_ps[:], ACT.Tanh, bias=zero_bias[:])
+            half_gate[i] = ring.tile([P, M], F32, name="half_gate")
+            nc.scalar.activation(half_gate[i][:], g_ps[:], ACT.Tanh, bias=zero_bias[:], scale=0.5)
+            diff[i] = ring.tile([P, M], F32, name="diff", bufs=2)
+            nc.vector.tensor_tensor(diff[i][:], answer[:], follow(i), ALU.subtract)
+
+        def gated(i):
+            step[i] = ring.tile([P, M], F32, name="step", bufs=2)
+            nc.vector.scalar_tensor_tensor(step[i][:], half_gate[i][:], 1.0, diff[i][:], ALU.add, ALU.mult)
+
+        def finish(i):
+            res = ring.tile([P, M], F32, name="res", bufs=4)
+            nc.vector.scalar_tensor_tensor(res[:], step[i][:], 0.5, follow(i), ALU.mult, ALU.add)
+            nc.sync.dma_start(out=out[P * i : P * (i + 1), :], in_=res[:])
+
+        for i in range(ROW_TILES + 2):
+            if i < ROW_TILES:
+                products(i)
+            if 1 <= i <= ROW_TILES:
+                gated(i - 1)
+            if i >= 2:
+                finish(i - 2)

@@ -23,10 +23,15 @@ FP4X4 = mybir.dt.float4_e2m1fn_x4
 ACT = mybir.ActivationFunctionType
 ALU = mybir.AluOpType
 
-EARLY = 3
-CAST = "gpsimd"
+EARLY = 4
+AHEAD = 2
+FREE = [3, 5]
+FIRST = [0, 1, 2]
+SECOND = [4, 6, 7]
+FUSED = []
+CAST = "scalar"
 GAIN = "vector"
-GROUPS = [[0, 1], [2, 3], [4, 5], [6], [7]]
+GROUPS = [[0, 1], [2, 3], [4, 5], [6, 7]]
 
 
 def tile_list_fugue_imitation_gate_kernel(
@@ -41,9 +46,8 @@ def tile_list_fugue_imitation_gate_kernel(
         offs_sb = keep.tile([P, S // 16], U16, name="offs_sb")
         pos1_sb = keep.tile([P, M // 16], U16, name="pos1_sb")
         pos2_sb = keep.tile([P, M // 16], U16, name="pos2_sb")
-        tab_scale = keep.tile([P, T], U8, name="tab_scale", align_bytes=64)
-        w1_scale = keep.tile([P, PASSES_1, H], U8, name="w1_scale", align_bytes=64)
-        wt_scale = keep.tile([P, PASSES_2, H], U8, name="wt_scale", align_bytes=64)
+        tab_scale = keep.tile([P, T], U8, name="tab_scale")
+        w1_scale = keep.tile([P, PASSES_1, H], U8, name="w1_scale", tag="scales", align_bytes=64)
         v_scale = [keep.tile([P, S], U8, name=f"v_scale{a}", align_bytes=64) for a in range(PASSES_1)]
         gain_rows = keep.tile([P, P], F32, name="gain_rows")
         zero_col = keep.tile([P, 1], F32, name="zero_col")
@@ -57,14 +61,20 @@ def tile_list_fugue_imitation_gate_kernel(
         nc.vector.memset(gain_rows[:], 0.0)
         for a in range(1, PASSES_1):
             nc.vector.memset(v_scale[a][:].bitcast(I32), 0)
-        nc.vector.memset(wt_scale[:].bitcast(I32), 0)
+        make_identity(nc, ident_f32[:])
+        make_identity(nc, ident_bf16[:])
         nc.scalar.activation(zero_bias[:], zero_col[:], ACT.Gelu_apprx_tanh)
 
         w1_i32 = w1_words.bitcast(I32)
-        w1_code = [keep.tile([P, PASSES_1, H], U8, name=f"w1_code{u}", align_bytes=64) for u in range(2)]
-        tab_code = [keep.tile([P, T], U32, name=f"tab_code{a}") for a in range(PASSES_1)]
+        w1_code = {}
+        tab_code = [
+            keep.tile([P, T], U32, name="tab_code0", tag="w1_code1", align_bytes=64),
+            keep.tile([P, T], U32, name="tab_code1", tag="wg_raw0"),
+            keep.tile([P, T], U32, name="tab_code2", tag="wg_raw1"),
+        ]
 
         def load_w1(u):
+            w1_code[u] = keep.tile([P, PASSES_1, H], U8, name=f"w1_code{u}", tag=f"w1_code{u}", align_bytes=64)
             nc.sync.dma_start(
                 out=w1_code[u][:].bitcast(I32),
                 in_=w1_i32[:, :, 256 * u : 256 * (u + 1)].rearrange("a p c -> p a c"),
@@ -77,56 +87,46 @@ def tile_list_fugue_imitation_gate_kernel(
             )
 
         nc.sync.dma_start(offs_sb[:], offs)
+        load_tab(0)
         for q in range(4):
             nc.sync.dma_start(
                 out=tab_scale[32 * q : 32 * q + 4 * PASSES_1, :].bitcast(I32),
                 in_=tab_scales.bitcast(I32)[:, 4 * q : 4 * q + 4, :],
             )
-        load_tab(0)
         load_w1(0)
-        make_identity(nc, ident_f32[:])
+        load_tab(1)
         for q in range(4):
-            nc.gpsimd.dma_start(
+            nc.sync.dma_start(
                 out=w1_scale[32 * q : 32 * q + 4, :, :].bitcast(I32),
                 in_=w1_scales.bitcast(I32)[:, 4 * q : 4 * q + 4, :].rearrange("a r c -> r a c"),
             )
-        nc.gpsimd.dma_start(out=gain_rows[0:ROW_TILES, :], in_=gain.rearrange("(i p) -> i p", p=P))
-        make_identity(nc, ident_bf16[:])
-        load_tab(1)
+        nc.scalar.dma_start(out=gain_rows[0:ROW_TILES, :], in_=gain.rearrange("(i p) -> i p", p=P))
         load_tab(2)
-        load_w1(1)
-        nc.sync.dma_start(pos1_sb[:], pos1)
-        nc.sync.dma_start(pos2_sb[:], pos2)
-        chunks = [(b, u) for u in range(2) for b in range(PASSES_2)]
-        wg_raw = {}
-        for b, u in chunks:
-            wg_raw[b, u] = keep.tile([P, 4, BANK], F32, name=f"wg_raw{b}{u}")
-            nc.sync.dma_start(
-                out=wg_raw[b, u][:],
-                in_=wg[512 * b : 512 * (b + 1), BANK * u : BANK * (u + 1)].rearrange("(p j) n -> p j n", j=4),
-            )
-        wt_code = keep.tile([P, PASSES_2, H], U32, name="wt_code", align_bytes=64)
-        nc.sync.dma_start(
-            out=wt_code[:].bitcast(I32),
-            in_=wt_words.rearrange("a p c i -> p a (c i)").bitcast(I32),
-        )
-        for q in range(4):
-            nc.sync.dma_start(
-                out=wt_scale[32 * q : 32 * q + 4, :, :].bitcast(I32),
-                in_=wt_scales.bitcast(I32)[:, 4 * q : 4 * q + 4, :].rearrange("a r c -> r a c"),
-            )
-
-        gain_ps = psum.tile([P, BANK], F32, name="gain_ps", tag="turn", bufs=2)
-        nc.tensor.transpose(gain_ps[:, 0:P], gain_rows[:], ident_f32[:])
-        gain_col = keep.tile([P, ROW_TILES], F32, name="gain_col")
-        nc.scalar.copy(gain_col[:], gain_ps[:, 0:ROW_TILES])
-
         nc.vector.tensor_copy(v_scale[0][:], tab_scale[:].indirect(offs_sb[:]))
         for a in range(1, PASSES_1):
             nc.scalar.dma_start(
                 out=v_scale[a][0:100, :].bitcast(I32), in_=v_scale[0][4 * a : 4 * a + 100, :].bitcast(I32)
             )
-        v_code = [keep.tile([P, S], U32, name=f"v_code{a}", align_bytes=64) for a in range(PASSES_1)]
+        nc.sync.dma_start(pos1_sb[:], pos1)
+        nc.sync.dma_start(pos2_sb[:], pos2)
+        chunks = [(b, u) for u in range(2) for b in range(PASSES_2)]
+        wg_raw = {}
+
+        def load_wg(c, tag, align):
+            b, u = chunks[c]
+            rows = wg[512 * b : 512 * (b + 1), :].rearrange("(p j) n -> p j n", j=4)
+            whole = keep.tile([P, 4, BANK], F32, name=f"wg_raw{c}", tag=tag, align_bytes=align)
+            nc.sync.dma_start(out=whole[:], in_=rows[:, :, BANK * u : BANK * (u + 1)])
+            for s in range(2):
+                wg_raw[c, s] = whole[:, :, 256 * s : 256 * (s + 1)]
+
+
+        gain_ps = psum.tile([P, BANK], F32, name="gain_ps", tag="bank", bufs=8)
+        nc.tensor.transpose(gain_ps[:, 0:P], gain_rows[:], ident_f32[:])
+        gain_col = keep.tile([P, ROW_TILES], F32, name="gain_col")
+        nc.scalar.copy(gain_col[:], gain_ps[:, 0:ROW_TILES])
+
+        v_code = [keep.tile([P, S], U32, name=f"v_code{a}", tag=f"v_code{a}", align_bytes=64) for a in range(PASSES_1)]
         for a in range(PASSES_1 - 1):
             nc.vector.tensor_copy(v_code[a][:], tab_code[a][:].indirect(offs_sb[:]))
         for u in range(2):
@@ -134,6 +134,9 @@ def tile_list_fugue_imitation_gate_kernel(
                 v_code[-1][:, BANK * u : BANK * (u + 1)],
                 tab_code[-1][:].indirect(offs_sb[:, 32 * u : 32 * (u + 1)]),
             )
+        load_w1(1)
+        load_wg(0, "wg_raw0", None)
+        load_wg(1, "wg_raw1", None)
 
         def stage1_pass(acc, i, u, a):
             cols = slice(BANK * u, BANK * (u + 1))
@@ -147,8 +150,6 @@ def tile_list_fugue_imitation_gate_kernel(
                 stop=(a == PASSES_1 - 1),
             )
 
-        h = [keep.tile([P, S], F32, name=f"h{i}") for i in range(ROW_TILES)]
-        lead = keep.tile([P, ROW_TILES, M], F32, name="lead", tag="lead_follow")
         x_rows = {}
         x_turned = [keep.tile([P, M_BLOCKS, 2, P], F32, name=f"x_turned{b}") for b in range(PASSES_2)]
         x_code = keep.tile([P, PASSES_2, M], U32, name="x_code", align_bytes=64)
@@ -161,11 +162,12 @@ def tile_list_fugue_imitation_gate_kernel(
             grouped = ring.tile([P, BANK, 4], BF16, name="wg_grouped", align_bytes=64)
             for s in range(2):
                 cols = slice(256 * s, 256 * (s + 1))
-                src = wg_raw[b, u][:, :, cols].rearrange("p j n -> p n j")
-                if CAST == "gpsimd":
-                    nc.gpsimd.tensor_scalar(grouped[:, cols, :], src, 1.0, 0.0, ALU.mult, ALU.add)
+                src = wg_raw[c, s].rearrange("p j (n i) -> p n j i", i=4)
+                dst = grouped[:, cols, :].rearrange("p (n i) j -> p n j i", i=4)
+                if c in []:
+                    nc.vector.tensor_copy(dst, src)
                 else:
-                    nc.scalar.copy(grouped[:, cols, :], src)
+                    nc.scalar.copy(dst, src)
             wg_code[b, u] = keep.tile([P, BANK], U32, name=f"wg_code{b}{u}", align_bytes=64)
             wg_scale[b, u] = keep.tile([P, BANK], U8, name=f"wg_scale{b}{u}", align_bytes=64)
             nc.vector.quantize_mx(
@@ -178,7 +180,7 @@ def tile_list_fugue_imitation_gate_kernel(
             nc.vector.tensor_copy(lead[:, i, :], h[i][:].indirect(pos1_sb[:]))
             act = ring.tile([P, M], F32, name="act")
             nc.scalar.activation(act[:], lead[:, i, :], ACT.Gelu_apprx_tanh)
-            x_rows[i] = ring.tile([P, M], BF16, name="x_rows", bufs=4)
+            x_rows[i] = ring.tile([P, M], BF16, name="x_rows", bufs=8)
             if GAIN == "vector":
                 nc.vector.tensor_scalar(x_rows[i][:], act[:], gain_col[:, i : i + 1], None, ALU.mult)
             elif GAIN == "gpsimd":
@@ -188,7 +190,7 @@ def tile_list_fugue_imitation_gate_kernel(
 
         def turn_out(group):
             n = len(group)
-            ps = psum.tile([P, M_BLOCKS, n, P], BF16, name="turn_out_ps", tag="turn", bufs=2)
+            ps = psum.tile([P, M_BLOCKS, n, P], BF16, name="turn_out_ps", tag="bank", bufs=8)
             for g, i in enumerate(group):
                 for mb in range(M_BLOCKS):
                     nc.tensor.transpose(ps[:, mb, g, :], x_rows[i][:, P * mb : P * (mb + 1)], ident_bf16[:])
@@ -202,7 +204,7 @@ def tile_list_fugue_imitation_gate_kernel(
         def turn_back(b, tag):
             grouped = keep.tile([P, 4 * M], BF16, name=f"x_grouped{b}", tag=tag, align_bytes=64)
             for half in range(2):
-                ps = psum.tile([P, 2, 2 * P], F32, name="turn_back_ps", tag="turn", bufs=2)
+                ps = psum.tile([P, 2, 2 * P], F32, name="turn_back_ps", tag="bank", bufs=8)
                 for mb in range(2):
                     for u in range(2):
                         nc.tensor.transpose(
@@ -215,53 +217,81 @@ def tile_list_fugue_imitation_gate_kernel(
             nc.vector.quantize_mx(out=x_code[:, b, :].bitcast(FP8X4), scales=x_scale[:, b, :], in_=grouped[:])
 
         acc = {}
-        for i in range(EARLY):
+
+        def open_rows(i):
             for u in range(2):
-                acc[i, u] = psum.tile([P, BANK], F32, name="acc", tag="acc", bufs=6)
-        for a in range(PASSES_1 - 1):
-            for i in range(EARLY):
-                for u in range(2):
-                    stage1_pass(acc[i, u], i, u, a)
-        for u in range(2):
-            for i in range(EARLY):
-                stage1_pass(acc[i, u], i, u, PASSES_1 - 1)
+                acc[i, u] = psum.tile([P, BANK], F32, name="acc", tag="bank", bufs=8)
+
+        def keep_rows(i):
+            for u in range(2):
                 nc.scalar.copy(h[i][:, BANK * u : BANK * (u + 1)], acc[i, u][:])
 
-        ends = {g[-1]: g for g in GROUPS}
-        for i in range(ROW_TILES):
-            ahead = i + EARLY
-            if ahead < ROW_TILES:
+        for i in range(EARLY):
+            open_rows(i)
+        for i in range(EARLY):
+            for u in range(2):
+                stage1_pass(acc[i, u], i, u, 0)
+        for i in range(EARLY):
+            for a in range(1, PASSES_1):
                 for u in range(2):
-                    bank = psum.tile([P, BANK], F32, name="acc", tag="acc", bufs=6)
+                    stage1_pass(acc[i, u], i, u, a)
+        h = [keep.tile([P, S], F32, name=f"h{i}", tag=f"h{i}") for i in range(ROW_TILES)]
+        lead = keep.tile([P, ROW_TILES, M], F32, name="lead", tag="lead_follow")
+        followers = {}
+
+        def follower(i, dst):
+            nc.vector.tensor_copy(dst, h[i][:].indirect(pos2_sb[:]))
+            followers[i] = dst
+
+        for i in range(AHEAD):
+            keep_rows(i)
+        for i in range(ROW_TILES):
+            if i + EARLY < ROW_TILES:
+                open_rows(i + EARLY)
+                for u in range(2):
                     for a in range(PASSES_1):
-                        stage1_pass(bank, ahead, u, a)
-                    nc.scalar.copy(h[ahead][:, BANK * u : BANK * (u + 1)], bank[:])
+                        stage1_pass(acc[i + EARLY, u], i + EARLY, u, a)
+            if i + AHEAD < ROW_TILES:
+                keep_rows(i + AHEAD)
             leader(i)
-            if i in ends:
-                turn_out(ends[i])
-            if i == 3:
-                turn_back(0, "x_grouped0")
-            if i % 2 == 1:
-                cast_wg(i // 2)
-
-        follow_a = keep.tile([P, 4, M], F32, name="follow_a", tag="lead_follow")
-        for i in range(4):
-            nc.vector.tensor_copy(follow_a[:, i, :], h[i][:].indirect(pos2_sb[:]))
+            if i in FREE:
+                follower(i, keep.tile([P, M], F32, name=f"follow{i}")[:])
+        wt_code = keep.tile([P, PASSES_2, H], U32, name="wt_code", tag="v_code2", align_bytes=64)
+        nc.sync.dma_start(
+            out=wt_code[:].bitcast(I32),
+            in_=wt_words.rearrange("a p c i -> p a (c i)").bitcast(I32),
+        )
+        load_wg(2, "v_code0", 64)
+        load_wg(3, "v_code1", 64)
+        wt_scale = keep.tile([P, PASSES_2, H], U8, name="wt_scale", tag="scales", align_bytes=64)
+        nc.gpsimd.memset(wt_scale[:].bitcast(I32), 0)
+        for q in range(4):
+            nc.sync.dma_start(
+                out=wt_scale[32 * q : 32 * q + 4, :, :].bitcast(I32),
+                in_=wt_scales.bitcast(I32)[:, 4 * q : 4 * q + 4, :].rearrange("a r c -> r a c"),
+            )
+        for group in GROUPS:
+            turn_out(group)
+        turn_back(0, "x_grouped0")
+        follow_a = keep.tile([P, len(FIRST), M], F32, name="follow_a", tag="lead_follow")
+        for k, i in enumerate(FIRST):
+            follower(i, follow_a[:, k, :])
         turn_back(1, "x_follow")
-        follow_b = keep.tile([P, 4, M], F32, name="follow_b", tag="x_follow", align_bytes=64)
-        for i in range(4, ROW_TILES):
-            nc.vector.tensor_copy(follow_b[:, i - 4, :], h[i][:].indirect(pos2_sb[:]))
+        cast_wg(0)
+        cast_wg(1)
+        if SECOND:
+            follow_b = keep.tile([P, len(SECOND), M], F32, name="follow_b", tag="x_follow", align_bytes=64)
+            for k, i in enumerate(SECOND):
+                follower(i, follow_b[:, k, :])
 
-        def follow(i):
-            return (follow_a if i < 4 else follow_b)[:, i % 4, :]
-
+        answers = {}
         half_gate = {}
         diff = {}
         step = {}
 
         def products(i):
             u, cols = i // 4, slice(P * (i % 4), P * (i % 4 + 1))
-            a_ps = psum.tile([P, BANK], F32, name="acc", tag="acc", bufs=6)
+            a_ps = psum.tile([P, BANK], F32, name="acc", tag="bank", bufs=8)
             for b in range(PASSES_2):
                 nc.tensor.matmul_mx(
                     out=a_ps[:],
@@ -272,7 +302,7 @@ def tile_list_fugue_imitation_gate_kernel(
                     start=(b == 0),
                     stop=(b == PASSES_2 - 1),
                 )
-            g_ps = psum.tile([P, BANK], F32, name="acc", tag="acc", bufs=6)
+            g_ps = psum.tile([P, BANK], F32, name="acc", tag="bank", bufs=8)
             for b in range(PASSES_2):
                 nc.tensor.matmul_mx(
                     out=g_ps[:],
@@ -283,25 +313,35 @@ def tile_list_fugue_imitation_gate_kernel(
                     start=(b == 0),
                     stop=(b == PASSES_2 - 1),
                 )
-            answer = ring.tile([P, M], F32, name="answer")
-            nc.scalar.activation(answer[:], a_ps[:], ACT.Tanh, bias=zero_bias[:])
+            sign = -1.0 if i in FUSED else 1.0
+            answers[i] = ring.tile([P, M], F32, name="answer", bufs=4)
+            nc.scalar.activation(answers[i][:], a_ps[:], ACT.Tanh, bias=zero_bias[:])
             half_gate[i] = ring.tile([P, M], F32, name="half_gate")
-            nc.scalar.activation(half_gate[i][:], g_ps[:], ACT.Tanh, bias=zero_bias[:], scale=0.5)
+            nc.scalar.activation(half_gate[i][:], g_ps[:], ACT.Tanh, bias=zero_bias[:], scale=0.5 * sign)
             diff[i] = ring.tile([P, M], F32, name="diff", bufs=2)
-            nc.vector.tensor_tensor(diff[i][:], answer[:], follow(i), ALU.subtract)
+            if i in FUSED:
+                nc.vector.tensor_tensor(diff[i][:], h[i][:].indirect(pos2_sb[:]), answers[i][:], ALU.subtract)
+            else:
+                nc.vector.tensor_tensor(diff[i][:], answers[i][:], followers[i], ALU.subtract)
 
         def gated(i):
             step[i] = ring.tile([P, M], F32, name="step", bufs=2)
             nc.vector.scalar_tensor_tensor(step[i][:], half_gate[i][:], 1.0, diff[i][:], ALU.add, ALU.mult)
 
         def finish(i):
-            res = ring.tile([P, M], F32, name="res", bufs=4)
-            nc.vector.scalar_tensor_tensor(res[:], step[i][:], 0.5, follow(i), ALU.mult, ALU.add)
-            nc.sync.dma_start(out=out[P * i : P * (i + 1), :], in_=res[:])
+            res = ring.tile([P, M], F32, name="res", bufs=3)
+            base = answers[i][:] if i in FUSED else followers[i]
+            parts = 2 if i == ROW_TILES - 1 else 1
+            for k in range(parts):
+                cols = slice(M // parts * k, M // parts * (k + 1))
+                nc.vector.scalar_tensor_tensor(res[:, cols], step[i][:, cols], 0.5, base[:, cols], ALU.mult, ALU.add)
+                nc.sync.dma_start(out=out[P * i : P * (i + 1), cols], in_=res[:, cols])
 
         for i in range(ROW_TILES + 2):
             if i < ROW_TILES:
                 products(i)
+            if i in (1, 2):
+                cast_wg(i + 1)
             if 1 <= i <= ROW_TILES:
                 gated(i - 1)
             if i >= 2:

@@ -27,8 +27,8 @@ EARLY = 4
 AHEAD = 2
 FREE = [3, 5]
 FIRST = [0, 1, 2]
-SECOND = [4, 6, 7]
-FUSED = []
+SECOND = [4]
+FUSED = [6, 7]
 CAST = "scalar"
 GAIN = "vector"
 GROUPS = [[0, 1], [2, 3], [4, 5], [6, 7]]
@@ -105,7 +105,7 @@ def tile_list_fugue_imitation_gate_kernel(
         nc.vector.tensor_copy(v_scale[0][:], tab_scale[:].indirect(offs_sb[:]))
         for a in range(1, PASSES_1):
             nc.scalar.dma_start(
-                out=v_scale[a][0:100, :].bitcast(I32), in_=v_scale[0][4 * a : 4 * a + 100, :].bitcast(I32)
+                out=v_scale[a][0:112, :].bitcast(I32), in_=v_scale[0][4 * a : 4 * a + 112, :].bitcast(I32)
             )
         nc.sync.dma_start(pos1_sb[:], pos1)
         nc.sync.dma_start(pos2_sb[:], pos2)

@@ -25,10 +25,10 @@ ALU = mybir.AluOpType
 
 EARLY = 4
 AHEAD = 2
-FREE = [3, 5]
+FREE = []
 FIRST = [0, 1, 2]
-SECOND = [4]
-FUSED = [6, 7]
+SECOND = [3, 4]
+FUSED = [5, 6, 7]
 CAST = "scalar"
 GAIN = "vector"
 GROUPS = [[0, 1], [2, 3], [4, 5], [6, 7]]
@@ -164,7 +164,7 @@ def tile_list_fugue_imitation_gate_kernel(
                 cols = slice(256 * s, 256 * (s + 1))
                 src = wg_raw[c, s].rearrange("p j (n i) -> p n j i", i=4)
                 dst = grouped[:, cols, :].rearrange("p (n i) j -> p n j i", i=4)
-                if c in []:
+                if c in [0, 1]:
                     nc.vector.tensor_copy(dst, src)
                 else:
                     nc.scalar.copy(dst, src)
@@ -254,6 +254,8 @@ def tile_list_fugue_imitation_gate_kernel(
             if i + AHEAD < ROW_TILES:
                 keep_rows(i + AHEAD)
             leader(i)
+            if i in (2, 4):
+                cast_wg(i // 2 - 1)
             if i in FREE:
                 follower(i, keep.tile([P, M], F32, name=f"follow{i}")[:])
         wt_code = keep.tile([P, PASSES_2, H], U32, name="wt_code", tag="v_code2", align_bytes=64)
@@ -277,8 +279,6 @@ def tile_list_fugue_imitation_gate_kernel(
         for k, i in enumerate(FIRST):
             follower(i, follow_a[:, k, :])
         turn_back(1, "x_follow")
-        cast_wg(0)
-        cast_wg(1)
         if SECOND:
             follow_b = keep.tile([P, len(SECOND), M], F32, name="follow_b", tag="x_follow", align_bytes=64)
             for k, i in enumerate(SECOND):

@@ -6,10 +6,10 @@ from concourse.masks import make_identity
 K, H, T, S, M = 1536, 1024, 2048, 1024, 512
 P = 128
 BANK = 512
+HALF = M // 2
 PASSES_1 = K // 512
 PASSES_2 = H // 512
 ROW_TILES = H // P
-M_BLOCKS = M // P
 FLOPS = 2 * K * H * S + 2 * 2 * H * H * M
 
 F32 = mybir.dt.float32
@@ -24,14 +24,14 @@ ACT = mybir.ActivationFunctionType
 ALU = mybir.AluOpType
 
 EARLY = 4
-AHEAD = 2
-FREE = []
-FIRST = [0, 1, 2]
-SECOND = [3, 4]
-FUSED = [5, 6, 7]
-CAST = "scalar"
-GAIN = "vector"
-GROUPS = [[0, 1], [2, 3], [4, 5], [6, 7]]
+SHIFT_ROWS = 100
+GROUPS = [[[0, 1], [2, 3], [4, 5], [6], [7]], [[0, 1], [2, 3], [4, 5], [6, 7]]]
+CAST = ["gpsimd"] * 4
+LOW, HIGH, ALL = slice(0, HALF), slice(HALF, M), slice(0, M)
+UNITS = [[(2 * j, cols), (2 * j + 1, cols)] for cols in (LOW, HIGH) for j in range(4)]
+CAST_TAG = ["wg_pair0", "wg_pair1"]
+CODE_TAG = ["act7_0", "x_grouped10"]
+PIECES = [1, 1, 1, 1]
 
 
 def tile_list_fugue_imitation_gate_kernel(
@@ -43,38 +43,35 @@ def tile_list_fugue_imitation_gate_kernel(
         ring = ctx.enter_context(tc.tile_pool(name="ring", bufs=3))
         psum = ctx.enter_context(tc.psum_pool(name="psum", bufs=1))
 
+        def bank(shape, dtype):
+            return psum.tile(shape, dtype, name="bank", tag="bank", bufs=8)
+
         offs_sb = keep.tile([P, S // 16], U16, name="offs_sb")
         pos1_sb = keep.tile([P, M // 16], U16, name="pos1_sb")
         pos2_sb = keep.tile([P, M // 16], U16, name="pos2_sb")
-        tab_scale = keep.tile([P, T], U8, name="tab_scale")
-        w1_scale = keep.tile([P, PASSES_1, H], U8, name="w1_scale", tag="scales", align_bytes=64)
+        tab_scale = keep.tile([P, T], U8, name="tab_scale", tag="tab_scale", align_bytes=64)
+        w1_scale = keep.tile([P, PASSES_1, H], U8, name="w1_scale", align_bytes=64)
+        wt_scale = keep.tile([P, PASSES_2, H], U8, name="wt_scale", align_bytes=64)
         v_scale = [keep.tile([P, S], U8, name=f"v_scale{a}", align_bytes=64) for a in range(PASSES_1)]
         gain_rows = keep.tile([P, P], F32, name="gain_rows")
         zero_col = keep.tile([P, 1], F32, name="zero_col")
         zero_bias = keep.tile([P, 1], F32, name="zero_bias")
-        ident_f32 = keep.tile([P, P], F32, name="ident_f32")
-        ident_bf16 = keep.tile([P, P], BF16, name="ident_bf16")
+        ident = keep.tile([P, P], F32, name="ident")
 
-        nc.gpsimd.memset(tab_scale[:].bitcast(I32), 0)
-        nc.vector.memset(w1_scale[:].bitcast(I32), 0)
+        nc.vector.memset(tab_scale[:].bitcast(I32), 0)
         nc.vector.memset(zero_col[:], 0.0)
-        nc.vector.memset(gain_rows[:], 0.0)
-        for a in range(1, PASSES_1):
-            nc.vector.memset(v_scale[a][:].bitcast(I32), 0)
-        make_identity(nc, ident_f32[:])
+        for rows in (slice(0, 24), slice(32, 64), slice(64, P)):
+            nc.vector.memset(gain_rows[rows, :].bitcast(I32), 0)
+        nc.gpsimd.dma_start(out=gain_rows[24:32, :], in_=gain.rearrange("(i p) -> i p", p=P))
+        make_identity(nc, ident[:])
+        ident_bf16 = keep.tile([P, P], BF16, name="ident_bf16")
         make_identity(nc, ident_bf16[:])
-        nc.scalar.activation(zero_bias[:], zero_col[:], ACT.Gelu_apprx_tanh)
 
         w1_i32 = w1_words.bitcast(I32)
-        w1_code = {}
-        tab_code = [
-            keep.tile([P, T], U32, name="tab_code0", tag="w1_code1", align_bytes=64),
-            keep.tile([P, T], U32, name="tab_code1", tag="wg_raw0"),
-            keep.tile([P, T], U32, name="tab_code2", tag="wg_raw1"),
-        ]
+        w1_code = [keep.tile([P, PASSES_1, H], U8, name=f"w1_code{u}", tag=f"w1_code{u}", align_bytes=64) for u in range(2)]
+        tab_code = [keep.tile([P, T], U32, name=f"tab_code{a}", tag=f"big{a}", align_bytes=64) for a in range(PASSES_1)]
 
         def load_w1(u):
-            w1_code[u] = keep.tile([P, PASSES_1, H], U8, name=f"w1_code{u}", tag=f"w1_code{u}", align_bytes=64)
             nc.sync.dma_start(
                 out=w1_code[u][:].bitcast(I32),
                 in_=w1_i32[:, :, 256 * u : 256 * (u + 1)].rearrange("a p c -> p a c"),
@@ -86,263 +83,334 @@ def tile_list_fugue_imitation_gate_kernel(
                 in_=tab_words[a].rearrange("p t i -> p (t i)").bitcast(I32),
             )
 
+        def load_scale_rows(queues, plane, rows):
+            for q in range(4):
+                queues[q].dma_start(
+                    out=plane[32 * q : 32 * q + 4, :, :].bitcast(I32),
+                    in_=rows.bitcast(I32)[:, 4 * q : 4 * q + 4, :].rearrange("a r c -> r a c"),
+                )
+
+        tab_rows = tab_scales.bitcast(I32)
         nc.sync.dma_start(offs_sb[:], offs)
+        load_scale_rows([nc.scalar, nc.scalar, nc.sync, nc.sync], w1_scale, w1_scales)
         load_tab(0)
         for q in range(4):
-            nc.sync.dma_start(
-                out=tab_scale[32 * q : 32 * q + 4 * PASSES_1, :].bitcast(I32),
-                in_=tab_scales.bitcast(I32)[:, 4 * q : 4 * q + 4, :],
-            )
+            nc.sync.dma_start(out=tab_scale[32 * q : 32 * q + 8, :].bitcast(I32), in_=tab_rows[0:2, 4 * q : 4 * q + 4, :])
+        nc.sync.dma_start(out=tab_scale[16:32, :].bitcast(I32), in_=tab_rows[2])
+        nc.scalar.activation(zero_bias[:], zero_col[:], ACT.Gelu_apprx_tanh)
+        ps = bank([P, BANK], F32)
+        nc.tensor.transpose(ps[:, 0:P], gain_rows[:], ident[:])
+        gain_col = keep.tile([P, ROW_TILES], F32, name="gain_col")
+        nc.scalar.copy(gain_col[:], ps[:, 24:32])
+        gain_all = keep.tile([P, H], F32, name="gain_all")
+        for b in range(PASSES_2):
+            ps = bank([P, BANK], F32)
+            for k in range(4):
+                i = 4 * b + k
+                nc.tensor.transpose(ps[:, P * k : P * (k + 1)], gain_col[:, i : i + 1].to_broadcast([P, P]), ident[:])
+            nc.scalar.copy(gain_all[:, BANK * b : BANK * (b + 1)], ps[:])
+
+
         load_w1(0)
         load_tab(1)
-        for q in range(4):
-            nc.sync.dma_start(
-                out=w1_scale[32 * q : 32 * q + 4, :, :].bitcast(I32),
-                in_=w1_scales.bitcast(I32)[:, 4 * q : 4 * q + 4, :].rearrange("a r c -> r a c"),
-            )
-        nc.scalar.dma_start(out=gain_rows[0:ROW_TILES, :], in_=gain.rearrange("(i p) -> i p", p=P))
         load_tab(2)
-        nc.vector.tensor_copy(v_scale[0][:], tab_scale[:].indirect(offs_sb[:]))
-        for a in range(1, PASSES_1):
-            nc.scalar.dma_start(
-                out=v_scale[a][0:112, :].bitcast(I32), in_=v_scale[0][4 * a : 4 * a + 112, :].bitcast(I32)
-            )
+        load_w1(1)
         nc.sync.dma_start(pos1_sb[:], pos1)
         nc.sync.dma_start(pos2_sb[:], pos2)
-        chunks = [(b, u) for u in range(2) for b in range(PASSES_2)]
-        wg_raw = {}
 
-        def load_wg(c, tag, align):
-            b, u = chunks[c]
-            rows = wg[512 * b : 512 * (b + 1), :].rearrange("(p j) n -> p j n", j=4)
-            whole = keep.tile([P, 4, BANK], F32, name=f"wg_raw{c}", tag=tag, align_bytes=align)
-            nc.sync.dma_start(out=whole[:], in_=rows[:, :, BANK * u : BANK * (u + 1)])
-            for s in range(2):
-                wg_raw[c, s] = whole[:, :, 256 * s : 256 * (s + 1)]
+        v_code = {}
 
+        def gather_words(a, u, tag):
+            v_code[a, u] = keep.tile([P, BANK], U32, name=f"v_code{a}{u}", tag=tag, align_bytes=64)
+            nc.vector.tensor_copy(v_code[a, u][:], tab_code[a][:].indirect(offs_sb[:, 32 * u : 32 * (u + 1)]))
 
-        gain_ps = psum.tile([P, BANK], F32, name="gain_ps", tag="bank", bufs=8)
-        nc.tensor.transpose(gain_ps[:, 0:P], gain_rows[:], ident_f32[:])
-        gain_col = keep.tile([P, ROW_TILES], F32, name="gain_col")
-        nc.scalar.copy(gain_col[:], gain_ps[:, 0:ROW_TILES])
-
-        v_code = [keep.tile([P, S], U32, name=f"v_code{a}", tag=f"v_code{a}", align_bytes=64) for a in range(PASSES_1)]
-        for a in range(PASSES_1 - 1):
-            nc.vector.tensor_copy(v_code[a][:], tab_code[a][:].indirect(offs_sb[:]))
+        gather_words(0, 0, "v_code00")
         for u in range(2):
             nc.vector.tensor_copy(
-                v_code[-1][:, BANK * u : BANK * (u + 1)],
-                tab_code[-1][:].indirect(offs_sb[:, 32 * u : 32 * (u + 1)]),
+                v_scale[0][:, BANK * u : BANK * (u + 1)], tab_scale[:].indirect(offs_sb[:, 32 * u : 32 * (u + 1)])
             )
-        load_w1(1)
-        load_wg(0, "wg_raw0", None)
-        load_wg(1, "wg_raw1", None)
+        for cols in [slice(0, BANK), slice(BANK, S)]:
+            nc.scalar.dma_start(
+                out=v_scale[1][0:SHIFT_ROWS, cols].bitcast(I32), in_=v_scale[0][4 : 4 + SHIFT_ROWS, cols].bitcast(I32)
+            )
+        for q in range(4):
+            nc.scalar.dma_start(
+                out=v_scale[2][32 * q : 32 * q + 4, :].bitcast(I32),
+                in_=v_scale[0][16 + 4 * q : 20 + 4 * q, :].bitcast(I32),
+            )
+        gather_words(0, 1, "tab_scale")
+        for a in range(1, PASSES_1):
+            for u in range(2):
+                gather_words(a, u, f"v_code{a}{u}")
 
-        def stage1_pass(acc, i, u, a):
+
+        chunks = [(b, u) for u in range(2) for b in range(PASSES_2)]
+        wg_raw = {}
+        wg_grouped = {}
+        wg_pair = {}
+        wg_code = {}
+        wg_scale = {}
+
+        def load_wg(c, tag, queue):
+            b, u = chunks[c]
+            rows = wg[512 * b : 512 * (b + 1), :].rearrange("(p j) n -> p j n", j=4)
+            wg_raw[c] = keep.tile([P, 4, BANK], F32, name=f"wg_raw{c}", tag=tag, align_bytes=64)
+            queue.dma_start(out=wg_raw[c][:], in_=rows[:, :, BANK * u : BANK * (u + 1)])
+
+        def cast_wg(c):
+            b, u = chunks[c]
+            if b == 0:
+                wg_pair[u] = keep.tile([P, PASSES_2, BANK, 4], BF16, name=f"wg_pair{u}", tag=CAST_TAG[u], align_bytes=64)
+            wg_grouped[c] = wg_pair[u][:, b, :, :]
+            for s in range(PIECES[c]):
+                cols = slice(BANK // PIECES[c] * s, BANK // PIECES[c] * (s + 1))
+                if CAST[c] == "gpsimd":
+                    nc.gpsimd.tensor_scalar(
+                        wg_grouped[c][:, cols, :], wg_raw[c][:, :, cols].rearrange("p j n -> p n j"),
+                        1.0, 0.0, ALU.mult, ALU.add,
+                    )
+                else:
+                    src = wg_raw[c][:, :, cols].rearrange("p j (n i) -> p n j i", i=4)
+                    dst = wg_grouped[c][:, cols, :].rearrange("p (n i) j -> p n j i", i=4)
+                    if CAST[c] == "vector":
+                        nc.vector.tensor_copy(dst, src)
+                    else:
+                        nc.scalar.copy(dst, src)
+
+        def quant_wg(u):
+            wg_code[u] = keep.tile([P, PASSES_2, BANK], U32, name=f"wg_code{u}", tag=CODE_TAG[u], align_bytes=64)
+            wg_scale[u] = keep.tile([P, PASSES_2, BANK], U8, name=f"wg_scale{u}", align_bytes=64)
+            nc.vector.quantize_mx(
+                out=wg_code[u][:].rearrange("p b n -> p (b n)").bitcast(FP8X4),
+                scales=wg_scale[u][:].rearrange("p b n -> p (b n)"),
+                in_=wg_pair[u][:].rearrange("p b n j -> p (b n j)"),
+            )
+
+        load_wg(0, "big0", nc.scalar)
+        load_wg(1, "big1", nc.scalar)
+        wt_code = keep.tile([P, PASSES_2, H], U32, name="wt_code", tag="big2", align_bytes=64)
+        nc.sync.dma_start(out=wt_code[:].bitcast(I32), in_=wt_words.rearrange("a p c i -> p a (c i)").bitcast(I32))
+        load_wg(2, "wg_raw2", nc.sync)
+        load_wg(3, "wg_raw3", nc.sync)
+        load_scale_rows([nc.sync] * 4, wt_scale, wt_scales)
+        for c in [0, 1, 2, 3]:
+            cast_wg(c)
+
+        acc = {}
+        h = [keep.tile([P, S], F32, name=f"h{i}") for i in range(ROW_TILES)]
+        lead = {}
+        x_turned = {}
+        x_code = [keep.tile([P, M], U32, name=f"x_code{b}", align_bytes=64) for b in range(PASSES_2)]
+        x_scale = [keep.tile([P, M], U8, name=f"x_scale{b}", align_bytes=64) for b in range(PASSES_2)]
+
+        def stage1_pass(i, u, a):
             cols = slice(BANK * u, BANK * (u + 1))
             nc.tensor.matmul_mx(
-                out=acc[:],
+                out=acc[i, u][:],
                 lhsT=w1_code[i // 4][:, a, 256 * (i % 4) : 256 * (i % 4 + 1)].bitcast(FP4X4),
                 lhsT_scale=w1_scale[:, a, P * i : P * (i + 1)],
-                rhs=v_code[a][:, cols].bitcast(FP8X4),
+                rhs=v_code[a, u][:].bitcast(FP8X4),
                 rhs_scale=v_scale[a][:, cols],
                 start=(a == 0),
                 stop=(a == PASSES_1 - 1),
             )
 
-        x_rows = {}
-        x_turned = [keep.tile([P, M_BLOCKS, 2, P], F32, name=f"x_turned{b}") for b in range(PASSES_2)]
-        x_code = keep.tile([P, PASSES_2, M], U32, name="x_code", align_bytes=64)
-        x_scale = keep.tile([P, PASSES_2, M], U8, name="x_scale", align_bytes=64)
-        wg_code = {}
-        wg_scale = {}
-
-        def cast_wg(c):
-            b, u = chunks[c]
-            grouped = ring.tile([P, BANK, 4], BF16, name="wg_grouped", align_bytes=64)
-            for s in range(2):
-                cols = slice(256 * s, 256 * (s + 1))
-                src = wg_raw[c, s].rearrange("p j (n i) -> p n j i", i=4)
-                dst = grouped[:, cols, :].rearrange("p (n i) j -> p n j i", i=4)
-                if c in [0, 1]:
-                    nc.vector.tensor_copy(dst, src)
-                else:
-                    nc.scalar.copy(dst, src)
-            wg_code[b, u] = keep.tile([P, BANK], U32, name=f"wg_code{b}{u}", align_bytes=64)
-            wg_scale[b, u] = keep.tile([P, BANK], U8, name=f"wg_scale{b}{u}", align_bytes=64)
-            nc.vector.quantize_mx(
-                out=wg_code[b, u][:].bitcast(FP8X4),
-                scales=wg_scale[b, u][:],
-                in_=grouped[:].rearrange("p n j -> p (n j)"),
-            )
-
-        def leader(i):
-            nc.vector.tensor_copy(lead[:, i, :], h[i][:].indirect(pos1_sb[:]))
-            act = ring.tile([P, M], F32, name="act")
-            nc.scalar.activation(act[:], lead[:, i, :], ACT.Gelu_apprx_tanh)
-            x_rows[i] = ring.tile([P, M], BF16, name="x_rows", bufs=8)
-            if GAIN == "vector":
-                nc.vector.tensor_scalar(x_rows[i][:], act[:], gain_col[:, i : i + 1], None, ALU.mult)
-            elif GAIN == "gpsimd":
-                nc.gpsimd.tensor_scalar(x_rows[i][:], act[:], gain_col[:, i : i + 1], 0.0, ALU.mult, ALU.add)
+        def keep_rows(i, u):
+            if (i, u) in []:
+                nc.vector.tensor_copy(h[i][:, BANK * u : BANK * (u + 1)], acc[i, u][:])
             else:
-                nc.scalar.activation(x_rows[i][:], act[:], ACT.Copy, scale=gain_col[:, i : i + 1])
-
-        def turn_out(group):
-            n = len(group)
-            ps = psum.tile([P, M_BLOCKS, n, P], BF16, name="turn_out_ps", tag="bank", bufs=8)
-            for g, i in enumerate(group):
-                for mb in range(M_BLOCKS):
-                    nc.tensor.transpose(ps[:, mb, g, :], x_rows[i][:, P * mb : P * (mb + 1)], ident_bf16[:])
-            first = 32 * (group[0] % 4)
-            words = ps[:].rearrange("p mb g r -> p (mb g r)").bitcast(F32)
-            nc.scalar.copy(
-                x_turned[group[0] // 4][:, :, :, first : first + 32 * n],
-                words.rearrange("p (mb w u) -> p mb u w", mb=M_BLOCKS, u=2),
-            )
-
-        def turn_back(b, tag):
-            grouped = keep.tile([P, 4 * M], BF16, name=f"x_grouped{b}", tag=tag, align_bytes=64)
-            for half in range(2):
-                ps = psum.tile([P, 2, 2 * P], F32, name="turn_back_ps", tag="bank", bufs=8)
-                for mb in range(2):
-                    for u in range(2):
-                        nc.tensor.transpose(
-                            ps[:, u, P * mb : P * (mb + 1)], x_turned[b][:, 2 * half + mb, u, :], ident_f32[:]
-                        )
-                nc.scalar.copy(
-                    grouped[:].bitcast(F32)[:, BANK * half : BANK * (half + 1)].rearrange("p (m u) -> p m u", u=2),
-                    ps[:].rearrange("p u m -> p m u"),
-                )
-            nc.vector.quantize_mx(out=x_code[:, b, :].bitcast(FP8X4), scales=x_scale[:, b, :], in_=grouped[:])
-
-        acc = {}
-
-        def open_rows(i):
-            for u in range(2):
-                acc[i, u] = psum.tile([P, BANK], F32, name="acc", tag="bank", bufs=8)
-
-        def keep_rows(i):
-            for u in range(2):
                 nc.scalar.copy(h[i][:, BANK * u : BANK * (u + 1)], acc[i, u][:])
 
-        for i in range(EARLY):
-            open_rows(i)
+        def leader(i, halves):
+            if len(halves) == 2:
+                if i % 2 == 0:
+                    pair = keep.tile([P, 2, 2, HALF], F32, name=f"lead{i}")
+                    for hf in range(2):
+                        lead[i, hf] = pair[:, :, hf, :]
+                    lead[i, 2] = pair
+                dst = lead[i - i % 2, 2][:, i % 2, :, :].rearrange("p a m -> p (a m)")
+            else:
+                g = [g for g in GROUPS[halves[0]] if i in g][0]
+                if i == g[0]:
+                    tag = f"lead{i}_{halves[0]}"
+                    tile = keep.tile([P, len(g), HALF], F32, name=tag, tag={"act0_1": "w1_code1", "act2_1": "lead7_0", "act4_1": "x_turned10", "act6_1": "lead7_0", "lead6_1": "v_code21"}.get(tag, tag), align_bytes=64)
+                    lead[i, halves[0]] = tile[:]
+                dst = lead[g[0], halves[0]][:, i - g[0], :]
+            nc.vector.tensor_copy(dst, h[i][:].indirect(pos1_sb[:, 16 * halves[0] : 16 * (halves[-1] + 1)]))
+
+        def turn_out(g, hf):
+            n, b = len(g), g[0] // 4
+            tag = f"act{g[0]}_{hf}"
+            act = keep.tile([P, n, HALF], F32, name=tag, tag={"act0_1": "w1_code1", "act2_1": "lead7_0", "act4_1": "x_turned10", "act6_1": "lead7_0", "lead6_1": "v_code21"}.get(tag, tag), align_bytes=64)
+            nc.scalar.activation(act[:], lead[g[0], hf], ACT.Gelu_apprx_tanh)
+            if g[0] % 4 == 0:
+                tag = f"x_turned{b}{hf}"
+                x_turned[b, hf] = keep.tile([P, 2, BANK], BF16, name=tag, tag=tag, align_bytes=64)
+            first = P * (g[0] % 4)
+            dst = x_turned[b, hf][:, :, first : first + n * P]
+            if (g[0], hf) in [(0, 1), (2, 1), (4, 1), (6, 1)]:
+                rows = ring.tile([P, n, HALF], BF16, name="x_rows")
+                ps = bank([P, 2, n * P], BF16)
+                for k in range(n):
+                    nc.scalar.activation(rows[:, k, :], act[:, k, :], ACT.Copy, scale=gain_col[:, g[k] : g[k] + 1])
+                    for mb in range(2):
+                        nc.tensor.transpose(
+                            ps[:, mb, P * k : P * (k + 1)], rows[:, k, P * mb : P * (mb + 1)], ident_bf16[:]
+                        )
+                nc.scalar.copy(dst.bitcast(F32), ps[:].bitcast(F32))
+            else:
+                ps = bank([P, 2, n * P], F32)
+                for k in range(n):
+                    for mb in range(2):
+                        nc.tensor.transpose(ps[:, mb, P * k : P * (k + 1)], act[:, k, P * mb : P * (mb + 1)], ident[:])
+                nc.vector.tensor_tensor(
+                    dst, ps[:], gain_all[:, P * g[0] : P * (g[0] + n)].unsqueeze(1).to_broadcast([P, 2, n * P]), ALU.mult
+                )
+
+        def turn_back(b, hf):
+            words = x_turned[b, hf][:].rearrange("p mb r -> p (mb r)").bitcast(F32)
+            ps = bank([P, 2, HALF], F32)
+            for mb in range(2):
+                for u in range(2):
+                    nc.tensor.transpose(
+                        ps[:, u, P * mb : P * (mb + 1)], words[:, 256 * mb + u : 256 * (mb + 1) : 2], ident[:]
+                    )
+            tag = f"x_grouped{b}{hf}"
+            grouped = keep.tile([P, 4 * HALF], BF16, name=tag, tag=tag, align_bytes=64)
+            nc.scalar.copy(
+                grouped[:].bitcast(F32).rearrange("p (m u) -> p m u", u=2), ps[:].rearrange("p u m -> p m u")
+            )
+            cols = slice(HALF * hf, HALF * (hf + 1))
+            nc.vector.quantize_mx(out=x_code[b][:, cols].bitcast(FP8X4), scales=x_scale[b][:, cols], in_=grouped[:])
+
         for i in range(EARLY):
             for u in range(2):
-                stage1_pass(acc[i, u], i, u, 0)
-        for i in range(EARLY):
-            for a in range(1, PASSES_1):
-                for u in range(2):
-                    stage1_pass(acc[i, u], i, u, a)
-        h = [keep.tile([P, S], F32, name=f"h{i}", tag=f"h{i}") for i in range(ROW_TILES)]
-        lead = keep.tile([P, ROW_TILES, M], F32, name="lead", tag="lead_follow")
-        followers = {}
-
-        def follower(i, dst):
-            nc.vector.tensor_copy(dst, h[i][:].indirect(pos2_sb[:]))
-            followers[i] = dst
-
-        for i in range(AHEAD):
-            keep_rows(i)
+                acc[i, u] = bank([P, BANK], F32)
+        for a in range(PASSES_1 - 1):
+            for u in range(2):
+                for i in range(EARLY):
+                    stage1_pass(i, u, a)
+        for i, u in [(0, 0), (1, 0), (2, 0), (0, 1), (1, 1), (3, 0), (2, 1), (3, 1)]:
+            stage1_pass(i, u, PASSES_1 - 1)
+        keep_rows(0, 0)
+        keep_rows(1, 0)
+        keep_rows(0, 1)
         for i in range(ROW_TILES):
+            if i + 1 < ROW_TILES:
+                keep_rows(i + 1, 1)
+            if i + 2 < ROW_TILES:
+                keep_rows(i + 2, 0)
             if i + EARLY < ROW_TILES:
-                open_rows(i + EARLY)
                 for u in range(2):
+                    acc[i + EARLY, u] = bank([P, BANK], F32)
                     for a in range(PASSES_1):
-                        stage1_pass(acc[i + EARLY, u], i + EARLY, u, a)
-            if i + AHEAD < ROW_TILES:
-                keep_rows(i + AHEAD)
-            leader(i)
-            if i in (2, 4):
-                cast_wg(i // 2 - 1)
-            if i in FREE:
-                follower(i, keep.tile([P, M], F32, name=f"follow{i}")[:])
-        wt_code = keep.tile([P, PASSES_2, H], U32, name="wt_code", tag="v_code2", align_bytes=64)
-        nc.sync.dma_start(
-            out=wt_code[:].bitcast(I32),
-            in_=wt_words.rearrange("a p c i -> p a (c i)").bitcast(I32),
-        )
-        load_wg(2, "v_code0", 64)
-        load_wg(3, "v_code1", 64)
-        wt_scale = keep.tile([P, PASSES_2, H], U8, name="wt_scale", tag="scales", align_bytes=64)
-        nc.gpsimd.memset(wt_scale[:].bitcast(I32), 0)
-        for q in range(4):
-            nc.sync.dma_start(
-                out=wt_scale[32 * q : 32 * q + 4, :, :].bitcast(I32),
-                in_=wt_scales.bitcast(I32)[:, 4 * q : 4 * q + 4, :].rearrange("a r c -> r a c"),
-            )
-        for group in GROUPS:
-            turn_out(group)
-        turn_back(0, "x_grouped0")
-        follow_a = keep.tile([P, len(FIRST), M], F32, name="follow_a", tag="lead_follow")
-        for k, i in enumerate(FIRST):
-            follower(i, follow_a[:, k, :])
-        turn_back(1, "x_follow")
-        if SECOND:
-            follow_b = keep.tile([P, len(SECOND), M], F32, name="follow_b", tag="x_follow", align_bytes=64)
-            for k, i in enumerate(SECOND):
-                follower(i, follow_b[:, k, :])
+                        stage1_pass(i + EARLY, u, a)
+            if i in [6, 7]:
+                leader(i, [0])
+            else:
+                leader(i, [0, 1])
+            for g in GROUPS[0]:
+                if g[-1] == i:
+                    turn_out(g, 0)
+            if i == ROW_TILES - 1:
+                for late in [6, 7]:
+                    leader(late, [1])
+            if i % 4 == 3:
+                turn_back(i // 4, 0)
+        for c in range(2):
+            if c not in [0, 1, 2, 3]:
+                cast_wg(c)
+        quant_wg(0)
+        if [] == []:
+            quant_wg(1)
 
-        answers = {}
+        answer = {}
         half_gate = {}
         diff = {}
         step = {}
 
-        def products(i):
-            u, cols = i // 4, slice(P * (i % 4), P * (i % 4 + 1))
-            a_ps = psum.tile([P, BANK], F32, name="acc", tag="bank", bufs=8)
-            for b in range(PASSES_2):
-                nc.tensor.matmul_mx(
-                    out=a_ps[:],
-                    lhsT=wt_code[:, b, P * i : P * (i + 1)].bitcast(FP8X4),
-                    lhsT_scale=wt_scale[:, b, P * i : P * (i + 1)],
-                    rhs=x_code[:, b, :].bitcast(FP8X4),
-                    rhs_scale=x_scale[:, b, :],
-                    start=(b == 0),
-                    stop=(b == PASSES_2 - 1),
+        def product(pieces, code, scale):
+            ps = bank([P, BANK], F32)
+            at = 0
+            for i, cols in pieces:
+                n = cols.stop - cols.start
+                for b in range(PASSES_2):
+                    nc.tensor.matmul_mx(
+                        out=ps[:, at : at + n],
+                        lhsT=code(b, i).bitcast(FP8X4),
+                        lhsT_scale=scale(b, i),
+                        rhs=x_code[b][:, cols].bitcast(FP8X4),
+                        rhs_scale=x_scale[b][:, cols],
+                        start=(b == 0),
+                        stop=(b == PASSES_2 - 1),
+                    )
+                at += n
+            return ps
+
+        def products(k):
+            a_ps = product(
+                UNITS[k], lambda b, i: wt_code[:, b, P * i : P * (i + 1)], lambda b, i: wt_scale[:, b, P * i : P * (i + 1)]
+            )
+            answer[k] = ring.tile([P, BANK], F32, name="answer", bufs=4)
+            nc.scalar.activation(answer[k][:], a_ps[:], ACT.Tanh, bias=zero_bias[:])
+            g_ps = product(
+                UNITS[k],
+                lambda b, i: wg_code[i // 4][:, b, P * (i % 4) : P * (i % 4 + 1)],
+                lambda b, i: wg_scale[i // 4][:, b, P * (i % 4) : P * (i % 4 + 1)],
+            )
+            half_gate[k] = ring.tile([P, BANK], F32, name="half_gate")
+            nc.scalar.activation(half_gate[k][:], g_ps[:], ACT.Tanh, bias=zero_bias[:], scale=-0.5)
+            diff[k] = ring.tile([P, BANK], F32, name="diff")
+
+        def follower(k, g):
+            if g < len(UNITS[k]):
+                i, cols = UNITS[k][g]
+                n = cols.stop - cols.start
+                nc.vector.tensor_tensor(
+                    diff[k][:, n * g : n * (g + 1)],
+                    h[i][:].indirect(pos2_sb[:, cols.start // 16 : cols.stop // 16]),
+                    answer[k][:, n * g : n * (g + 1)],
+                    ALU.subtract,
                 )
-            g_ps = psum.tile([P, BANK], F32, name="acc", tag="bank", bufs=8)
-            for b in range(PASSES_2):
-                nc.tensor.matmul_mx(
-                    out=g_ps[:],
-                    lhsT=wg_code[b, u][:, cols].bitcast(FP8X4),
-                    lhsT_scale=wg_scale[b, u][:, cols],
-                    rhs=x_code[:, b, :].bitcast(FP8X4),
-                    rhs_scale=x_scale[:, b, :],
-                    start=(b == 0),
-                    stop=(b == PASSES_2 - 1),
-                )
-            sign = -1.0 if i in FUSED else 1.0
-            answers[i] = ring.tile([P, M], F32, name="answer", bufs=4)
-            nc.scalar.activation(answers[i][:], a_ps[:], ACT.Tanh, bias=zero_bias[:])
-            half_gate[i] = ring.tile([P, M], F32, name="half_gate")
-            nc.scalar.activation(half_gate[i][:], g_ps[:], ACT.Tanh, bias=zero_bias[:], scale=0.5 * sign)
-            diff[i] = ring.tile([P, M], F32, name="diff", bufs=2)
-            if i in FUSED:
-                nc.vector.tensor_tensor(diff[i][:], h[i][:].indirect(pos2_sb[:]), answers[i][:], ALU.subtract)
+
+        def gated(k):
+            step[k] = ring.tile([P, BANK], F32, name="step", bufs=2)
+            nc.vector.scalar_tensor_tensor(step[k][:], half_gate[k][:], 1.0, diff[k][:], ALU.add, ALU.mult)
+
+        def finish(k):
+            res = ring.tile([P, BANK], F32, name="res")
+            i, cols = UNITS[k][0]
+            n = len(UNITS[k])
+            rows = out[P * i : P * (i + n), cols].rearrange("(g p) m -> p g m", p=P)
+            if k == len(UNITS) - 1:
+                for g in range(2):
+                    part = slice(HALF * g, HALF * (g + 1))
+                    nc.vector.scalar_tensor_tensor(
+                        res[:, part], step[k][:, part], 0.5, answer[k][:, part], ALU.mult, ALU.add
+                    )
+                    nc.sync.dma_start(out=rows[:, g, :] if n == 2 else rows[:, 0, part], in_=res[:, part])
             else:
-                nc.vector.tensor_tensor(diff[i][:], answers[i][:], followers[i], ALU.subtract)
+                nc.vector.scalar_tensor_tensor(res[:], step[k][:], 0.5, answer[k][:], ALU.mult, ALU.add)
+                nc.sync.dma_start(out=rows, in_=res[:].rearrange("p (g m) -> p g m", g=n))
 
-        def gated(i):
-            step[i] = ring.tile([P, M], F32, name="step", bufs=2)
-            nc.vector.scalar_tensor_tensor(step[i][:], half_gate[i][:], 1.0, diff[i][:], ALU.add, ALU.mult)
-
-        def finish(i):
-            res = ring.tile([P, M], F32, name="res", bufs=3)
-            base = answers[i][:] if i in FUSED else followers[i]
-            parts = 2 if i == ROW_TILES - 1 else 1
-            for k in range(parts):
-                cols = slice(M // parts * k, M // parts * (k + 1))
-                nc.vector.scalar_tensor_tensor(res[:, cols], step[i][:, cols], 0.5, base[:, cols], ALU.mult, ALU.add)
-                nc.sync.dma_start(out=out[P * i : P * (i + 1), cols], in_=res[:, cols])
-
-        for i in range(ROW_TILES + 2):
-            if i < ROW_TILES:
-                products(i)
-            if i in (1, 2):
-                cast_wg(i + 1)
-            if 1 <= i <= ROW_TILES:
-                gated(i - 1)
-            if i >= 2:
-                finish(i - 2)
+        for k in range(len(UNITS) + 1):
+            if k < len(UNITS):
+                products(k)
+                follower(k, 0)
+            if k >= 1:
+                gated(k - 1)
+            if k < len(UNITS):
+                follower(k, 1)
+            if k >= 1:
+                finish(k - 1)
+            for g, at in zip(GROUPS[1], [0, 1, 1, 2]):
+                if at == k:
+                    turn_out(g, 1)
+                    if g[-1] % 4 == 3:
+                        turn_back(g[-1] // 4, 1)
+            if k in []:
+                c = 2 + [].index(k)
+                if c not in [0, 1, 2, 3]:
+                    cast_wg(c)
+                if c == 3:
+                    quant_wg(1)

@@ -31,7 +31,7 @@ LOW, HIGH, ALL = slice(0, HALF), slice(HALF, M), slice(0, M)
 UNITS = [[(2 * j, cols), (2 * j + 1, cols)] for cols in (LOW, HIGH) for j in range(4)]
 CAST_TAG = ["wg_pair0", "wg_pair1"]
 CODE_TAG = ["act7_0", "x_grouped10"]
-PIECES = [1, 1, 1, 1]
+PIECES = [2, 2, 2, 2]
 
 
 def tile_list_fugue_imitation_gate_kernel(
@@ -200,7 +200,7 @@ def tile_list_fugue_imitation_gate_kernel(
         h = [keep.tile([P, S], F32, name=f"h{i}") for i in range(ROW_TILES)]
         lead = {}
         x_turned = {}
-        x_code = [keep.tile([P, M], U32, name=f"x_code{b}", align_bytes=64) for b in range(PASSES_2)]
+        x_code = [keep.tile([P, M], U32, name=f"x_code{b}", tag=["wg_raw3", "x_code1"][b], align_bytes=64) for b in range(PASSES_2)]
         x_scale = [keep.tile([P, M], U8, name=f"x_scale{b}", align_bytes=64) for b in range(PASSES_2)]
 
         def stage1_pass(i, u, a):
@@ -238,11 +238,18 @@ def tile_list_fugue_imitation_gate_kernel(
                 dst = lead[g[0], halves[0]][:, i - g[0], :]
             nc.vector.tensor_copy(dst, h[i][:].indirect(pos1_sb[:, 16 * halves[0] : 16 * (halves[-1] + 1)]))
 
-        def turn_out(g, hf):
-            n, b = len(g), g[0] // 4
+        acts = {}
+
+        def activate(g, hf):
+            n = len(g)
             tag = f"act{g[0]}_{hf}"
             act = keep.tile([P, n, HALF], F32, name=tag, tag={"act0_1": "w1_code1", "act2_1": "lead7_0", "act4_1": "x_turned10", "act6_1": "lead7_0", "lead6_1": "v_code21"}.get(tag, tag), align_bytes=64)
             nc.scalar.activation(act[:], lead[g[0], hf], ACT.Gelu_apprx_tanh)
+            acts[g[0], hf] = act
+
+        def turn_out(g, hf):
+            n, b = len(g), g[0] // 4
+            act = acts[g[0], hf]
             if g[0] % 4 == 0:
                 tag = f"x_turned{b}{hf}"
                 x_turned[b, hf] = keep.tile([P, 2, BANK], BF16, name=tag, tag=tag, align_bytes=64)
@@ -311,12 +318,19 @@ def tile_list_fugue_imitation_gate_kernel(
                 leader(i, [0, 1])
             for g in GROUPS[0]:
                 if g[-1] == i:
-                    turn_out(g, 0)
-            if i == ROW_TILES - 1:
-                for late in [6, 7]:
-                    leader(late, [1])
-            if i % 4 == 3:
-                turn_back(i // 4, 0)
+                    activate(g, 0)
+                    if i < 8:
+                        turn_out(g, 0)
+            if i == 3 and 8 >= 4:
+                turn_back(0, 0)
+        for g in GROUPS[0]:
+            if g[-1] >= 8:
+                turn_out(g, 0)
+                if g[-1] == 3:
+                    turn_back(0, 0)
+        turn_back(1, 0)
+        for late in [6, 7]:
+            leader(late, [1])
         for c in range(2):
             if c not in [0, 1, 2, 3]:
                 cast_wg(c)
@@ -331,20 +345,18 @@ def tile_list_fugue_imitation_gate_kernel(
 
         def product(pieces, code, scale):
             ps = bank([P, BANK], F32)
-            at = 0
-            for i, cols in pieces:
-                n = cols.stop - cols.start
-                for b in range(PASSES_2):
+            for b in range(PASSES_2):
+                for g, (i, cols) in enumerate(pieces):
+                    n = cols.stop - cols.start
                     nc.tensor.matmul_mx(
-                        out=ps[:, at : at + n],
+                        out=ps[:, n * g : n * (g + 1)],
                         lhsT=code(b, i).bitcast(FP8X4),
                         lhsT_scale=scale(b, i),
                         rhs=x_code[b][:, cols].bitcast(FP8X4),
                         rhs_scale=x_scale[b][:, cols],
-                        start=(b == 0),
-                        stop=(b == PASSES_2 - 1),
+                        start=(b == 0 and g == 0),
+                        stop=(b == PASSES_2 - 1 and g == len(pieces) - 1),
                     )
-                at += n
             return ps
 
         def products(k):
@@ -405,6 +417,7 @@ def tile_list_fugue_imitation_gate_kernel(
                 finish(k - 1)
             for g, at in zip(GROUPS[1], [0, 1, 1, 2]):
                 if at == k:
+                    activate(g, 1)
                     turn_out(g, 1)
                     if g[-1] % 4 == 3:
                         turn_back(g[-1] // 4, 1)

@@ -24,13 +24,12 @@ ACT = mybir.ActivationFunctionType
 ALU = mybir.AluOpType
 
 EARLY = 4
-SHIFT_ROWS = 100
-GROUPS = [[[0, 1], [2, 3], [4, 5], [6], [7]], [[0, 1], [2, 3], [4, 5], [6, 7]]]
+GROUPS = [[[0, 1], [2, 3], [4, 5], [6, 7]], [[0, 1], [2, 3], [4, 5], [6, 7]]]
 CAST = ["gpsimd"] * 4
 LOW, HIGH, ALL = slice(0, HALF), slice(HALF, M), slice(0, M)
 UNITS = [[(2 * j, cols), (2 * j + 1, cols)] for cols in (LOW, HIGH) for j in range(4)]
 CAST_TAG = ["wg_pair0", "wg_pair1"]
-CODE_TAG = ["act7_0", "x_grouped10"]
+CODE_TAG = ["x_turned10", "x_grouped10"]
 PIECES = [2, 2, 2, 2]
 
 
@@ -49,16 +48,17 @@ def tile_list_fugue_imitation_gate_kernel(
         offs_sb = keep.tile([P, S // 16], U16, name="offs_sb")
         pos1_sb = keep.tile([P, M // 16], U16, name="pos1_sb")
         pos2_sb = keep.tile([P, M // 16], U16, name="pos2_sb")
-        tab_scale = keep.tile([P, T], U8, name="tab_scale", tag="tab_scale", align_bytes=64)
-        w1_scale = keep.tile([P, PASSES_1, H], U8, name="w1_scale", align_bytes=64)
-        wt_scale = keep.tile([P, PASSES_2, H], U8, name="wt_scale", align_bytes=64)
-        v_scale = [keep.tile([P, S], U8, name=f"v_scale{a}", align_bytes=64) for a in range(PASSES_1)]
+        tab_scale = keep.tile([P, T], U8, name="tab_scale", tag="big2", align_bytes=64)
+        w1_scale = keep.tile([P, PASSES_1, H], U8, name="w1_scale", tag="w1_scale", align_bytes=64)
+        picked_scale = keep.tile([P, S], U8, name="picked_scale", tag="picked", align_bytes=64)
+        v_scale = [keep.tile([P, S], U8, name=f"v_scale{a}", tag=f"v_scale{a}", align_bytes=64) for a in range(PASSES_1)]
         gain_rows = keep.tile([P, P], F32, name="gain_rows")
         zero_col = keep.tile([P, 1], F32, name="zero_col")
         zero_bias = keep.tile([P, 1], F32, name="zero_bias")
         ident = keep.tile([P, P], F32, name="ident")
 
-        nc.vector.memset(tab_scale[:].bitcast(I32), 0)
+        for rows in (slice(32, 64), slice(64, 112)):
+            nc.vector.memset(tab_scale[rows, :].bitcast(I32), 0)
         nc.vector.memset(zero_col[:], 0.0)
         for rows in (slice(0, 24), slice(32, 64), slice(64, P)):
             nc.vector.memset(gain_rows[rows, :].bitcast(I32), 0)
@@ -68,16 +68,18 @@ def tile_list_fugue_imitation_gate_kernel(
         make_identity(nc, ident_bf16[:])
 
         w1_i32 = w1_words.bitcast(I32)
-        w1_code = [keep.tile([P, PASSES_1, H], U8, name=f"w1_code{u}", tag=f"w1_code{u}", align_bytes=64) for u in range(2)]
-        tab_code = [keep.tile([P, T], U32, name=f"tab_code{a}", tag=f"big{a}", align_bytes=64) for a in range(PASSES_1)]
+        w1_code = {}
+        tab_code = {}
 
-        def load_w1(u):
+        def load_w1(u, tag):
+            w1_code[u] = keep.tile([P, PASSES_1, H], U8, name=f"w1_code{u}", tag=tag, align_bytes=64)
             nc.sync.dma_start(
                 out=w1_code[u][:].bitcast(I32),
                 in_=w1_i32[:, :, 256 * u : 256 * (u + 1)].rearrange("a p c -> p a c"),
             )
 
         def load_tab(a):
+            tab_code[a] = keep.tile([P, T], U32, name=f"tab_code{a}", tag=f"big{a}", align_bytes=64)
             nc.sync.dma_start(
                 out=tab_code[a][:].bitcast(I32),
                 in_=tab_words[a].rearrange("p t i -> p (t i)").bitcast(I32),
@@ -92,11 +94,12 @@ def tile_list_fugue_imitation_gate_kernel(
 
         tab_rows = tab_scales.bitcast(I32)
         nc.sync.dma_start(offs_sb[:], offs)
-        load_scale_rows([nc.scalar, nc.scalar, nc.sync, nc.sync], w1_scale, w1_scales)
+        nc.sync.dma_start(pos1_sb[:], pos1)
+        nc.sync.dma_start(pos2_sb[:], pos2)
+        nc.scalar.dma_start(out=tab_scale[0:32, :].bitcast(I32), in_=tab_rows[0:2].rearrange("a q c -> (a q) c"))
+        nc.scalar.dma_start(out=tab_scale[112:128, :].bitcast(I32), in_=tab_rows[2])
         load_tab(0)
-        for q in range(4):
-            nc.sync.dma_start(out=tab_scale[32 * q : 32 * q + 8, :].bitcast(I32), in_=tab_rows[0:2, 4 * q : 4 * q + 4, :])
-        nc.sync.dma_start(out=tab_scale[16:32, :].bitcast(I32), in_=tab_rows[2])
+        load_scale_rows([nc.scalar, nc.scalar, nc.sync, nc.sync], w1_scale, w1_scales)
         nc.scalar.activation(zero_bias[:], zero_col[:], ACT.Gelu_apprx_tanh)
         ps = bank([P, BANK], F32)
         nc.tensor.transpose(ps[:, 0:P], gain_rows[:], ident[:])
@@ -111,12 +114,8 @@ def tile_list_fugue_imitation_gate_kernel(
             nc.scalar.copy(gain_all[:, BANK * b : BANK * (b + 1)], ps[:])
 
 
-        load_w1(0)
         load_tab(1)
-        load_tab(2)
-        load_w1(1)
-        nc.sync.dma_start(pos1_sb[:], pos1)
-        nc.sync.dma_start(pos2_sb[:], pos2)
+        load_w1(0, "w1_code0")
 
         v_code = {}
 
@@ -124,25 +123,22 @@ def tile_list_fugue_imitation_gate_kernel(
             v_code[a, u] = keep.tile([P, BANK], U32, name=f"v_code{a}{u}", tag=tag, align_bytes=64)
             nc.vector.tensor_copy(v_code[a, u][:], tab_code[a][:].indirect(offs_sb[:, 32 * u : 32 * (u + 1)]))
 
-        gather_words(0, 0, "v_code00")
-        for u in range(2):
-            nc.vector.tensor_copy(
-                v_scale[0][:, BANK * u : BANK * (u + 1)], tab_scale[:].indirect(offs_sb[:, 32 * u : 32 * (u + 1)])
+        nc.vector.tensor_copy(picked_scale[:], tab_scale[:].indirect(offs_sb[:]))
+        moves = [(a, q) for a in range(PASSES_1) for q in range(4)]
+        for k, (a, q) in enumerate(moves):
+            if k == 5:
+                load_tab(2)
+            if k == 8:
+                late_moves = moves[8:]
+                break
+            first = (0, 16, 112)[a] + 4 * q
+            queue = nc.gpsimd if k >= 10 else nc.sync
+            queue.dma_start(
+                out=v_scale[a][32 * q : 32 * q + 4, :].bitcast(I32), in_=picked_scale[first : first + 4, :].bitcast(I32)
             )
-        for cols in [slice(0, BANK), slice(BANK, S)]:
-            nc.scalar.dma_start(
-                out=v_scale[1][0:SHIFT_ROWS, cols].bitcast(I32), in_=v_scale[0][4 : 4 + SHIFT_ROWS, cols].bitcast(I32)
-            )
-        for q in range(4):
-            nc.scalar.dma_start(
-                out=v_scale[2][32 * q : 32 * q + 4, :].bitcast(I32),
-                in_=v_scale[0][16 + 4 * q : 20 + 4 * q, :].bitcast(I32),
-            )
-        gather_words(0, 1, "tab_scale")
-        for a in range(1, PASSES_1):
+        for a in range(PASSES_1):
             for u in range(2):
                 gather_words(a, u, f"v_code{a}{u}")
-
 
         chunks = [(b, u) for u in range(2) for b in range(PASSES_2)]
         wg_raw = {}
@@ -186,21 +182,31 @@ def tile_list_fugue_imitation_gate_kernel(
                 in_=wg_pair[u][:].rearrange("p b n j -> p (b n j)"),
             )
 
-        load_wg(0, "big0", nc.scalar)
-        load_wg(1, "big1", nc.scalar)
-        wt_code = keep.tile([P, PASSES_2, H], U32, name="wt_code", tag="big2", align_bytes=64)
+        load_w1(1, "big0")
+        for k, (a, q) in enumerate(late_moves):
+            first = 112 + 4 * q
+            queue = nc.gpsimd if k + 8 >= 10 else nc.sync
+            queue.dma_start(
+                out=v_scale[a][32 * q : 32 * q + 4, :].bitcast(I32), in_=picked_scale[first : first + 4, :].bitcast(I32)
+            )
+        load_wg(0, "big1", nc.sync)
+        load_wg(1, "picked", nc.sync)
+        load_wg(2, "big2", nc.sync)
+        cast_wg(0)
+        load_wg(3, "big1", nc.sync)
+        cast_wg(1)
+        wt_code = keep.tile([P, PASSES_2, H], U32, name="wt_code", tag="picked", align_bytes=64)
         nc.sync.dma_start(out=wt_code[:].bitcast(I32), in_=wt_words.rearrange("a p c i -> p a (c i)").bitcast(I32))
-        load_wg(2, "wg_raw2", nc.sync)
-        load_wg(3, "wg_raw3", nc.sync)
+        cast_wg(2)
+        wt_scale = keep.tile([P, PASSES_2, H], U8, name="wt_scale", tag="big2", align_bytes=64)
         load_scale_rows([nc.sync] * 4, wt_scale, wt_scales)
-        for c in [0, 1, 2, 3]:
-            cast_wg(c)
+        cast_wg(3)
 
         acc = {}
         h = [keep.tile([P, S], F32, name=f"h{i}") for i in range(ROW_TILES)]
         lead = {}
         x_turned = {}
-        x_code = [keep.tile([P, M], U32, name=f"x_code{b}", tag=["wg_raw3", "x_code1"][b], align_bytes=64) for b in range(PASSES_2)]
+        x_code = [keep.tile([P, M], U32, name=f"x_code{b}", tag=["x_code0", "x_code1"][b], align_bytes=64) for b in range(PASSES_2)]
         x_scale = [keep.tile([P, M], U8, name=f"x_scale{b}", align_bytes=64) for b in range(PASSES_2)]
 
         def stage1_pass(i, u, a):
@@ -216,7 +222,7 @@ def tile_list_fugue_imitation_gate_kernel(
             )
 
         def keep_rows(i, u):
-            if (i, u) in []:
+            if (i, u) in [(1, 0), (2, 0)]:
                 nc.vector.tensor_copy(h[i][:, BANK * u : BANK * (u + 1)], acc[i, u][:])
             else:
                 nc.scalar.copy(h[i][:, BANK * u : BANK * (u + 1)], acc[i, u][:])
@@ -233,7 +239,7 @@ def tile_list_fugue_imitation_gate_kernel(
                 g = [g for g in GROUPS[halves[0]] if i in g][0]
                 if i == g[0]:
                     tag = f"lead{i}_{halves[0]}"
-                    tile = keep.tile([P, len(g), HALF], F32, name=tag, tag={"act0_1": "w1_code1", "act2_1": "lead7_0", "act4_1": "x_turned10", "act6_1": "lead7_0", "lead6_1": "v_code21"}.get(tag, tag), align_bytes=64)
+                    tile = keep.tile([P, len(g), HALF], F32, name=tag, tag={"act0_0": "v_code00", "act2_0": "v_code01", "act4_0": "w1_scale", "act6_0": "v_scale2", "lead6_1": "v_scale2", "act0_1": "v_code21", "act2_1": "x_turned00", "act4_1": "x_grouped00"}.get(tag, tag), align_bytes=64)
                     lead[i, halves[0]] = tile[:]
                 dst = lead[g[0], halves[0]][:, i - g[0], :]
             nc.vector.tensor_copy(dst, h[i][:].indirect(pos1_sb[:, 16 * halves[0] : 16 * (halves[-1] + 1)]))
@@ -243,14 +249,14 @@ def tile_list_fugue_imitation_gate_kernel(
         def activate(g, hf):
             n = len(g)
             tag = f"act{g[0]}_{hf}"
-            act = keep.tile([P, n, HALF], F32, name=tag, tag={"act0_1": "w1_code1", "act2_1": "lead7_0", "act4_1": "x_turned10", "act6_1": "lead7_0", "lead6_1": "v_code21"}.get(tag, tag), align_bytes=64)
+            act = keep.tile([P, n, HALF], F32, name=tag, tag={"act0_0": "v_code00", "act2_0": "v_code01", "act4_0": "w1_scale", "act6_0": "v_scale2", "lead6_1": "v_scale2", "act0_1": "v_code21", "act2_1": "x_turned00", "act4_1": "x_grouped00"}.get(tag, tag), align_bytes=64)
             nc.scalar.activation(act[:], lead[g[0], hf], ACT.Gelu_apprx_tanh)
             acts[g[0], hf] = act
 
         def turn_out(g, hf):
             n, b = len(g), g[0] // 4
             act = acts[g[0], hf]
-            if g[0] % 4 == 0:
+            if (b, hf) not in x_turned:
                 tag = f"x_turned{b}{hf}"
                 x_turned[b, hf] = keep.tile([P, 2, BANK], BF16, name=tag, tag=tag, align_bytes=64)
             first = P * (g[0] % 4)
@@ -293,12 +299,13 @@ def tile_list_fugue_imitation_gate_kernel(
         for i in range(EARLY):
             for u in range(2):
                 acc[i, u] = bank([P, BANK], F32)
-        for a in range(PASSES_1 - 1):
-            for u in range(2):
-                for i in range(EARLY):
+        for u in range(2):
+            for i in range(EARLY):
+                stage1_pass(i, u, 0)
+        for i in range(EARLY):
+            for a in range(1, PASSES_1):
+                for u in range(2):
                     stage1_pass(i, u, a)
-        for i, u in [(0, 0), (1, 0), (2, 0), (0, 1), (1, 1), (3, 0), (2, 1), (3, 1)]:
-            stage1_pass(i, u, PASSES_1 - 1)
         keep_rows(0, 0)
         keep_rows(1, 0)
         keep_rows(0, 1)
@@ -317,17 +324,20 @@ def tile_list_fugue_imitation_gate_kernel(
             else:
                 leader(i, [0, 1])
             for g in GROUPS[0]:
-                if g[-1] == i:
+                if g[-1] == i and i < 0:
                     activate(g, 0)
-                    if i < 8:
-                        turn_out(g, 0)
-            if i == 3 and 8 >= 4:
-                turn_back(0, 0)
-        for g in GROUPS[0]:
-            if g[-1] >= 8:
+            for g, at in zip(GROUPS[0], [8, 8, 8, 8]):
+                if at == i:
+                    turn_out(g, 0)
+                    if g[-1] == 3:
+                        turn_back(0, 0)
+        for g, at in zip(GROUPS[0], [8, 8, 8, 8]):
+            if g[-1] >= 0:
+                activate(g, 0)
+            if at == 8:
                 turn_out(g, 0)
-                if g[-1] == 3:
-                    turn_back(0, 0)
+        if [8, 8, 8, 8][1] == 8:
+            turn_back(0, 0)
         turn_back(1, 0)
         for late in [6, 7]:
             leader(late, [1])
@@ -338,6 +348,7 @@ def tile_list_fugue_imitation_gate_kernel(
         if [] == []:
             quant_wg(1)
 
+        turned = []
         answer = {}
         half_gate = {}
         diff = {}
@@ -419,8 +430,9 @@ def tile_list_fugue_imitation_gate_kernel(
                 if at == k:
                     activate(g, 1)
                     turn_out(g, 1)
-                    if g[-1] % 4 == 3:
-                        turn_back(g[-1] // 4, 1)
+                    turned.extend(g)
+                    if all(i in turned for i in range(g[0] // 4 * 4, g[0] // 4 * 4 + 4)):
+                        turn_back(g[0] // 4, 1)
             if k in []:
                 c = 2 + [].index(k)
                 if c not in [0, 1, 2, 3]:

@@ -222,7 +222,7 @@ def tile_list_fugue_imitation_gate_kernel(
             )
 
         def keep_rows(i, u):
-            if (i, u) in [(1, 0), (2, 0)]:
+            if (i, u) in [(1, 0)]:
                 nc.vector.tensor_copy(h[i][:, BANK * u : BANK * (u + 1)], acc[i, u][:])
             else:
                 nc.scalar.copy(h[i][:, BANK * u : BANK * (u + 1)], acc[i, u][:])
@@ -296,6 +296,18 @@ def tile_list_fugue_imitation_gate_kernel(
             cols = slice(HALF * hf, HALF * (hf + 1))
             nc.vector.quantize_mx(out=x_code[b][:, cols].bitcast(FP8X4), scales=x_scale[b][:, cols], in_=grouped[:])
 
+        for k in range(3):
+            if k == 0:
+                idle = bank([P, BANK], F32)
+            nc.tensor.matmul_mx(
+                out=idle[:],
+                lhsT=v_code[0, 0][:, 0:P].bitcast(FP8X4),
+                lhsT_scale=picked_scale[:, 0:P],
+                rhs=v_code[0, 0][:].bitcast(FP8X4),
+                rhs_scale=picked_scale[:, 0:BANK],
+                start=True,
+                stop=True,
+            )
         for i in range(EARLY):
             for u in range(2):
                 acc[i, u] = bank([P, BANK], F32)
@@ -336,6 +348,18 @@ def tile_list_fugue_imitation_gate_kernel(
                 activate(g, 0)
             if at == 8:
                 turn_out(g, 0)
+                for k in range({}.get(g[0], 0)):
+                    if k == 0:
+                        idle = bank([P, BANK], F32)
+                    nc.tensor.matmul_mx(
+                        out=idle[:],
+                        lhsT=v_code[1, 1][:, 0:P].bitcast(FP8X4),
+                        lhsT_scale=v_scale[1][:, 0:P],
+                        rhs=v_code[1, 1][:].bitcast(FP8X4),
+                        rhs_scale=v_scale[1][:, 0:BANK],
+                        start=True,
+                        stop=True,
+                    )
         if [8, 8, 8, 8][1] == 8:
             turn_back(0, 0)
         turn_back(1, 0)

@@ -348,7 +348,7 @@ def tile_list_fugue_imitation_gate_kernel(
                 activate(g, 0)
             if at == 8:
                 turn_out(g, 0)
-                for k in range({}.get(g[0], 0)):
+                for k in range({2: 2, 4: 2}.get(g[0], 0)):
                     if k == 0:
                         idle = bank([P, BANK], F32)
                     nc.tensor.matmul_mx(

@@ -132,7 +132,7 @@ def tile_list_fugue_imitation_gate_kernel(
                 late_moves = moves[8:]
                 break
             first = (0, 16, 112)[a] + 4 * q
-            queue = nc.gpsimd if k >= 10 else nc.sync
+            queue = nc.gpsimd if k in [10, 11] else nc.sync
             queue.dma_start(
                 out=v_scale[a][32 * q : 32 * q + 4, :].bitcast(I32), in_=picked_scale[first : first + 4, :].bitcast(I32)
             )
@@ -185,7 +185,7 @@ def tile_list_fugue_imitation_gate_kernel(
         load_w1(1, "big0")
         for k, (a, q) in enumerate(late_moves):
             first = 112 + 4 * q
-            queue = nc.gpsimd if k + 8 >= 10 else nc.sync
+            queue = nc.gpsimd if k + 8 in [10, 11] else nc.sync
             queue.dma_start(
                 out=v_scale[a][32 * q : 32 * q + 4, :].bitcast(I32), in_=picked_scale[first : first + 4, :].bitcast(I32)
             )
@@ -296,18 +296,21 @@ def tile_list_fugue_imitation_gate_kernel(
             cols = slice(HALF * hf, HALF * (hf + 1))
             nc.vector.quantize_mx(out=x_code[b][:, cols].bitcast(FP8X4), scales=x_scale[b][:, cols], in_=grouped[:])
 
-        for k in range(3):
-            if k == 0:
-                idle = bank([P, BANK], F32)
-            nc.tensor.matmul_mx(
-                out=idle[:],
-                lhsT=v_code[0, 0][:, 0:P].bitcast(FP8X4),
-                lhsT_scale=picked_scale[:, 0:P],
-                rhs=v_code[0, 0][:].bitcast(FP8X4),
-                rhs_scale=picked_scale[:, 0:BANK],
-                start=True,
-                stop=True,
-            )
+        def warm_up(count, code, scale):
+            for k in range(count):
+                if k == 0:
+                    idle = bank([P, BANK], F32)
+                nc.tensor.matmul_mx(
+                    out=idle[:],
+                    lhsT=code[:, 0:P].bitcast(FP8X4),
+                    lhsT_scale=scale[:, 0:P],
+                    rhs=code[:].bitcast(FP8X4),
+                    rhs_scale=scale[:, 0:BANK],
+                    start=True,
+                    stop=True,
+                )
+
+        warm_up(3, v_code[0, 0], picked_scale)
         for i in range(EARLY):
             for u in range(2):
                 acc[i, u] = bank([P, BANK], F32)
@@ -348,21 +351,12 @@ def tile_list_fugue_imitation_gate_kernel(
                 activate(g, 0)
             if at == 8:
                 turn_out(g, 0)
-                for k in range({2: 2, 4: 2}.get(g[0], 0)):
-                    if k == 0:
-                        idle = bank([P, BANK], F32)
-                    nc.tensor.matmul_mx(
-                        out=idle[:],
-                        lhsT=v_code[1, 1][:, 0:P].bitcast(FP8X4),
-                        lhsT_scale=v_scale[1][:, 0:P],
-                        rhs=v_code[1, 1][:].bitcast(FP8X4),
-                        rhs_scale=v_scale[1][:, 0:BANK],
-                        start=True,
-                        stop=True,
-                    )
+                warm_up({2: 2, 4: 2}.get(g[0], 0), v_code[1, 1], v_scale[1])
         if [8, 8, 8, 8][1] == 8:
             turn_back(0, 0)
+        warm_up(0, v_code[1, 1], v_scale[1])
         turn_back(1, 0)
+        warm_up(1, v_code[1, 1], v_scale[1])
         for late in [6, 7]:
             leader(late, [1])
         for c in range(2):
@@ -422,7 +416,12 @@ def tile_list_fugue_imitation_gate_kernel(
 
         def gated(k):
             step[k] = ring.tile([P, BANK], F32, name="step", bufs=2)
-            nc.vector.scalar_tensor_tensor(step[k][:], half_gate[k][:], 1.0, diff[k][:], ALU.add, ALU.mult)
+            parts = 2 if k == len(UNITS) - 1 and True else 1
+            for g in range(parts):
+                piece = slice(BANK // parts * g, BANK // parts * (g + 1))
+                nc.vector.scalar_tensor_tensor(
+                    step[k][:, piece], half_gate[k][:, piece], 1.0, diff[k][:, piece], ALU.add, ALU.mult
+                )
 
         def finish(k):
             res = ring.tile([P, BANK], F32, name="res")

@@ -39,6 +39,7 @@ def tile_list_fugue_imitation_gate_kernel(
     nc = tc.nc
     with ExitStack() as ctx:
         keep = ctx.enter_context(tc.tile_pool(name="keep", bufs=1))
+        laid = ctx.enter_context(tc.tile_pool(name="laid", bufs=1))
         ring = ctx.enter_context(tc.tile_pool(name="ring", bufs=3))
         psum = ctx.enter_context(tc.psum_pool(name="psum", bufs=1))
 
@@ -48,7 +49,7 @@ def tile_list_fugue_imitation_gate_kernel(
         offs_sb = keep.tile([P, S // 16], U16, name="offs_sb")
         pos1_sb = keep.tile([P, M // 16], U16, name="pos1_sb")
         pos2_sb = keep.tile([P, M // 16], U16, name="pos2_sb")
-        tab_scale = keep.tile([P, T], U8, name="tab_scale", tag="big2", align_bytes=64)
+        tab_scale = laid.tile([P, T], U8, name="tab_scale", offset=1024, align_bytes=64)
         w1_scale = keep.tile([P, PASSES_1, H], U8, name="w1_scale", tag="w1_scale", align_bytes=64)
         picked_scale = keep.tile([P, S], U8, name="picked_scale", tag="picked", align_bytes=64)
         v_scale = [keep.tile([P, S], U8, name=f"v_scale{a}", tag=f"v_scale{a}", align_bytes=64) for a in range(PASSES_1)]
@@ -79,7 +80,10 @@ def tile_list_fugue_imitation_gate_kernel(
             )
 
         def load_tab(a):
-            tab_code[a] = keep.tile([P, T], U32, name=f"tab_code{a}", tag=f"big{a}", align_bytes=64)
+            if a == 2:
+                tab_code[a] = laid.tile([P, T], U32, name="tab_code2", offset=2048, align_bytes=64)
+            else:
+                tab_code[a] = keep.tile([P, T], U32, name=f"tab_code{a}", tag=f"big{a}", align_bytes=64)
             nc.sync.dma_start(
                 out=tab_code[a][:].bitcast(I32),
                 in_=tab_words[a].rearrange("p t i -> p (t i)").bitcast(I32),
@@ -115,7 +119,8 @@ def tile_list_fugue_imitation_gate_kernel(
 
 
         load_tab(1)
-        load_w1(0, "w1_code0")
+        w1_first = keep.tile([P, H], U8, name="w1_first", align_bytes=64)
+        nc.sync.dma_start(out=w1_first[:].bitcast(I32), in_=w1_i32[0, :, 0:256])
 
         v_code = {}
 
@@ -128,6 +133,8 @@ def tile_list_fugue_imitation_gate_kernel(
         for k, (a, q) in enumerate(moves):
             if k == 5:
                 load_tab(2)
+                w1_next = laid.tile([P, 2, H], U8, name="w1_next", offset=0, align_bytes=64)
+                nc.sync.dma_start(out=w1_next[:].bitcast(I32), in_=w1_i32[1:3, :, 0:256].rearrange("a p c -> p a c"))
             if k == 8:
                 late_moves = moves[8:]
                 break
@@ -150,7 +157,10 @@ def tile_list_fugue_imitation_gate_kernel(
         def load_wg(c, tag, queue):
             b, u = chunks[c]
             rows = wg[512 * b : 512 * (b + 1), :].rearrange("(p j) n -> p j n", j=4)
-            wg_raw[c] = keep.tile([P, 4, BANK], F32, name=f"wg_raw{c}", tag=tag, align_bytes=64)
+            if tag == "big2":
+                wg_raw[c] = laid.tile([P, 4, BANK], F32, name=f"wg_raw{c}", offset=2048, align_bytes=64)
+            else:
+                wg_raw[c] = keep.tile([P, 4, BANK], F32, name=f"wg_raw{c}", tag=tag, align_bytes=64)
             queue.dma_start(out=wg_raw[c][:], in_=rows[:, :, BANK * u : BANK * (u + 1)])
 
         def cast_wg(c):
@@ -198,7 +208,7 @@ def tile_list_fugue_imitation_gate_kernel(
         wt_code = keep.tile([P, PASSES_2, H], U32, name="wt_code", tag="picked", align_bytes=64)
         nc.sync.dma_start(out=wt_code[:].bitcast(I32), in_=wt_words.rearrange("a p c i -> p a (c i)").bitcast(I32))
         cast_wg(2)
-        wt_scale = keep.tile([P, PASSES_2, H], U8, name="wt_scale", tag="big2", align_bytes=64)
+        wt_scale = laid.tile([P, PASSES_2, H], U8, name="wt_scale", offset=2048, align_bytes=64)
         load_scale_rows([nc.sync] * 4, wt_scale, wt_scales)
         cast_wg(3)
 
@@ -211,9 +221,10 @@ def tile_list_fugue_imitation_gate_kernel(
 
         def stage1_pass(i, u, a):
             cols = slice(BANK * u, BANK * (u + 1))
+            words = w1_code[1][:, a, :] if i >= 4 else w1_first[:] if a == 0 else w1_next[:, a - 1, :]
             nc.tensor.matmul_mx(
                 out=acc[i, u][:],
-                lhsT=w1_code[i // 4][:, a, 256 * (i % 4) : 256 * (i % 4 + 1)].bitcast(FP4X4),
+                lhsT=words[:, 256 * (i % 4) : 256 * (i % 4 + 1)].bitcast(FP4X4),
                 lhsT_scale=w1_scale[:, a, P * i : P * (i + 1)],
                 rhs=v_code[a, u][:].bitcast(FP8X4),
                 rhs_scale=v_scale[a][:, cols],

@@ -24,7 +24,7 @@ ACT = mybir.ActivationFunctionType
 ALU = mybir.AluOpType
 
 EARLY = 4
-GROUPS = [[[0, 1], [2, 3], [4, 5], [6, 7]], [[0, 1], [2, 3], [4, 5], [6, 7]]]
+GROUPS = [[[0, 1], [2, 3], [4, 5], [6], [7]], [[0, 1], [2, 3], [4, 5], [6, 7]]]
 CAST = ["gpsimd"] * 4
 LOW, HIGH, ALL = slice(0, HALF), slice(HALF, M), slice(0, M)
 UNITS = [[(2 * j, cols), (2 * j + 1, cols)] for cols in (LOW, HIGH) for j in range(4)]
@@ -73,15 +73,15 @@ def tile_list_fugue_imitation_gate_kernel(
         tab_code = {}
 
         def load_w1(u, tag):
-            w1_code[u] = keep.tile([P, PASSES_1, H], U8, name=f"w1_code{u}", tag=tag, align_bytes=64)
+            w1_code[u] = laid.tile([P, PASSES_1, H], U8, name=f"w1_code{u}", offset=10240, align_bytes=64)
             nc.sync.dma_start(
                 out=w1_code[u][:].bitcast(I32),
                 in_=w1_i32[:, :, 256 * u : 256 * (u + 1)].rearrange("a p c -> p a c"),
             )
 
         def load_tab(a):
-            if a == 2:
-                tab_code[a] = laid.tile([P, T], U32, name="tab_code2", offset=2048, align_bytes=64)
+            if a != 1:
+                tab_code[a] = laid.tile([P, T], U32, name=f"tab_code{a}", offset=2048 if a else 10240, align_bytes=64)
             else:
                 tab_code[a] = keep.tile([P, T], U32, name=f"tab_code{a}", tag=f"big{a}", align_bytes=64)
             nc.sync.dma_start(
@@ -133,8 +133,8 @@ def tile_list_fugue_imitation_gate_kernel(
         for k, (a, q) in enumerate(moves):
             if k == 5:
                 load_tab(2)
-                w1_next = laid.tile([P, 2, H], U8, name="w1_next", offset=0, align_bytes=64)
-                nc.sync.dma_start(out=w1_next[:].bitcast(I32), in_=w1_i32[1:3, :, 0:256].rearrange("a p c -> p a c"))
+                w1_next = laid.tile([P, 2, BANK], U8, name="w1_next", offset=512, align_bytes=64)
+                nc.sync.dma_start(out=w1_next[:].bitcast(I32), in_=w1_i32[1:3, :, 0:128].rearrange("a p c -> p a c"))
             if k == 8:
                 late_moves = moves[8:]
                 break
@@ -199,6 +199,8 @@ def tile_list_fugue_imitation_gate_kernel(
             queue.dma_start(
                 out=v_scale[a][32 * q : 32 * q + 4, :].bitcast(I32), in_=picked_scale[first : first + 4, :].bitcast(I32)
             )
+        w1_last = laid.tile([P, 2, BANK], U8, name="w1_last", offset=14336, align_bytes=64)
+        nc.sync.dma_start(out=w1_last[:].bitcast(I32), in_=w1_i32[1:3, :, 128:256].rearrange("a p c -> p a c"))
         load_wg(0, "big1", nc.sync)
         load_wg(1, "picked", nc.sync)
         load_wg(2, "big2", nc.sync)
@@ -221,10 +223,15 @@ def tile_list_fugue_imitation_gate_kernel(
 
         def stage1_pass(i, u, a):
             cols = slice(BANK * u, BANK * (u + 1))
-            words = w1_code[1][:, a, :] if i >= 4 else w1_first[:] if a == 0 else w1_next[:, a - 1, :]
+            if i >= 4:
+                words = w1_code[1][:, a, 256 * (i - 4) : 256 * (i - 3)]
+            elif a == 0:
+                words = w1_first[:, 256 * i : 256 * (i + 1)]
+            else:
+                words = (w1_next, w1_last)[i // 2][:, a - 1, 256 * (i % 2) : 256 * (i % 2 + 1)]
             nc.tensor.matmul_mx(
                 out=acc[i, u][:],
-                lhsT=words[:, 256 * (i % 4) : 256 * (i % 4 + 1)].bitcast(FP4X4),
+                lhsT=words.bitcast(FP4X4),
                 lhsT_scale=w1_scale[:, a, P * i : P * (i + 1)],
                 rhs=v_code[a, u][:].bitcast(FP8X4),
                 rhs_scale=v_scale[a][:, cols],
@@ -250,7 +257,7 @@ def tile_list_fugue_imitation_gate_kernel(
                 g = [g for g in GROUPS[halves[0]] if i in g][0]
                 if i == g[0]:
                     tag = f"lead{i}_{halves[0]}"
-                    tile = keep.tile([P, len(g), HALF], F32, name=tag, tag={"act0_0": "v_code00", "act2_0": "v_code01", "act4_0": "w1_scale", "act6_0": "v_scale2", "lead6_1": "v_scale2", "act0_1": "v_code21", "act2_1": "x_turned00", "act4_1": "x_grouped00"}.get(tag, tag), align_bytes=64)
+                    tile = keep.tile([P, len(g), HALF], F32, name=tag, tag={"act0_0": "v_code00", "act2_0": "v_code01", "act4_0": "w1_scale", "act6_0": "v_scale2", "lead6_1": "act7_0", "act0_1": "v_code21", "act2_1": "x_turned00", "act4_1": "x_grouped00"}.get(tag, tag), align_bytes=64)
                     lead[i, halves[0]] = tile[:]
                 dst = lead[g[0], halves[0]][:, i - g[0], :]
             nc.vector.tensor_copy(dst, h[i][:].indirect(pos1_sb[:, 16 * halves[0] : 16 * (halves[-1] + 1)]))
@@ -260,7 +267,10 @@ def tile_list_fugue_imitation_gate_kernel(
         def activate(g, hf):
             n = len(g)
             tag = f"act{g[0]}_{hf}"
-            act = keep.tile([P, n, HALF], F32, name=tag, tag={"act0_0": "v_code00", "act2_0": "v_code01", "act4_0": "w1_scale", "act6_0": "v_scale2", "lead6_1": "v_scale2", "act0_1": "v_code21", "act2_1": "x_turned00", "act4_1": "x_grouped00"}.get(tag, tag), align_bytes=64)
+            if tag in []:
+                act = laid.tile([P, n, HALF], F32, name=tag, offset=14336, align_bytes=64)
+            else:
+                act = keep.tile([P, n, HALF], F32, name=tag, tag={"act0_0": "v_code00", "act2_0": "v_code01", "act4_0": "w1_scale", "act6_0": "v_scale2", "lead6_1": "act7_0", "act0_1": "v_code21", "act2_1": "x_turned00", "act4_1": "x_grouped00"}.get(tag, tag), align_bytes=64)
             nc.scalar.activation(act[:], lead[g[0], hf], ACT.Gelu_apprx_tanh)
             acts[g[0], hf] = act
 
@@ -293,17 +303,19 @@ def tile_list_fugue_imitation_gate_kernel(
 
         def turn_back(b, hf):
             words = x_turned[b, hf][:].rearrange("p mb r -> p (mb r)").bitcast(F32)
-            ps = bank([P, 2, HALF], F32)
-            for mb in range(2):
-                for u in range(2):
-                    nc.tensor.transpose(
-                        ps[:, u, P * mb : P * (mb + 1)], words[:, 256 * mb + u : 256 * (mb + 1) : 2], ident[:]
-                    )
             tag = f"x_grouped{b}{hf}"
             grouped = keep.tile([P, 4 * HALF], BF16, name=tag, tag=tag, align_bytes=64)
-            nc.scalar.copy(
-                grouped[:].bitcast(F32).rearrange("p (m u) -> p m u", u=2), ps[:].rearrange("p u m -> p m u")
-            )
+            for blocks in [[0], [1]] if (b, hf) in [] else [[0, 1]]:
+                ps = bank([P, 2, P * len(blocks)], F32)
+                for k, mb in enumerate(blocks):
+                    for u in range(2):
+                        nc.tensor.transpose(
+                            ps[:, u, P * k : P * (k + 1)], words[:, 256 * mb + u : 256 * (mb + 1) : 2], ident[:]
+                        )
+                nc.scalar.copy(
+                    grouped[:].bitcast(F32)[:, 256 * blocks[0] : 256 * (blocks[-1] + 1)].rearrange("p (m u) -> p m u", u=2),
+                    ps[:].rearrange("p u m -> p m u"),
+                )
             cols = slice(HALF * hf, HALF * (hf + 1))
             nc.vector.quantize_mx(out=x_code[b][:, cols].bitcast(FP8X4), scales=x_scale[b][:, cols], in_=grouped[:])
 
@@ -328,10 +340,12 @@ def tile_list_fugue_imitation_gate_kernel(
         for u in range(2):
             for i in range(EARLY):
                 stage1_pass(i, u, 0)
-        for i in range(EARLY):
-            for a in range(1, PASSES_1):
-                for u in range(2):
+        for pair in range(0, EARLY, 2):
+            for i in (pair, pair + 1):
+                for u, a in ((0, 1), (1, 1), (0, 2)):
                     stage1_pass(i, u, a)
+            for i in (pair, pair + 1):
+                stage1_pass(i, 1, 2)
         keep_rows(0, 0)
         keep_rows(1, 0)
         keep_rows(0, 1)
@@ -349,25 +363,27 @@ def tile_list_fugue_imitation_gate_kernel(
                 leader(i, [0])
             else:
                 leader(i, [0, 1])
+            if i == 7:
+                pass
             for g in GROUPS[0]:
                 if g[-1] == i and i < 0:
                     activate(g, 0)
-            for g, at in zip(GROUPS[0], [8, 8, 8, 8]):
+            for g, at in zip(GROUPS[0], [8, 8, 8, 8, 8]):
                 if at == i:
                     turn_out(g, 0)
                     if g[-1] == 3:
                         turn_back(0, 0)
-        for g, at in zip(GROUPS[0], [8, 8, 8, 8]):
+        for g, at in zip(GROUPS[0], [8, 8, 8, 8, 8]):
             if g[-1] >= 0:
                 activate(g, 0)
             if at == 8:
                 turn_out(g, 0)
-                warm_up({2: 2, 4: 2}.get(g[0], 0), v_code[1, 1], v_scale[1])
-        if [8, 8, 8, 8][1] == 8:
+                warm_up({2: 2}.get(g[0], 0), v_code[1, 1], v_scale[1])
+        if [8, 8, 8, 8, 8][1] == 8:
             turn_back(0, 0)
         warm_up(0, v_code[1, 1], v_scale[1])
         turn_back(1, 0)
-        warm_up(1, v_code[1, 1], v_scale[1])
+        warm_up(3, v_code[1, 1], v_scale[1])
         for late in [6, 7]:
             leader(late, [1])
         for c in range(2):
@@ -399,17 +415,33 @@ def tile_list_fugue_imitation_gate_kernel(
                     )
             return ps
 
+        sums = {}
+
         def products(k):
-            a_ps = product(
-                UNITS[k], lambda b, i: wt_code[:, b, P * i : P * (i + 1)], lambda b, i: wt_scale[:, b, P * i : P * (i + 1)]
+            sums[k] = (
+                [
+                    product(
+                        pieces,
+                        lambda b, i: wt_code[:, b, P * i : P * (i + 1)],
+                        lambda b, i: wt_scale[:, b, P * i : P * (i + 1)],
+                    )
+                    for pieces in ([UNITS[k][:1], UNITS[k][1:]] if k == 0 and False else [UNITS[k]])
+                ],
+                product(
+                    UNITS[k],
+                    lambda b, i: wg_code[i // 4][:, b, P * (i % 4) : P * (i % 4 + 1)],
+                    lambda b, i: wg_scale[i // 4][:, b, P * (i % 4) : P * (i % 4 + 1)],
+                ),
             )
+
+        def squash(k):
+            if k not in sums:
+                products(k)
+            a_ps, g_ps = sums[k]
             answer[k] = ring.tile([P, BANK], F32, name="answer", bufs=4)
-            nc.scalar.activation(answer[k][:], a_ps[:], ACT.Tanh, bias=zero_bias[:])
-            g_ps = product(
-                UNITS[k],
-                lambda b, i: wg_code[i // 4][:, b, P * (i % 4) : P * (i % 4 + 1)],
-                lambda b, i: wg_scale[i // 4][:, b, P * (i % 4) : P * (i % 4 + 1)],
-            )
+            n = BANK // len(a_ps)
+            for g, ps in enumerate(a_ps):
+                nc.scalar.activation(answer[k][:, n * g : n * (g + 1)], ps[:, 0:n], ACT.Tanh, bias=zero_bias[:])
             half_gate[k] = ring.tile([P, BANK], F32, name="half_gate")
             nc.scalar.activation(half_gate[k][:], g_ps[:], ACT.Tanh, bias=zero_bias[:], scale=-0.5)
             diff[k] = ring.tile([P, BANK], F32, name="diff")
@@ -452,7 +484,7 @@ def tile_list_fugue_imitation_gate_kernel(
 
         for k in range(len(UNITS) + 1):
             if k < len(UNITS):
-                products(k)
+                squash(k)
                 follower(k, 0)
             if k >= 1:
                 gated(k - 1)
@@ -460,7 +492,9 @@ def tile_list_fugue_imitation_gate_kernel(
                 follower(k, 1)
             if k >= 1:
                 finish(k - 1)
-            for g, at in zip(GROUPS[1], [0, 1, 1, 2]):
+            if k + 1 in [1, 2]:
+                products(k + 1)
+            for g, at in zip(GROUPS[1], [0, 0, 1, 1]):
                 if at == k:
                     activate(g, 1)
                     turn_out(g, 1)

@@ -24,13 +24,7 @@ ACT = mybir.ActivationFunctionType
 ALU = mybir.AluOpType
 
 EARLY = 4
-GROUPS = [[[0, 1], [2, 3], [4, 5], [6], [7]], [[0, 1], [2, 3], [4, 5], [6, 7]]]
-CAST = ["gpsimd"] * 4
-LOW, HIGH, ALL = slice(0, HALF), slice(HALF, M), slice(0, M)
-UNITS = [[(2 * j, cols), (2 * j + 1, cols)] for cols in (LOW, HIGH) for j in range(4)]
-CAST_TAG = ["wg_pair0", "wg_pair1"]
-CODE_TAG = ["x_turned10", "x_grouped10"]
-PIECES = [2, 2, 2, 2]
+UNITS = [(2 * j, hf) for hf in range(2) for j in range(4)]
 
 
 def tile_list_fugue_imitation_gate_kernel(
@@ -43,467 +37,381 @@ def tile_list_fugue_imitation_gate_kernel(
         ring = ctx.enter_context(tc.tile_pool(name="ring", bufs=3))
         psum = ctx.enter_context(tc.psum_pool(name="psum", bufs=1))
 
-        def bank(shape, dtype):
-            return psum.tile(shape, dtype, name="bank", tag="bank", bufs=8)
+        def bank(n, name, shape, dtype=F32):
+            return psum.tile(shape, dtype, name=name, offset=2048 * n)
 
         offs_sb = keep.tile([P, S // 16], U16, name="offs_sb")
         pos1_sb = keep.tile([P, M // 16], U16, name="pos1_sb")
         pos2_sb = keep.tile([P, M // 16], U16, name="pos2_sb")
-        tab_scale = laid.tile([P, T], U8, name="tab_scale", offset=1024, align_bytes=64)
-        w1_scale = keep.tile([P, PASSES_1, H], U8, name="w1_scale", tag="w1_scale", align_bytes=64)
-        picked_scale = keep.tile([P, S], U8, name="picked_scale", tag="picked", align_bytes=64)
-        v_scale = [keep.tile([P, S], U8, name=f"v_scale{a}", tag=f"v_scale{a}", align_bytes=64) for a in range(PASSES_1)]
-        gain_rows = keep.tile([P, P], F32, name="gain_rows")
+        tab_scale = keep.tile([P, T], U8, name="tab_scale", align_bytes=64)
+        w1_scale = keep.tile([P, PASSES_1, H], U8, name="w1_scale", align_bytes=64)
+        v_scale = [keep.tile([P, S], U8, name=f"v_scale{a}", align_bytes=64) for a in range(PASSES_1)]
         zero_col = keep.tile([P, 1], F32, name="zero_col")
         zero_bias = keep.tile([P, 1], F32, name="zero_bias")
         ident = keep.tile([P, P], F32, name="ident")
-
-        for rows in (slice(32, 64), slice(64, 112)):
-            nc.vector.memset(tab_scale[rows, :].bitcast(I32), 0)
-        nc.vector.memset(zero_col[:], 0.0)
-        for rows in (slice(0, 24), slice(32, 64), slice(64, P)):
-            nc.vector.memset(gain_rows[rows, :].bitcast(I32), 0)
-        nc.gpsimd.dma_start(out=gain_rows[24:32, :], in_=gain.rearrange("(i p) -> i p", p=P))
-        make_identity(nc, ident[:])
         ident_bf16 = keep.tile([P, P], BF16, name="ident_bf16")
+
+        nc.gpsimd.memset(tab_scale[0:112, :].bitcast(I32), 0)
+        nc.vector.memset(zero_col[:], 0.0)
+        nc.scalar.activation(zero_bias[:], zero_col[:], ACT.Gelu_apprx_tanh)
+        gain_rows = keep.tile([P, P], F32, name="gain_rows")
+        gain_col = keep.tile([P, ROW_TILES], F32, name="gain_col")
+        nc.vector.memset(gain_rows[:], 0.0)
+        nc.scalar.dma_start(out=gain_rows[0:ROW_TILES, :], in_=gain.rearrange("(i p) -> i p", p=P))
+        make_identity(nc, ident[:])
         make_identity(nc, ident_bf16[:])
+        ps = bank(7, "gain_turned", [P, P])
+        nc.tensor.transpose(ps[:], gain_rows[:], ident[:])
+        nc.scalar.copy(gain_col[:], ps[:, 0:ROW_TILES])
 
         w1_i32 = w1_words.bitcast(I32)
-        w1_code = {}
+        tab_rows = tab_scales.bitcast(I32)
         tab_code = {}
 
-        def load_w1(u, tag):
-            w1_code[u] = laid.tile([P, PASSES_1, H], U8, name=f"w1_code{u}", offset=10240, align_bytes=64)
-            nc.sync.dma_start(
-                out=w1_code[u][:].bitcast(I32),
-                in_=w1_i32[:, :, 256 * u : 256 * (u + 1)].rearrange("a p c -> p a c"),
-            )
-
         def load_tab(a):
-            if a != 1:
-                tab_code[a] = laid.tile([P, T], U32, name=f"tab_code{a}", offset=2048 if a else 10240, align_bytes=64)
-            else:
-                tab_code[a] = keep.tile([P, T], U32, name=f"tab_code{a}", tag=f"big{a}", align_bytes=64)
+            tab_code[a] = keep.tile([P, T], U32, name=f"tab_code{a}", tag=f"big{a}", align_bytes=64)
             nc.sync.dma_start(
                 out=tab_code[a][:].bitcast(I32),
                 in_=tab_words[a].rearrange("p t i -> p (t i)").bitcast(I32),
             )
 
-        def load_scale_rows(queues, plane, rows):
+        def load_w1(name, passes, tiles):
+            tile = keep.tile([P, len(passes), 256 * len(tiles)], U8, name=name, align_bytes=64)
+            nc.sync.dma_start(
+                out=tile[:].bitcast(I32),
+                in_=w1_i32[passes.start : passes.stop, :, 64 * tiles.start : 64 * tiles.stop].rearrange("a p c -> p a c"),
+            )
+            for a in passes:
+                for i in tiles:
+                    w1_code[a, i] = tile[:, a - passes.start, 256 * (i - tiles.start) : 256 * (i - tiles.start + 1)]
+
+        def load_scale_rows(plane, rows):
             for q in range(4):
-                queues[q].dma_start(
+                nc.sync.dma_start(
                     out=plane[32 * q : 32 * q + 4, :, :].bitcast(I32),
                     in_=rows.bitcast(I32)[:, 4 * q : 4 * q + 4, :].rearrange("a r c -> r a c"),
                 )
 
-        tab_rows = tab_scales.bitcast(I32)
+        def move_scale_rows(a):
+            for q in range(4):
+                first = 32 * q + 4 if a == 1 else 112 + 4 * q
+                nc.sync.dma_start(
+                    out=v_scale[a][32 * q : 32 * q + 4, :].bitcast(I32), in_=v_scale[0][first : first + 4, :].bitcast(I32)
+                )
+
+        w1_code = {}
         nc.sync.dma_start(offs_sb[:], offs)
-        nc.sync.dma_start(pos1_sb[:], pos1)
-        nc.sync.dma_start(pos2_sb[:], pos2)
-        nc.scalar.dma_start(out=tab_scale[0:32, :].bitcast(I32), in_=tab_rows[0:2].rearrange("a q c -> (a q) c"))
-        nc.scalar.dma_start(out=tab_scale[112:128, :].bitcast(I32), in_=tab_rows[2])
+        nc.sync.dma_start(out=tab_scale[112:128, :].bitcast(I32), in_=tab_rows[2])
+        for q in range(4):
+            nc.sync.dma_start(
+                out=tab_scale[32 * q : 32 * q + 8, :].bitcast(I32), in_=tab_rows[0:2, 4 * q : 4 * q + 4, :]
+            )
         load_tab(0)
-        load_scale_rows([nc.scalar, nc.scalar, nc.sync, nc.sync], w1_scale, w1_scales)
-        nc.scalar.activation(zero_bias[:], zero_col[:], ACT.Gelu_apprx_tanh)
-        ps = bank([P, BANK], F32)
-        nc.tensor.transpose(ps[:, 0:P], gain_rows[:], ident[:])
-        gain_col = keep.tile([P, ROW_TILES], F32, name="gain_col")
-        nc.scalar.copy(gain_col[:], ps[:, 24:32])
-        gain_all = keep.tile([P, H], F32, name="gain_all")
-        for b in range(PASSES_2):
-            ps = bank([P, BANK], F32)
-            for k in range(4):
-                i = 4 * b + k
-                nc.tensor.transpose(ps[:, P * k : P * (k + 1)], gain_col[:, i : i + 1].to_broadcast([P, P]), ident[:])
-            nc.scalar.copy(gain_all[:, BANK * b : BANK * (b + 1)], ps[:])
-
-
+        load_scale_rows(w1_scale, w1_scales)
+        load_w1("w1_first", range(0, 2), range(0, EARLY))
         load_tab(1)
-        w1_first = keep.tile([P, H], U8, name="w1_first", align_bytes=64)
-        nc.sync.dma_start(out=w1_first[:].bitcast(I32), in_=w1_i32[0, :, 0:256])
+        nc.vector.tensor_copy(v_scale[0][:], tab_scale[:].indirect(offs_sb[:]))
+        move_scale_rows(1)
+        load_tab(2)
+        move_scale_rows(2)
+        load_w1("w1_next", range(2, 3), range(0, EARLY))
+        load_w1("w1_last", range(0, 3), range(EARLY, ROW_TILES))
+        nc.sync.dma_start(pos1_sb[:], pos1)
+
+        def column_pieces(a, u):
+            return [slice(0, HALF), slice(HALF, BANK)] if (a, u) == (0, 0) else [slice(0, BANK)]
 
         v_code = {}
-
-        def gather_words(a, u, tag):
-            v_code[a, u] = keep.tile([P, BANK], U32, name=f"v_code{a}{u}", tag=tag, align_bytes=64)
-            nc.vector.tensor_copy(v_code[a, u][:], tab_code[a][:].indirect(offs_sb[:, 32 * u : 32 * (u + 1)]))
-
-        nc.vector.tensor_copy(picked_scale[:], tab_scale[:].indirect(offs_sb[:]))
-        moves = [(a, q) for a in range(PASSES_1) for q in range(4)]
-        for k, (a, q) in enumerate(moves):
-            if k == 5:
-                load_tab(2)
-                w1_next = laid.tile([P, 2, BANK], U8, name="w1_next", offset=512, align_bytes=64)
-                nc.sync.dma_start(out=w1_next[:].bitcast(I32), in_=w1_i32[1:3, :, 0:128].rearrange("a p c -> p a c"))
-            if k == 8:
-                late_moves = moves[8:]
-                break
-            first = (0, 16, 112)[a] + 4 * q
-            queue = nc.gpsimd if k in [10, 11] else nc.sync
-            queue.dma_start(
-                out=v_scale[a][32 * q : 32 * q + 4, :].bitcast(I32), in_=picked_scale[first : first + 4, :].bitcast(I32)
-            )
         for a in range(PASSES_1):
             for u in range(2):
-                gather_words(a, u, f"v_code{a}{u}")
-
-        chunks = [(b, u) for u in range(2) for b in range(PASSES_2)]
-        wg_raw = {}
-        wg_grouped = {}
-        wg_pair = {}
-        wg_code = {}
-        wg_scale = {}
-
-        def load_wg(c, tag, queue):
-            b, u = chunks[c]
-            rows = wg[512 * b : 512 * (b + 1), :].rearrange("(p j) n -> p j n", j=4)
-            if tag == "big2":
-                wg_raw[c] = laid.tile([P, 4, BANK], F32, name=f"wg_raw{c}", offset=2048, align_bytes=64)
-            else:
-                wg_raw[c] = keep.tile([P, 4, BANK], F32, name=f"wg_raw{c}", tag=tag, align_bytes=64)
-            queue.dma_start(out=wg_raw[c][:], in_=rows[:, :, BANK * u : BANK * (u + 1)])
-
-        def cast_wg(c):
-            b, u = chunks[c]
-            if b == 0:
-                wg_pair[u] = keep.tile([P, PASSES_2, BANK, 4], BF16, name=f"wg_pair{u}", tag=CAST_TAG[u], align_bytes=64)
-            wg_grouped[c] = wg_pair[u][:, b, :, :]
-            for s in range(PIECES[c]):
-                cols = slice(BANK // PIECES[c] * s, BANK // PIECES[c] * (s + 1))
-                if CAST[c] == "gpsimd":
-                    nc.gpsimd.tensor_scalar(
-                        wg_grouped[c][:, cols, :], wg_raw[c][:, :, cols].rearrange("p j n -> p n j"),
-                        1.0, 0.0, ALU.mult, ALU.add,
+                v_code[a, u] = keep.tile([P, BANK], U32, name=f"v_code{a}{u}", tag=f"v_code{a}{u}", align_bytes=64)
+                for cols in column_pieces(a, u):
+                    nc.vector.tensor_copy(
+                        v_code[a, u][:, cols],
+                        tab_code[a][:].indirect(offs_sb[:, 32 * u + cols.start // 16 : 32 * u + cols.stop // 16]),
                     )
-                else:
-                    src = wg_raw[c][:, :, cols].rearrange("p j (n i) -> p n j i", i=4)
-                    dst = wg_grouped[c][:, cols, :].rearrange("p (n i) j -> p n j i", i=4)
-                    if CAST[c] == "vector":
-                        nc.vector.tensor_copy(dst, src)
-                    else:
-                        nc.scalar.copy(dst, src)
 
-        def quant_wg(u):
-            wg_code[u] = keep.tile([P, PASSES_2, BANK], U32, name=f"wg_code{u}", tag=CODE_TAG[u], align_bytes=64)
-            wg_scale[u] = keep.tile([P, PASSES_2, BANK], U8, name=f"wg_scale{u}", align_bytes=64)
+        wg_pair = [laid.tile([P, PASSES_2, BANK, 4], BF16, name=f"wg_pair{u}", offset=8192 * (u + 1), align_bytes=64) for u in range(2)]
+
+        def load_and_cast_wg(u, b, tag):
+            rows = wg[512 * b : 512 * (b + 1), :].rearrange("(p j) n -> p j n", j=4)
+            raw = keep.tile([P, 4, BANK], F32, name=f"wg_raw{u}{b}", tag=tag, align_bytes=64)
+            nc.sync.dma_start(out=raw[:], in_=rows[:, :, BANK * u : BANK * (u + 1)])
+            for s in range(2):
+                cols = slice(HALF * s, HALF * (s + 1))
+                nc.gpsimd.tensor_scalar(
+                    wg_pair[u][:, b, cols, :], raw[:, :, cols].rearrange("p j n -> p n j"), 1.0, 0.0, ALU.mult, ALU.add
+                )
+
+        gain_word = keep.tile([P, PASSES_2, 4], F32, name="gain_word")
+        load_and_cast_wg(0, 0, "big0")
+        load_and_cast_wg(0, 1, "big1")
+        nc.gpsimd.dma_start(out=gain_word[:], in_=gain.rearrange("(b p t) -> p b t", b=PASSES_2, t=4))
+        wt_code = keep.tile([P, PASSES_2, H], U32, name="wt_code", align_bytes=64)
+        nc.sync.dma_start(out=wt_code[:].bitcast(I32), in_=wt_words.rearrange("a p c i -> p a (c i)").bitcast(I32))
+        wt_scale = keep.tile([P, PASSES_2, H], U8, name="wt_scale", align_bytes=64)
+        load_scale_rows(wt_scale, wt_scales)
+        nc.sync.dma_start(pos2_sb[:], pos2)
+        load_and_cast_wg(1, 0, "big2")
+        load_and_cast_wg(1, 1, "big0")
+
+        acc = {}
+        h = [keep.tile([P, S], F32, name=f"h{i}") for i in range(ROW_TILES)]
+        lead = {}
+
+        def stage1_pass(i, u, a, cols=slice(0, BANK)):
+            if a == 0 and cols.start == 0:
+                acc[i, u] = bank((2 * i + u) % 8, f"acc{i}{u}", [P, BANK])
+            nc.tensor.matmul_mx(
+                out=acc[i, u][:, cols],
+                lhsT=w1_code[a, i].bitcast(FP4X4),
+                lhsT_scale=w1_scale[:, a, P * i : P * (i + 1)],
+                rhs=v_code[a, u][:, cols].bitcast(FP8X4),
+                rhs_scale=v_scale[a][:, BANK * u + cols.start : BANK * u + cols.stop],
+                start=(a == 0 and cols.start == 0),
+                stop=(a == PASSES_1 - 1),
+            )
+
+        def keep_rows(i, u):
+            if u == 0 and i in (1, 3):
+                nc.vector.tensor_copy(h[i][:, BANK * u : BANK * (u + 1)], acc[i, u][:])
+            else:
+                nc.scalar.copy(h[i][:, BANK * u : BANK * (u + 1)], acc[i, u][:])
+
+        def leader(dst, i, halves):
+            nc.vector.tensor_copy(dst, h[i][:].indirect(pos1_sb[:, 16 * halves[0] : 16 * (halves[-1] + 1)]))
+
+        act_turned = [keep.tile([P, 2, 4, P], F32, name=f"act_turned{b}", align_bytes=64) for b in range(PASSES_2)]
+
+        def first_out(tiles, n):
+            ps = bank(n, f"out0{tiles[0]}", [P, 2, len(tiles) * P])
+            for k, i in enumerate(tiles):
+                for mb in range(2):
+                    nc.tensor.transpose(ps[:, mb, P * k : P * (k + 1)], lead[i, 0][:, P * mb : P * (mb + 1)], ident[:])
+            nc.scalar.activation(
+                act_turned[tiles[0] // 4][:, :, :, 32 * (tiles[0] % 4) : 32 * (tiles[-1] % 4 + 1)],
+                ps[:].rearrange("m mb (p t) -> m mb t p", t=4),
+                ACT.Gelu_apprx_tanh,
+            )
+
+        for cols in column_pieces(0, 0):
+            for i in range(EARLY):
+                stage1_pass(i, 0, 0, cols)
+        for a in range(PASSES_1):
+            for u in range(2):
+                for i in range(EARLY):
+                    if (a, u) != (0, 0):
+                        stage1_pass(i, u, a)
+        for i in range(EARLY):
+            keep_rows(i, 0)
+        last_first = [
+            keep.tile([P, HALF], F32, name="lead6_first"),
+            laid.tile([P, HALF], F32, name="lead7_first", offset=3072, align_bytes=64),
+        ]
+        for i in range(ROW_TILES):
+            if i >= EARLY:
+                for u in range(2):
+                    for a in range(PASSES_1):
+                        stage1_pass(i, u, a)
+                keep_rows(i, 0)
+            keep_rows(i, 1)
+            if i < 6:
+                if i % 2 == 0:
+                    pair = keep.tile([P, 2, M], F32, name=f"lead{i}")
+                leader(pair[:, i % 2, :], i, [0, 1])
+                for hf in range(2):
+                    lead[i, hf] = pair[:, i % 2, HALF * hf : HALF * (hf + 1)]
+                    lead[i - i % 2, "pair", hf] = pair[:, :, HALF * hf : HALF * (hf + 1)]
+            else:
+                leader(last_first[i - 6][:], i, [0])
+                lead[i, 0] = last_first[i - 6][:]
+
+        x_grouped = [
+            laid.tile([P, PASSES_2, 4 * HALF], BF16, name="x_grouped0", offset=26624, align_bytes=64),
+            keep.tile([P, PASSES_2, 4 * HALF], BF16, name="x_grouped1", align_bytes=64),
+        ]
+        x_code = {0: keep.tile([P, PASSES_2, HALF], U32, name="x_code0", align_bytes=64)}
+        x_scale = [keep.tile([P, PASSES_2, HALF], U8, name=f"x_scale{hf}", align_bytes=64) for hf in range(2)]
+
+        def quantize_x(hf, passes):
+            nc.vector.quantize_mx(
+                out=x_code[hf][:, passes, :].rearrange("p b m -> p (b m)").bitcast(FP8X4),
+                scales=x_scale[hf][:, passes, :].rearrange("p b m -> p (b m)"),
+                in_=x_grouped[hf][:, passes, :].rearrange("p b m -> p (b m)"),
+            )
+
+        for tiles, n in (((0, 1), 4), ((2, 3), 5), ((4, 5), 6), ((6,), 3), ((7,), 7)):
+            first_out(tiles, n)
+        for b in range(PASSES_2):
+            act = act_turned[b]
+            for mb in range(2):
+                ps = bank([[0, 1], [2, 4]][b][mb], f"back0{b}{mb}", [P, 4, P])
+                for t in range(4):
+                    nc.tensor.transpose(ps[:, t, :], act[:, mb, t, :], ident[:])
+                nc.vector.tensor_tensor(
+                    x_grouped[0][:, b, BANK * mb : BANK * (mb + 1)].rearrange("p (m t) -> p m t", t=4),
+                    ps[:].rearrange("p t m -> p m t"),
+                    gain_word[:, b, :].unsqueeze(1).to_broadcast([P, P, 4]),
+                    ALU.mult,
+                )
+            quantize_x(0, slice(b, b + 1))
+
+        last_second = [
+            laid.tile([P, HALF], F32, name="lead6_second", offset=2560, align_bytes=64),
+            keep.tile([P, HALF], F32, name="lead7_second"),
+        ]
+        for i in (7, 6):
+            leader(last_second[i - 6][:], i, [1])
+            lead[i, 1] = last_second[i - 6][:]
+
+        wg_code = [
+            laid.tile([P, PASSES_2, BANK], U32, name=f"wg_code{u}", offset=24576 + 4096 * u, align_bytes=64)
+            for u in range(2)
+        ]
+        wg_scale = [keep.tile([P, PASSES_2, BANK], U8, name=f"wg_scale{u}", align_bytes=64) for u in range(2)]
+        for u in range(2):
             nc.vector.quantize_mx(
                 out=wg_code[u][:].rearrange("p b n -> p (b n)").bitcast(FP8X4),
                 scales=wg_scale[u][:].rearrange("p b n -> p (b n)"),
                 in_=wg_pair[u][:].rearrange("p b n j -> p (b n j)"),
             )
 
-        load_w1(1, "big0")
-        for k, (a, q) in enumerate(late_moves):
-            first = 112 + 4 * q
-            queue = nc.gpsimd if k + 8 in [10, 11] else nc.sync
-            queue.dma_start(
-                out=v_scale[a][32 * q : 32 * q + 4, :].bitcast(I32), in_=picked_scale[first : first + 4, :].bitcast(I32)
-            )
-        w1_last = laid.tile([P, 2, BANK], U8, name="w1_last", offset=14336, align_bytes=64)
-        nc.sync.dma_start(out=w1_last[:].bitcast(I32), in_=w1_i32[1:3, :, 128:256].rearrange("a p c -> p a c"))
-        load_wg(0, "big1", nc.sync)
-        load_wg(1, "picked", nc.sync)
-        load_wg(2, "big2", nc.sync)
-        cast_wg(0)
-        load_wg(3, "big1", nc.sync)
-        cast_wg(1)
-        wt_code = keep.tile([P, PASSES_2, H], U32, name="wt_code", tag="picked", align_bytes=64)
-        nc.sync.dma_start(out=wt_code[:].bitcast(I32), in_=wt_words.rearrange("a p c i -> p a (c i)").bitcast(I32))
-        cast_wg(2)
-        wt_scale = laid.tile([P, PASSES_2, H], U8, name="wt_scale", offset=2048, align_bytes=64)
-        load_scale_rows([nc.sync] * 4, wt_scale, wt_scales)
-        cast_wg(3)
-
-        acc = {}
-        h = [keep.tile([P, S], F32, name=f"h{i}") for i in range(ROW_TILES)]
-        lead = {}
         x_turned = {}
-        x_code = [keep.tile([P, M], U32, name=f"x_code{b}", tag=["x_code0", "x_code1"][b], align_bytes=64) for b in range(PASSES_2)]
-        x_scale = [keep.tile([P, M], U8, name=f"x_scale{b}", align_bytes=64) for b in range(PASSES_2)]
 
-        def stage1_pass(i, u, a):
-            cols = slice(BANK * u, BANK * (u + 1))
-            if i >= 4:
-                words = w1_code[1][:, a, 256 * (i - 4) : 256 * (i - 3)]
-            elif a == 0:
-                words = w1_first[:, 256 * i : 256 * (i + 1)]
+        def second_out(j, n):
+            b = j // 2
+            if j % 2 == 0:
+                act = keep.tile([P, 2, HALF], F32, name=f"act{j}", tag="v_code21", align_bytes=64)
             else:
-                words = (w1_next, w1_last)[i // 2][:, a - 1, 256 * (i % 2) : 256 * (i % 2 + 1)]
-            nc.tensor.matmul_mx(
-                out=acc[i, u][:],
-                lhsT=words.bitcast(FP4X4),
-                lhsT_scale=w1_scale[:, a, P * i : P * (i + 1)],
-                rhs=v_code[a, u][:].bitcast(FP8X4),
-                rhs_scale=v_scale[a][:, cols],
-                start=(a == 0),
-                stop=(a == PASSES_1 - 1),
+                act = laid.tile([P, 2, HALF], F32, name=f"act{j}", offset=3584, align_bytes=64)
+            if j < 3:
+                nc.scalar.activation(act[:], lead[2 * j, "pair", 1], ACT.Gelu_apprx_tanh)
+            else:
+                for k in range(2):
+                    nc.scalar.activation(act[:, k, :], lead[2 * j + k, 1], ACT.Gelu_apprx_tanh)
+            if j % 2 == 0:
+                x_turned[b] = keep.tile([P, 2, BANK], BF16, name=f"x_turned{b}", align_bytes=64)
+            rows = keep.tile([P, 2, HALF], BF16, name=f"x_rows{j}")
+            ps = bank(n, f"out1{j}", [P, 2, 2 * P], BF16)
+            for k in range(2):
+                nc.scalar.activation(rows[:, k, :], act[:, k, :], ACT.Copy, scale=gain_col[:, 2 * j + k : 2 * j + k + 1])
+                for mb in range(2):
+                    nc.tensor.transpose(ps[:, mb, P * k : P * (k + 1)], rows[:, k, P * mb : P * (mb + 1)], ident_bf16[:])
+            dst = x_turned[b][:, :, 2 * P * (j % 2) : 2 * P * (j % 2 + 1)]
+            nc.scalar.copy(dst.bitcast(F32), ps[:].bitcast(F32))
+
+        def second_back(b, n):
+            words = x_turned[b][:].rearrange("p mb r -> p (mb r)").bitcast(F32)
+            ps = bank(n, f"back1{b}", [P, 2, 2 * P])
+            for mb in range(2):
+                for u in range(2):
+                    nc.tensor.transpose(ps[:, u, P * mb : P * (mb + 1)], words[:, 256 * mb + u : 256 * (mb + 1) : 2], ident[:])
+            nc.scalar.copy(
+                x_grouped[1][:, b, :].bitcast(F32).rearrange("p (m u) -> p m u", u=2), ps[:].rearrange("p u m -> p m u")
             )
 
-        def keep_rows(i, u):
-            if (i, u) in [(1, 0)]:
-                nc.vector.tensor_copy(h[i][:, BANK * u : BANK * (u + 1)], acc[i, u][:])
-            else:
-                nc.scalar.copy(h[i][:, BANK * u : BANK * (u + 1)], acc[i, u][:])
-
-        def leader(i, halves):
-            if len(halves) == 2:
-                if i % 2 == 0:
-                    pair = keep.tile([P, 2, 2, HALF], F32, name=f"lead{i}")
-                    for hf in range(2):
-                        lead[i, hf] = pair[:, :, hf, :]
-                    lead[i, 2] = pair
-                dst = lead[i - i % 2, 2][:, i % 2, :, :].rearrange("p a m -> p (a m)")
-            else:
-                g = [g for g in GROUPS[halves[0]] if i in g][0]
-                if i == g[0]:
-                    tag = f"lead{i}_{halves[0]}"
-                    tile = keep.tile([P, len(g), HALF], F32, name=tag, tag={"act0_0": "v_code00", "act2_0": "v_code01", "act4_0": "w1_scale", "act6_0": "v_scale2", "lead6_1": "act7_0", "act0_1": "v_code21", "act2_1": "x_turned00", "act4_1": "x_grouped00"}.get(tag, tag), align_bytes=64)
-                    lead[i, halves[0]] = tile[:]
-                dst = lead[g[0], halves[0]][:, i - g[0], :]
-            nc.vector.tensor_copy(dst, h[i][:].indirect(pos1_sb[:, 16 * halves[0] : 16 * (halves[-1] + 1)]))
-
-        acts = {}
-
-        def activate(g, hf):
-            n = len(g)
-            tag = f"act{g[0]}_{hf}"
-            if tag in []:
-                act = laid.tile([P, n, HALF], F32, name=tag, offset=14336, align_bytes=64)
-            else:
-                act = keep.tile([P, n, HALF], F32, name=tag, tag={"act0_0": "v_code00", "act2_0": "v_code01", "act4_0": "w1_scale", "act6_0": "v_scale2", "lead6_1": "act7_0", "act0_1": "v_code21", "act2_1": "x_turned00", "act4_1": "x_grouped00"}.get(tag, tag), align_bytes=64)
-            nc.scalar.activation(act[:], lead[g[0], hf], ACT.Gelu_apprx_tanh)
-            acts[g[0], hf] = act
-
-        def turn_out(g, hf):
-            n, b = len(g), g[0] // 4
-            act = acts[g[0], hf]
-            if (b, hf) not in x_turned:
-                tag = f"x_turned{b}{hf}"
-                x_turned[b, hf] = keep.tile([P, 2, BANK], BF16, name=tag, tag=tag, align_bytes=64)
-            first = P * (g[0] % 4)
-            dst = x_turned[b, hf][:, :, first : first + n * P]
-            if (g[0], hf) in [(0, 1), (2, 1), (4, 1), (6, 1)]:
-                rows = ring.tile([P, n, HALF], BF16, name="x_rows")
-                ps = bank([P, 2, n * P], BF16)
-                for k in range(n):
-                    nc.scalar.activation(rows[:, k, :], act[:, k, :], ACT.Copy, scale=gain_col[:, g[k] : g[k] + 1])
-                    for mb in range(2):
-                        nc.tensor.transpose(
-                            ps[:, mb, P * k : P * (k + 1)], rows[:, k, P * mb : P * (mb + 1)], ident_bf16[:]
-                        )
-                nc.scalar.copy(dst.bitcast(F32), ps[:].bitcast(F32))
-            else:
-                ps = bank([P, 2, n * P], F32)
-                for k in range(n):
-                    for mb in range(2):
-                        nc.tensor.transpose(ps[:, mb, P * k : P * (k + 1)], act[:, k, P * mb : P * (mb + 1)], ident[:])
-                nc.vector.tensor_tensor(
-                    dst, ps[:], gain_all[:, P * g[0] : P * (g[0] + n)].unsqueeze(1).to_broadcast([P, 2, n * P]), ALU.mult
-                )
-
-        def turn_back(b, hf):
-            words = x_turned[b, hf][:].rearrange("p mb r -> p (mb r)").bitcast(F32)
-            tag = f"x_grouped{b}{hf}"
-            grouped = keep.tile([P, 4 * HALF], BF16, name=tag, tag=tag, align_bytes=64)
-            for blocks in [[0], [1]] if (b, hf) in [] else [[0, 1]]:
-                ps = bank([P, 2, P * len(blocks)], F32)
-                for k, mb in enumerate(blocks):
-                    for u in range(2):
-                        nc.tensor.transpose(
-                            ps[:, u, P * k : P * (k + 1)], words[:, 256 * mb + u : 256 * (mb + 1) : 2], ident[:]
-                        )
-                nc.scalar.copy(
-                    grouped[:].bitcast(F32)[:, 256 * blocks[0] : 256 * (blocks[-1] + 1)].rearrange("p (m u) -> p m u", u=2),
-                    ps[:].rearrange("p u m -> p m u"),
-                )
-            cols = slice(HALF * hf, HALF * (hf + 1))
-            nc.vector.quantize_mx(out=x_code[b][:, cols].bitcast(FP8X4), scales=x_scale[b][:, cols], in_=grouped[:])
-
-        def warm_up(count, code, scale):
-            for k in range(count):
-                if k == 0:
-                    idle = bank([P, BANK], F32)
-                nc.tensor.matmul_mx(
-                    out=idle[:],
-                    lhsT=code[:, 0:P].bitcast(FP8X4),
-                    lhsT_scale=scale[:, 0:P],
-                    rhs=code[:].bitcast(FP8X4),
-                    rhs_scale=scale[:, 0:BANK],
-                    start=True,
-                    stop=True,
-                )
-
-        warm_up(3, v_code[0, 0], picked_scale)
-        for i in range(EARLY):
-            for u in range(2):
-                acc[i, u] = bank([P, BANK], F32)
-        for u in range(2):
-            for i in range(EARLY):
-                stage1_pass(i, u, 0)
-        for pair in range(0, EARLY, 2):
-            for i in (pair, pair + 1):
-                for u, a in ((0, 1), (1, 1), (0, 2)):
-                    stage1_pass(i, u, a)
-            for i in (pair, pair + 1):
-                stage1_pass(i, 1, 2)
-        keep_rows(0, 0)
-        keep_rows(1, 0)
-        keep_rows(0, 1)
-        for i in range(ROW_TILES):
-            if i + 1 < ROW_TILES:
-                keep_rows(i + 1, 1)
-            if i + 2 < ROW_TILES:
-                keep_rows(i + 2, 0)
-            if i + EARLY < ROW_TILES:
-                for u in range(2):
-                    acc[i + EARLY, u] = bank([P, BANK], F32)
-                    for a in range(PASSES_1):
-                        stage1_pass(i + EARLY, u, a)
-            if i in [6, 7]:
-                leader(i, [0])
-            else:
-                leader(i, [0, 1])
-            if i == 7:
-                pass
-            for g in GROUPS[0]:
-                if g[-1] == i and i < 0:
-                    activate(g, 0)
-            for g, at in zip(GROUPS[0], [8, 8, 8, 8, 8]):
-                if at == i:
-                    turn_out(g, 0)
-                    if g[-1] == 3:
-                        turn_back(0, 0)
-        for g, at in zip(GROUPS[0], [8, 8, 8, 8, 8]):
-            if g[-1] >= 0:
-                activate(g, 0)
-            if at == 8:
-                turn_out(g, 0)
-                warm_up({2: 2}.get(g[0], 0), v_code[1, 1], v_scale[1])
-        if [8, 8, 8, 8, 8][1] == 8:
-            turn_back(0, 0)
-        warm_up(0, v_code[1, 1], v_scale[1])
-        turn_back(1, 0)
-        warm_up(3, v_code[1, 1], v_scale[1])
-        for late in [6, 7]:
-            leader(late, [1])
-        for c in range(2):
-            if c not in [0, 1, 2, 3]:
-                cast_wg(c)
-        quant_wg(0)
-        if [] == []:
-            quant_wg(1)
-
-        turned = []
         answer = {}
         half_gate = {}
         diff = {}
         step = {}
 
-        def product(pieces, code, scale):
-            ps = bank([P, BANK], F32)
+        def product(k, name, n, code, scale):
+            first, hf = UNITS[k]
+            ps = bank(n, f"{name}{k}", [P, BANK])
             for b in range(PASSES_2):
-                for g, (i, cols) in enumerate(pieces):
-                    n = cols.stop - cols.start
+                for g in range(2):
                     nc.tensor.matmul_mx(
-                        out=ps[:, n * g : n * (g + 1)],
-                        lhsT=code(b, i).bitcast(FP8X4),
-                        lhsT_scale=scale(b, i),
-                        rhs=x_code[b][:, cols].bitcast(FP8X4),
-                        rhs_scale=x_scale[b][:, cols],
+                        out=ps[:, HALF * g : HALF * (g + 1)],
+                        lhsT=code(b, first + g).bitcast(FP8X4),
+                        lhsT_scale=scale(b, first + g),
+                        rhs=x_code[hf][:, b, :].bitcast(FP8X4),
+                        rhs_scale=x_scale[hf][:, b, :],
                         start=(b == 0 and g == 0),
-                        stop=(b == PASSES_2 - 1 and g == len(pieces) - 1),
+                        stop=(b == PASSES_2 - 1 and g == 1),
                     )
             return ps
 
-        sums = {}
-
-        def products(k):
-            sums[k] = (
-                [
-                    product(
-                        pieces,
-                        lambda b, i: wt_code[:, b, P * i : P * (i + 1)],
-                        lambda b, i: wt_scale[:, b, P * i : P * (i + 1)],
-                    )
-                    for pieces in ([UNITS[k][:1], UNITS[k][1:]] if k == 0 and False else [UNITS[k]])
-                ],
-                product(
-                    UNITS[k],
-                    lambda b, i: wg_code[i // 4][:, b, P * (i % 4) : P * (i % 4 + 1)],
-                    lambda b, i: wg_scale[i // 4][:, b, P * (i % 4) : P * (i % 4 + 1)],
-                ),
+        def propose(k, n):
+            ps = product(
+                k, "answer_sum", n,
+                lambda b, i: wt_code[:, b, P * i : P * (i + 1)],
+                lambda b, i: wt_scale[:, b, P * i : P * (i + 1)],
             )
+            if k == 0:
+                answer[k] = keep.tile([P, BANK], F32, name="first_answer", tag="first_answer", align_bytes=64)
+            else:
+                answer[k] = ring.tile([P, BANK], F32, name="answer", bufs=4)
+            nc.scalar.activation(answer[k][:], ps[:], ACT.Tanh, bias=zero_bias[:])
 
-        def squash(k):
-            if k not in sums:
-                products(k)
-            a_ps, g_ps = sums[k]
-            answer[k] = ring.tile([P, BANK], F32, name="answer", bufs=4)
-            n = BANK // len(a_ps)
-            for g, ps in enumerate(a_ps):
-                nc.scalar.activation(answer[k][:, n * g : n * (g + 1)], ps[:, 0:n], ACT.Tanh, bias=zero_bias[:])
-            half_gate[k] = ring.tile([P, BANK], F32, name="half_gate")
-            nc.scalar.activation(half_gate[k][:], g_ps[:], ACT.Tanh, bias=zero_bias[:], scale=-0.5)
-            diff[k] = ring.tile([P, BANK], F32, name="diff")
+        def weigh(k, n):
+            ps = product(
+                k, "gate_sum", n,
+                lambda b, i: wg_code[i // 4][:, b, P * (i % 4) : P * (i % 4 + 1)],
+                lambda b, i: wg_scale[i // 4][:, b, P * (i % 4) : P * (i % 4 + 1)],
+            )
+            half_gate[k] = ring.tile([P, BANK], F32, name="half_gate", bufs=4)
+            nc.scalar.activation(half_gate[k][:], ps[:], ACT.Tanh, bias=zero_bias[:], scale=-0.5)
 
         def follower(k, g):
-            if g < len(UNITS[k]):
-                i, cols = UNITS[k][g]
-                n = cols.stop - cols.start
-                nc.vector.tensor_tensor(
-                    diff[k][:, n * g : n * (g + 1)],
-                    h[i][:].indirect(pos2_sb[:, cols.start // 16 : cols.stop // 16]),
-                    answer[k][:, n * g : n * (g + 1)],
-                    ALU.subtract,
-                )
+            first, hf = UNITS[k]
+            if g == 0:
+                diff[k] = laid.tile([P, BANK], F32, name=f"diff{k}", offset=16384 + 2048 * (k % 4), align_bytes=64)
+            nc.vector.tensor_tensor(
+                diff[k][:, HALF * g : HALF * (g + 1)],
+                h[first + g][:].indirect(pos2_sb[:, 16 * hf : 16 * (hf + 1)]),
+                answer[k][:, HALF * g : HALF * (g + 1)],
+                ALU.subtract,
+            )
+
+        def pieces(k):
+            return [LOW, HIGH] if k == len(UNITS) - 1 else [slice(0, BANK)]
+
+        LOW, HIGH = slice(0, HALF), slice(HALF, BANK)
 
         def gated(k):
             step[k] = ring.tile([P, BANK], F32, name="step", bufs=2)
-            parts = 2 if k == len(UNITS) - 1 and True else 1
-            for g in range(parts):
-                piece = slice(BANK // parts * g, BANK // parts * (g + 1))
+            for piece in pieces(k):
                 nc.vector.scalar_tensor_tensor(
                     step[k][:, piece], half_gate[k][:, piece], 1.0, diff[k][:, piece], ALU.add, ALU.mult
                 )
 
         def finish(k):
             res = ring.tile([P, BANK], F32, name="res")
-            i, cols = UNITS[k][0]
-            n = len(UNITS[k])
-            rows = out[P * i : P * (i + n), cols].rearrange("(g p) m -> p g m", p=P)
-            if k == len(UNITS) - 1:
-                for g in range(2):
-                    part = slice(HALF * g, HALF * (g + 1))
-                    nc.vector.scalar_tensor_tensor(
-                        res[:, part], step[k][:, part], 0.5, answer[k][:, part], ALU.mult, ALU.add
-                    )
-                    nc.sync.dma_start(out=rows[:, g, :] if n == 2 else rows[:, 0, part], in_=res[:, part])
-            else:
-                nc.vector.scalar_tensor_tensor(res[:], step[k][:], 0.5, answer[k][:], ALU.mult, ALU.add)
-                nc.sync.dma_start(out=rows, in_=res[:].rearrange("p (g m) -> p g m", g=n))
+            first, hf = UNITS[k]
+            rows = out[P * first : P * (first + 2), HALF * hf : HALF * (hf + 1)].rearrange("(g p) m -> p g m", p=P)
+            for piece in pieces(k):
+                nc.vector.scalar_tensor_tensor(res[:, piece], step[k][:, piece], 0.5, answer[k][:, piece], ALU.mult, ALU.add)
+                nc.sync.dma_start(
+                    out=rows[:, piece.start // HALF : piece.stop // HALF, :],
+                    in_=res[:, piece].rearrange("p (g m) -> p g m", m=HALF),
+                )
 
+        answer_bank = [5, 0, 1, 3, 7, 0, 1, 3]
+        gate_bank = [2, 4, 5, 6, 2, 4, 5, 6]
+        propose(0, answer_bank[0])
+        second_out(0, 7)
+        second_out(1, 6)
         for k in range(len(UNITS) + 1):
+            if k == 0:
+                second_back(0, 7)
+            if k == 1:
+                second_out(2, 6)
+            if k == 2:
+                second_out(3, 7)
+            if k + 1 < len(UNITS) and k != 3:
+                propose(k + 1, answer_bank[k + 1])
+            if k == 2:
+                second_back(1, 6)
             if k < len(UNITS):
-                squash(k)
+                weigh(k, gate_bank[k])
                 follower(k, 0)
             if k >= 1:
                 gated(k - 1)
             if k < len(UNITS):
                 follower(k, 1)
+            if k == 3:
+                x_code[1] = keep.tile([P, PASSES_2, HALF], U32, name="x_code1", tag="first_answer", align_bytes=64)
+                quantize_x(1, slice(0, 2))
+                propose(4, answer_bank[4])
             if k >= 1:
                 finish(k - 1)
-            if k + 1 in [1, 2]:
-                products(k + 1)
-            for g, at in zip(GROUPS[1], [0, 0, 1, 1]):
-                if at == k:
-                    activate(g, 1)
-                    turn_out(g, 1)
-                    turned.extend(g)
-                    if all(i in turned for i in range(g[0] // 4 * 4, g[0] // 4 * 4 + 4)):
-                        turn_back(g[0] // 4, 1)
-            if k in []:
-                c = 2 + [].index(k)
-                if c not in [0, 1, 2, 3]:
-                    cast_wg(c)
-                if c == 3:
-                    quant_wg(1)

@@ -115,7 +115,6 @@ def tile_list_fugue_imitation_gate_kernel(
         load_tab(2)
         move_scale_rows(2)
         load_w1("w1_next", range(2, 3), range(0, EARLY))
-        load_w1("w1_last", range(0, 3), range(EARLY, ROW_TILES))
         nc.sync.dma_start(pos1_sb[:], pos1)
 
         def column_pieces(a, u):
@@ -137,23 +136,32 @@ def tile_list_fugue_imitation_gate_kernel(
             rows = wg[512 * b : 512 * (b + 1), :].rearrange("(p j) n -> p j n", j=4)
             raw = keep.tile([P, 4, BANK], F32, name=f"wg_raw{u}{b}", tag=tag, align_bytes=64)
             nc.sync.dma_start(out=raw[:], in_=rows[:, :, BANK * u : BANK * (u + 1)])
-            for s in range(2):
-                cols = slice(HALF * s, HALF * (s + 1))
-                nc.gpsimd.tensor_scalar(
-                    wg_pair[u][:, b, cols, :], raw[:, :, cols].rearrange("p j n -> p n j"), 1.0, 0.0, ALU.mult, ALU.add
-                )
+            nc.gpsimd.tensor_scalar(
+                wg_pair[u][:, b, :, :], raw[:].rearrange("p j n -> p n j"), 1.0, 0.0, ALU.mult, ALU.add
+            )
 
         gain_word = keep.tile([P, PASSES_2, 4], F32, name="gain_word")
         load_and_cast_wg(0, 0, "big0")
+        load_w1("w1_last", range(0, 3), range(EARLY, ROW_TILES))
         load_and_cast_wg(0, 1, "big1")
         nc.gpsimd.dma_start(out=gain_word[:], in_=gain.rearrange("(b p t) -> p b t", b=PASSES_2, t=4))
-        wt_code = keep.tile([P, PASSES_2, H], U32, name="wt_code", align_bytes=64)
-        nc.sync.dma_start(out=wt_code[:].bitcast(I32), in_=wt_words.rearrange("a p c i -> p a (c i)").bitcast(I32))
+        load_and_cast_wg(1, 0, "big2")
+        wt_code = {}
+
+        def load_wt(tiles):
+            tile = keep.tile([P, PASSES_2, P * len(tiles)], U32, name=f"wt_code{tiles.start}", align_bytes=64)
+            words = wt_words.rearrange("a p c i -> p a (c i)").bitcast(I32)
+            nc.sync.dma_start(out=tile[:].bitcast(I32), in_=words[:, :, P * tiles.start : P * tiles.stop])
+            for b in range(PASSES_2):
+                for i in tiles:
+                    wt_code[b, i] = tile[:, b, P * (i - tiles.start) : P * (i - tiles.start + 1)]
+
+        load_wt(range(0, 4))
         wt_scale = keep.tile([P, PASSES_2, H], U8, name="wt_scale", align_bytes=64)
         load_scale_rows(wt_scale, wt_scales)
-        nc.sync.dma_start(pos2_sb[:], pos2)
-        load_and_cast_wg(1, 0, "big2")
         load_and_cast_wg(1, 1, "big0")
+        load_wt(range(4, ROW_TILES))
+        nc.sync.dma_start(pos2_sb[:], pos2)
 
         acc = {}
         h = [keep.tile([P, S], F32, name=f"h{i}") for i in range(ROW_TILES)]
@@ -189,8 +197,10 @@ def tile_list_fugue_imitation_gate_kernel(
                 for mb in range(2):
                     nc.tensor.transpose(ps[:, mb, P * k : P * (k + 1)], lead[i, 0][:, P * mb : P * (mb + 1)], ident[:])
             nc.scalar.activation(
-                act_turned[tiles[0] // 4][:, :, :, 32 * (tiles[0] % 4) : 32 * (tiles[-1] % 4 + 1)],
-                ps[:].rearrange("m mb (p t) -> m mb t p", t=4),
+                act_turned[tiles[0] // 4][:, :, :, 32 * (tiles[0] % 4) : 32 * (tiles[-1] % 4 + 1)].rearrange(
+                    "m mb t p -> m mb p t"
+                ),
+                ps[:].rearrange("m mb (p t) -> m mb p t", t=4),
                 ACT.Gelu_apprx_tanh,
             )
 
@@ -291,7 +301,7 @@ def tile_list_fugue_imitation_gate_kernel(
                     nc.scalar.activation(act[:, k, :], lead[2 * j + k, 1], ACT.Gelu_apprx_tanh)
             if j % 2 == 0:
                 x_turned[b] = keep.tile([P, 2, BANK], BF16, name=f"x_turned{b}", align_bytes=64)
-            rows = keep.tile([P, 2, HALF], BF16, name=f"x_rows{j}")
+            rows = ring.tile([P, 2, HALF], BF16, name="x_rows", bufs=2)
             ps = bank(n, f"out1{j}", [P, 2, 2 * P], BF16)
             for k in range(2):
                 nc.scalar.activation(rows[:, k, :], act[:, k, :], ACT.Copy, scale=gain_col[:, 2 * j + k : 2 * j + k + 1])
@@ -334,7 +344,7 @@ def tile_list_fugue_imitation_gate_kernel(
         def propose(k, n):
             ps = product(
                 k, "answer_sum", n,
-                lambda b, i: wt_code[:, b, P * i : P * (i + 1)],
+                lambda b, i: wt_code[b, i],
                 lambda b, i: wt_scale[:, b, P * i : P * (i + 1)],
             )
             if k == 0:

@@ -250,7 +250,22 @@ def tile_list_fugue_imitation_gate_kernel(
                 in_=x_grouped[hf][:, passes, :].rearrange("p b m -> p (b m)"),
             )
 
+        def warm_up(n):
+            idle = bank(n, f"idle{n}", [P, BANK])
+            for a in range(2):
+                nc.tensor.matmul_mx(
+                    out=idle[:],
+                    lhsT=w1_code[a, 0].bitcast(FP4X4),
+                    lhsT_scale=w1_scale[:, a, 0:P],
+                    rhs=v_code[a, 0][:].bitcast(FP8X4),
+                    rhs_scale=v_scale[a][:, 0:BANK],
+                    start=True,
+                    stop=True,
+                )
+
         for tiles, n in (((0, 1), 4), ((2, 3), 5), ((4, 5), 6), ((6,), 3), ((7,), 7)):
+            if tiles == (7,):
+                warm_up(2)
             first_out(tiles, n)
         for b in range(PASSES_2):
             act = act_turned[b]
@@ -264,6 +279,7 @@ def tile_list_fugue_imitation_gate_kernel(
                     gain_word[:, b, :].unsqueeze(1).to_broadcast([P, P, 4]),
                     ALU.mult,
                 )
+            warm_up(6 + b)
             quantize_x(0, slice(b, b + 1))
 
         last_second = [

@@ -44,7 +44,7 @@ def tile_list_fugue_imitation_gate_kernel(
         pos1_sb = keep.tile([P, M // 16], U16, name="pos1_sb")
         pos2_sb = keep.tile([P, M // 16], U16, name="pos2_sb")
         tab_scale = keep.tile([P, T], U8, name="tab_scale", align_bytes=64)
-        w1_scale = keep.tile([P, PASSES_1, H], U8, name="w1_scale", align_bytes=64)
+        w1_scale = [keep.tile([P, PASSES_1, BANK], U8, name=f"w1_scale{g}", align_bytes=64) for g in range(2)]
         v_scale = [keep.tile([P, S], U8, name=f"v_scale{a}", align_bytes=64) for a in range(PASSES_1)]
         zero_col = keep.tile([P, 1], F32, name="zero_col")
         zero_bias = keep.tile([P, 1], F32, name="zero_bias")
@@ -86,18 +86,16 @@ def tile_list_fugue_imitation_gate_kernel(
                     w1_code[a, i] = tile[:, a - passes.start, 256 * (i - tiles.start) : 256 * (i - tiles.start + 1)]
 
         def load_scale_rows(plane, rows):
-            for q in range(4):
+            for r in range(4):
                 nc.sync.dma_start(
-                    out=plane[32 * q : 32 * q + 4, :, :].bitcast(I32),
-                    in_=rows.bitcast(I32)[:, 4 * q : 4 * q + 4, :].rearrange("a r c -> r a c"),
+                    out=plane[r:P:32, :, :].bitcast(I32),
+                    in_=rows.bitcast(I32)[:, r:16:4, :].rearrange("a q c -> q a c"),
                 )
 
         def move_scale_rows(a):
-            for q in range(4):
-                first = 32 * q + 4 if a == 1 else 112 + 4 * q
-                nc.sync.dma_start(
-                    out=v_scale[a][32 * q : 32 * q + 4, :].bitcast(I32), in_=v_scale[0][first : first + 4, :].bitcast(I32)
-                )
+            for r in range(4):
+                rows = slice(4 + r, P, 32) if a == 1 else slice(112 + r, P, 4)
+                nc.sync.dma_start(out=v_scale[a][r:P:32, :].bitcast(I32), in_=v_scale[0][rows, :].bitcast(I32))
 
         w1_code = {}
         nc.sync.dma_start(offs_sb[:], offs)
@@ -107,7 +105,7 @@ def tile_list_fugue_imitation_gate_kernel(
                 out=tab_scale[32 * q : 32 * q + 8, :].bitcast(I32), in_=tab_rows[0:2, 4 * q : 4 * q + 4, :]
             )
         load_tab(0)
-        load_scale_rows(w1_scale, w1_scales)
+        load_scale_rows(w1_scale[0], w1_scales[:, :, 0:BANK])
         load_w1("w1_first", range(0, 2), range(0, EARLY))
         load_tab(1)
         nc.vector.tensor_copy(v_scale[0][:], tab_scale[:].indirect(offs_sb[:]))
@@ -143,6 +141,7 @@ def tile_list_fugue_imitation_gate_kernel(
         gain_word = keep.tile([P, PASSES_2, 4], F32, name="gain_word")
         load_and_cast_wg(0, 0, "big0")
         load_w1("w1_last", range(0, 3), range(EARLY, ROW_TILES))
+        load_scale_rows(w1_scale[1], w1_scales[:, :, BANK:H])
         load_and_cast_wg(0, 1, "big1")
         nc.gpsimd.dma_start(out=gain_word[:], in_=gain.rearrange("(b p t) -> p b t", b=PASSES_2, t=4))
         load_and_cast_wg(1, 0, "big2")
@@ -173,7 +172,7 @@ def tile_list_fugue_imitation_gate_kernel(
             nc.tensor.matmul_mx(
                 out=acc[i, u][:, cols],
                 lhsT=w1_code[a, i].bitcast(FP4X4),
-                lhsT_scale=w1_scale[:, a, P * i : P * (i + 1)],
+                lhsT_scale=w1_scale[i // EARLY][:, a, P * (i % EARLY) : P * (i % EARLY + 1)],
                 rhs=v_code[a, u][:, cols].bitcast(FP8X4),
                 rhs_scale=v_scale[a][:, BANK * u + cols.start : BANK * u + cols.stop],
                 start=(a == 0 and cols.start == 0),
@@ -256,7 +255,7 @@ def tile_list_fugue_imitation_gate_kernel(
                 nc.tensor.matmul_mx(
                     out=idle[:],
                     lhsT=w1_code[a, 0].bitcast(FP4X4),
-                    lhsT_scale=w1_scale[:, a, 0:P],
+                    lhsT_scale=w1_scale[0][:, a, 0:P],
                     rhs=v_code[a, 0][:].bitcast(FP8X4),
                     rhs_scale=v_scale[a][:, 0:BANK],
                     start=True,

@@ -62,7 +62,7 @@ def tile_list_fugue_imitation_gate_kernel(
         make_identity(nc, ident_bf16[:])
         ps = bank(7, "gain_turned", [P, P])
         nc.tensor.transpose(ps[:], gain_rows[:], ident[:])
-        nc.scalar.copy(gain_col[:], ps[:, 0:ROW_TILES])
+        nc.scalar.activation(gain_col[:], ps[:, 0:ROW_TILES], ACT.Identity, bias=zero_bias[:])
 
         w1_i32 = w1_words.bitcast(I32)
         tab_rows = tab_scales.bitcast(I32)
@@ -273,9 +273,9 @@ def tile_list_fugue_imitation_gate_kernel(
                 for t in range(4):
                     nc.tensor.transpose(ps[:, t, :], act[:, mb, t, :], ident[:])
                 nc.vector.tensor_tensor(
-                    x_grouped[0][:, b, BANK * mb : BANK * (mb + 1)].rearrange("p (m t) -> p m t", t=4),
-                    ps[:].rearrange("p t m -> p m t"),
-                    gain_word[:, b, :].unsqueeze(1).to_broadcast([P, P, 4]),
+                    x_grouped[0][:, b, BANK * mb : BANK * (mb + 1)].rearrange("p (m e t) -> p m t e", e=2, t=4),
+                    ps[:].rearrange("p t (m e) -> p m t e", e=2),
+                    gain_word[:, b, :].unsqueeze(1).unsqueeze(3).to_broadcast([P, P // 2, 4, 2]),
                     ALU.mult,
                 )
             warm_up(6 + b)
@@ -332,7 +332,8 @@ def tile_list_fugue_imitation_gate_kernel(
                 for u in range(2):
                     nc.tensor.transpose(ps[:, u, P * mb : P * (mb + 1)], words[:, 256 * mb + u : 256 * (mb + 1) : 2], ident[:])
             nc.scalar.copy(
-                x_grouped[1][:, b, :].bitcast(F32).rearrange("p (m u) -> p m u", u=2), ps[:].rearrange("p u m -> p m u")
+                x_grouped[1][:, b, :].bitcast(F32).rearrange("p (m e u) -> p m u e", e=2, u=2),
+                ps[:].rearrange("p u (m e) -> p m u e", e=2),
             )
 
         answer = {}
@@ -366,7 +367,7 @@ def tile_list_fugue_imitation_gate_kernel(
                 answer[k] = keep.tile([P, BANK], F32, name="first_answer", tag="first_answer", align_bytes=64)
             else:
                 answer[k] = ring.tile([P, BANK], F32, name="answer", bufs=4)
-            nc.scalar.activation(answer[k][:], ps[:], ACT.Tanh, bias=zero_bias[:])
+            nc.scalar.activation(answer[k][:], ps[:], ACT.Tanh)
 
         def weigh(k, n):
             ps = product(
@@ -375,7 +376,7 @@ def tile_list_fugue_imitation_gate_kernel(
                 lambda b, i: wg_scale[i // 4][:, b, P * (i % 4) : P * (i % 4 + 1)],
             )
             half_gate[k] = ring.tile([P, BANK], F32, name="half_gate", bufs=4)
-            nc.scalar.activation(half_gate[k][:], ps[:], ACT.Tanh, bias=zero_bias[:], scale=-0.5)
+            nc.scalar.activation(half_gate[k][:], ps[:], ACT.Tanh, scale=-0.5)
 
         def follower(k, g):
             first, hf = UNITS[k]

@@ -155,11 +155,11 @@ def tile_list_fugue_imitation_gate_kernel(
                 for i in tiles:
                     wt_code[b, i] = tile[:, b, P * (i - tiles.start) : P * (i - tiles.start + 1)]
 
-        load_wt(range(0, 4))
+        load_wt(range(0, 2))
         wt_scale = keep.tile([P, PASSES_2, H], U8, name="wt_scale", align_bytes=64)
         load_scale_rows(wt_scale, wt_scales)
         load_and_cast_wg(1, 1, "big0")
-        load_wt(range(4, ROW_TILES))
+        load_wt(range(2, ROW_TILES))
         nc.sync.dma_start(pos2_sb[:], pos2)
 
         acc = {}
@@ -242,11 +242,11 @@ def tile_list_fugue_imitation_gate_kernel(
         x_code = {0: keep.tile([P, PASSES_2, HALF], U32, name="x_code0", align_bytes=64)}
         x_scale = [keep.tile([P, PASSES_2, HALF], U8, name=f"x_scale{hf}", align_bytes=64) for hf in range(2)]
 
-        def quantize_x(hf, passes):
+        def quantize_x(hf):
             nc.vector.quantize_mx(
-                out=x_code[hf][:, passes, :].rearrange("p b m -> p (b m)").bitcast(FP8X4),
-                scales=x_scale[hf][:, passes, :].rearrange("p b m -> p (b m)"),
-                in_=x_grouped[hf][:, passes, :].rearrange("p b m -> p (b m)"),
+                out=x_code[hf][:].rearrange("p b m -> p (b m)").bitcast(FP8X4),
+                scales=x_scale[hf][:].rearrange("p b m -> p (b m)"),
+                in_=x_grouped[hf][:].rearrange("p b m -> p (b m)"),
             )
 
         def warm_up(n):
@@ -279,7 +279,7 @@ def tile_list_fugue_imitation_gate_kernel(
                     ALU.mult,
                 )
             warm_up(6 + b)
-            quantize_x(0, slice(b, b + 1))
+        quantize_x(0)
 
         last_second = [
             laid.tile([P, HALF], F32, name="lead6_second", offset=2560, align_bytes=64),
@@ -437,7 +437,7 @@ def tile_list_fugue_imitation_gate_kernel(
                 follower(k, 1)
             if k == 3:
                 x_code[1] = keep.tile([P, PASSES_2, HALF], U32, name="x_code1", tag="first_answer", align_bytes=64)
-                quantize_x(1, slice(0, 2))
+                quantize_x(1)
                 propose(4, answer_bank[4])
             if k >= 1:
                 finish(k - 1)

@@ -52,17 +52,9 @@ def tile_list_fugue_imitation_gate_kernel(
         ident_bf16 = keep.tile([P, P], BF16, name="ident_bf16")
 
         nc.gpsimd.memset(tab_scale[0:112, :].bitcast(I32), 0)
-        nc.vector.memset(zero_col[:], 0.0)
-        nc.scalar.activation(zero_bias[:], zero_col[:], ACT.Gelu_apprx_tanh)
         gain_rows = keep.tile([P, P], F32, name="gain_rows")
         gain_col = keep.tile([P, ROW_TILES], F32, name="gain_col")
         nc.vector.memset(gain_rows[:], 0.0)
-        nc.scalar.dma_start(out=gain_rows[0:ROW_TILES, :], in_=gain.rearrange("(i p) -> i p", p=P))
-        make_identity(nc, ident[:])
-        make_identity(nc, ident_bf16[:])
-        ps = bank(7, "gain_turned", [P, P])
-        nc.tensor.transpose(ps[:], gain_rows[:], ident[:])
-        nc.scalar.activation(gain_col[:], ps[:, 0:ROW_TILES], ACT.Identity, bias=zero_bias[:])
 
         w1_i32 = w1_words.bitcast(I32)
         tab_rows = tab_scales.bitcast(I32)
@@ -101,9 +93,17 @@ def tile_list_fugue_imitation_gate_kernel(
         nc.sync.dma_start(offs_sb[:], offs)
         nc.sync.dma_start(out=tab_scale[112:128, :].bitcast(I32), in_=tab_rows[2])
         for q in range(4):
-            nc.sync.dma_start(
+            (nc.sync, nc.scalar)[q // 2].dma_start(
                 out=tab_scale[32 * q : 32 * q + 8, :].bitcast(I32), in_=tab_rows[0:2, 4 * q : 4 * q + 4, :]
             )
+        nc.scalar.dma_start(out=gain_rows[0:ROW_TILES, :], in_=gain.rearrange("(i p) -> i p", p=P))
+        make_identity(nc, ident[:])
+        make_identity(nc, ident_bf16[:])
+        nc.gpsimd.memset(zero_col[:], 0.0)
+        nc.scalar.activation(zero_bias[:], zero_col[:], ACT.Gelu_apprx_tanh)
+        ps = bank(7, "gain_turned", [P, P])
+        nc.tensor.transpose(ps[:], gain_rows[:], ident[:])
+        nc.scalar.activation(gain_col[:], ps[:, 0:ROW_TILES], ACT.Identity, bias=zero_bias[:])
         load_tab(0)
         load_scale_rows(w1_scale[0], w1_scales[:, :, 0:BANK])
         load_w1("w1_first", range(0, 2), range(0, EARLY))
@@ -145,6 +145,7 @@ def tile_list_fugue_imitation_gate_kernel(
         load_and_cast_wg(0, 1, "big1")
         nc.gpsimd.dma_start(out=gain_word[:], in_=gain.rearrange("(b p t) -> p b t", b=PASSES_2, t=4))
         load_and_cast_wg(1, 0, "big2")
+        load_and_cast_wg(1, 1, "big0")
         wt_code = {}
 
         def load_wt(tiles):
@@ -158,7 +159,6 @@ def tile_list_fugue_imitation_gate_kernel(
         load_wt(range(0, 2))
         wt_scale = keep.tile([P, PASSES_2, H], U8, name="wt_scale", align_bytes=64)
         load_scale_rows(wt_scale, wt_scales)
-        load_and_cast_wg(1, 1, "big0")
         load_wt(range(2, ROW_TILES))
         nc.sync.dma_start(pos2_sb[:], pos2)
 
@@ -234,6 +234,9 @@ def tile_list_fugue_imitation_gate_kernel(
             else:
                 leader(last_first[i - 6][:], i, [0])
                 lead[i, 0] = last_first[i - 6][:]
+            if i == 6:
+                first_out((0, 1), 0)
+                first_out((2, 3), 1)
 
         x_grouped = [
             laid.tile([P, PASSES_2, 4 * HALF], BF16, name="x_grouped0", offset=26624, align_bytes=64),
@@ -262,14 +265,12 @@ def tile_list_fugue_imitation_gate_kernel(
                     stop=True,
                 )
 
-        for tiles, n in (((0, 1), 4), ((2, 3), 5), ((4, 5), 6), ((6,), 3), ((7,), 7)):
-            if tiles == (7,):
-                warm_up(2)
+        for tiles, n in (((4, 5), 2), ((6,), 3), ((7,), 7)):
             first_out(tiles, n)
         for b in range(PASSES_2):
             act = act_turned[b]
             for mb in range(2):
-                ps = bank([[0, 1], [2, 4]][b][mb], f"back0{b}{mb}", [P, 4, P])
+                ps = bank([[4, 5], [0, 1]][b][mb], f"back0{b}{mb}", [P, 4, P])
                 for t in range(4):
                     nc.tensor.transpose(ps[:, t, :], act[:, mb, t, :], ident[:])
                 nc.vector.tensor_tensor(
@@ -282,7 +283,7 @@ def tile_list_fugue_imitation_gate_kernel(
         quantize_x(0)
 
         last_second = [
-            laid.tile([P, HALF], F32, name="lead6_second", offset=2560, align_bytes=64),
+            keep.tile([P, HALF], F32, name="lead6_second"),
             keep.tile([P, HALF], F32, name="lead7_second"),
         ]
         for i in (7, 6):
@@ -402,7 +403,7 @@ def tile_list_fugue_imitation_gate_kernel(
                 )
 
         def finish(k):
-            res = ring.tile([P, BANK], F32, name="res")
+            res = ring.tile([P, BANK], F32, name="res", bufs=len(UNITS))
             first, hf = UNITS[k]
             rows = out[P * first : P * (first + 2), HALF * hf : HALF * (hf + 1)].rearrange("(g p) m -> p g m", p=P)
             for piece in pieces(k):
@@ -412,8 +413,8 @@ def tile_list_fugue_imitation_gate_kernel(
                     in_=res[:, piece].rearrange("p (g m) -> p g m", m=HALF),
                 )
 
-        answer_bank = [5, 0, 1, 3, 7, 0, 1, 3]
-        gate_bank = [2, 4, 5, 6, 2, 4, 5, 6]
+        answer_bank = [2, 0, 1, 3, 7, 0, 1, 3]
+        gate_bank = [4, 5, 2, 6, 4, 5, 2, 6]
         propose(0, answer_bank[0])
         second_out(0, 7)
         second_out(1, 6)
@@ -431,7 +432,7 @@ def tile_list_fugue_imitation_gate_kernel(
             if k < len(UNITS):
                 weigh(k, gate_bank[k])
                 follower(k, 0)
-            if k >= 1:
+            if k >= 1 and k not in (3, 4):
                 gated(k - 1)
             if k < len(UNITS):
                 follower(k, 1)
@@ -439,5 +440,8 @@ def tile_list_fugue_imitation_gate_kernel(
                 x_code[1] = keep.tile([P, PASSES_2, HALF], U32, name="x_code1", tag="first_answer", align_bytes=64)
                 quantize_x(1)
                 propose(4, answer_bank[4])
-            if k >= 1:
+                for last_step in (gated, finish):
+                    last_step(2)
+                    last_step(3)
+            if k >= 1 and k not in (3, 4):
                 finish(k - 1)

@@ -54,7 +54,15 @@ def tile_list_fugue_imitation_gate_kernel(
         nc.gpsimd.memset(tab_scale[0:112, :].bitcast(I32), 0)
         gain_rows = keep.tile([P, P], F32, name="gain_rows")
         gain_col = keep.tile([P, ROW_TILES], F32, name="gain_col")
+        nc.vector.memset(zero_col[:], 0.0)
+        nc.scalar.activation(zero_bias[:], zero_col[:], ACT.Gelu_apprx_tanh)
         nc.vector.memset(gain_rows[:], 0.0)
+        nc.scalar.dma_start(out=gain_rows[24:32, :], in_=gain.rearrange("(i p) -> i p", p=P))
+        make_identity(nc, ident[:])
+        make_identity(nc, ident_bf16[:])
+        ps = bank(7, "gain_turned", [P, P])
+        nc.tensor.transpose(ps[:], gain_rows[:], ident[:])
+        nc.scalar.activation(gain_col[:], ps[:, 24:32], ACT.Identity, bias=zero_bias[:])
 
         w1_i32 = w1_words.bitcast(I32)
         tab_rows = tab_scales.bitcast(I32)
@@ -92,18 +100,10 @@ def tile_list_fugue_imitation_gate_kernel(
         w1_code = {}
         nc.sync.dma_start(offs_sb[:], offs)
         nc.sync.dma_start(out=tab_scale[112:128, :].bitcast(I32), in_=tab_rows[2])
-        for q in range(4):
-            (nc.sync, nc.scalar)[q // 2].dma_start(
+        for q in (0, 2, 1, 3):
+            nc.sync.dma_start(
                 out=tab_scale[32 * q : 32 * q + 8, :].bitcast(I32), in_=tab_rows[0:2, 4 * q : 4 * q + 4, :]
             )
-        nc.scalar.dma_start(out=gain_rows[0:ROW_TILES, :], in_=gain.rearrange("(i p) -> i p", p=P))
-        make_identity(nc, ident[:])
-        make_identity(nc, ident_bf16[:])
-        nc.gpsimd.memset(zero_col[:], 0.0)
-        nc.scalar.activation(zero_bias[:], zero_col[:], ACT.Gelu_apprx_tanh)
-        ps = bank(7, "gain_turned", [P, P])
-        nc.tensor.transpose(ps[:], gain_rows[:], ident[:])
-        nc.scalar.activation(gain_col[:], ps[:, 0:ROW_TILES], ACT.Identity, bias=zero_bias[:])
         load_tab(0)
         load_scale_rows(w1_scale[0], w1_scales[:, :, 0:BANK])
         load_w1("w1_first", range(0, 2), range(0, EARLY))

@@ -364,10 +364,7 @@ def tile_list_fugue_imitation_gate_kernel(
                 lambda b, i: wt_code[b, i],
                 lambda b, i: wt_scale[:, b, P * i : P * (i + 1)],
             )
-            if k == 0:
-                answer[k] = keep.tile([P, BANK], F32, name="first_answer", tag="first_answer", align_bytes=64)
-            else:
-                answer[k] = ring.tile([P, BANK], F32, name="answer", bufs=4)
+            answer[k] = ring.tile([P, BANK], F32, name="answer", bufs=8)
             nc.scalar.activation(answer[k][:], ps[:], ACT.Tanh)
 
         def weigh(k, n):
@@ -376,7 +373,10 @@ def tile_list_fugue_imitation_gate_kernel(
                 lambda b, i: wg_code[i // 4][:, b, P * (i % 4) : P * (i % 4 + 1)],
                 lambda b, i: wg_scale[i // 4][:, b, P * (i % 4) : P * (i % 4 + 1)],
             )
-            half_gate[k] = ring.tile([P, BANK], F32, name="half_gate", bufs=4)
+            if k == 0:
+                half_gate[k] = keep.tile([P, BANK], F32, name="first_gate", tag="first_gate", align_bytes=64)
+            else:
+                half_gate[k] = ring.tile([P, BANK], F32, name="half_gate", bufs=4)
             nc.scalar.activation(half_gate[k][:], ps[:], ACT.Tanh, scale=-0.5)
 
         def follower(k, g):
@@ -396,7 +396,7 @@ def tile_list_fugue_imitation_gate_kernel(
         LOW, HIGH = slice(0, HALF), slice(HALF, BANK)
 
         def gated(k):
-            step[k] = ring.tile([P, BANK], F32, name="step", bufs=2)
+            step[k] = ring.tile([P, BANK], F32, name="step", bufs=3)
             for piece in pieces(k):
                 nc.vector.scalar_tensor_tensor(
                     step[k][:, piece], half_gate[k][:, piece], 1.0, diff[k][:, piece], ALU.add, ALU.mult
@@ -406,6 +406,22 @@ def tile_list_fugue_imitation_gate_kernel(
             res = ring.tile([P, BANK], F32, name="res", bufs=len(UNITS))
             first, hf = UNITS[k]
             rows = out[P * first : P * (first + 2), HALF * hf : HALF * (hf + 1)].rearrange("(g p) m -> p g m", p=P)
+            if k in sum_banks:
+                blocks = [slice(P * j, P * (j + 1)) for j in range(4)]
+                ps = bank(sum_banks[k][0], f"twice_out{k}", [P, BANK])
+                for block in blocks:
+                    for n, term in enumerate((step[k], answer[k], answer[k])):
+                        nc.tensor.matmul(
+                            ps[:, block], lhsT=term[:, block], rhs=ident[:], start=(n == 0), stop=(n == 2), is_transpose=True
+                        )
+                twice = ring.tile([P, BANK], F32, name="twice", bufs=2)
+                nc.scalar.copy(twice[:], ps[:])
+                ps = bank(sum_banks[k][1], f"twice_back{k}", [P, BANK])
+                for block in blocks:
+                    nc.tensor.transpose(ps[:, block], twice[:, block], ident[:])
+                nc.scalar.activation(res[:], ps[:], ACT.Copy, scale=0.5)
+                nc.sync.dma_start(out=rows, in_=res[:].rearrange("p (g m) -> p g m", m=HALF))
+                return
             for piece in pieces(k):
                 nc.vector.scalar_tensor_tensor(res[:, piece], step[k][:, piece], 0.5, answer[k][:, piece], ALU.mult, ALU.add)
                 nc.sync.dma_start(
@@ -415,6 +431,7 @@ def tile_list_fugue_imitation_gate_kernel(
 
         answer_bank = [2, 0, 1, 3, 7, 0, 1, 3]
         gate_bank = [4, 5, 2, 6, 4, 5, 2, 6]
+        sum_banks = {0: (5, 1), 4: (7, 4)}
         propose(0, answer_bank[0])
         second_out(0, 7)
         second_out(1, 6)
@@ -437,11 +454,15 @@ def tile_list_fugue_imitation_gate_kernel(
             if k < len(UNITS):
                 follower(k, 1)
             if k == 3:
-                x_code[1] = keep.tile([P, PASSES_2, HALF], U32, name="x_code1", tag="first_answer", align_bytes=64)
+                x_code[1] = keep.tile([P, PASSES_2, HALF], U32, name="x_code1", tag="first_gate", align_bytes=64)
                 quantize_x(1)
                 propose(4, answer_bank[4])
                 for last_step in (gated, finish):
                     last_step(2)
                     last_step(3)
-            if k >= 1 and k not in (3, 4):
+            if k == len(UNITS) - 1:
+                finish(4)
+            if k == 2:
+                finish(0)
+            if k >= 2 and k not in (3, 4, 5):
                 finish(k - 1)

@@ -252,19 +252,6 @@ def tile_list_fugue_imitation_gate_kernel(
                 in_=x_grouped[hf][:].rearrange("p b m -> p (b m)"),
             )
 
-        def warm_up(n):
-            idle = bank(n, f"idle{n}", [P, BANK])
-            for a in range(2):
-                nc.tensor.matmul_mx(
-                    out=idle[:],
-                    lhsT=w1_code[a, 0].bitcast(FP4X4),
-                    lhsT_scale=w1_scale[0][:, a, 0:P],
-                    rhs=v_code[a, 0][:].bitcast(FP8X4),
-                    rhs_scale=v_scale[a][:, 0:BANK],
-                    start=True,
-                    stop=True,
-                )
-
         for tiles, n in (((4, 5), 2), ((6,), 3), ((7,), 7)):
             first_out(tiles, n)
         for b in range(PASSES_2):
@@ -279,7 +266,6 @@ def tile_list_fugue_imitation_gate_kernel(
                     gain_word[:, b, :].unsqueeze(1).unsqueeze(3).to_broadcast([P, P // 2, 4, 2]),
                     ALU.mult,
                 )
-            warm_up(6 + b)
         quantize_x(0)
 
         last_second = [

@@ -24,7 +24,8 @@ ACT = mybir.ActivationFunctionType
 ALU = mybir.AluOpType
 
 EARLY = 4
-UNITS = [(2 * j, hf) for hf in range(2) for j in range(4)]
+TURNED = [(0, 0), (0, 2), (0, 4), (0, 6)]
+PLAIN = [(1, 0), (1, 2), (1, 4), (1, 6)]
 
 
 def tile_list_fugue_imitation_gate_kernel(
@@ -148,18 +149,15 @@ def tile_list_fugue_imitation_gate_kernel(
         load_and_cast_wg(1, 1, "big0")
         wt_code = {}
 
-        def load_wt(tiles):
-            tile = keep.tile([P, PASSES_2, P * len(tiles)], U32, name=f"wt_code{tiles.start}", align_bytes=64)
+        def load_wt(u):
+            wt_code[u] = keep.tile([P, PASSES_2, BANK], U32, name=f"wt_code{u}", align_bytes=64)
             words = wt_words.rearrange("a p c i -> p a (c i)").bitcast(I32)
-            nc.sync.dma_start(out=tile[:].bitcast(I32), in_=words[:, :, P * tiles.start : P * tiles.stop])
-            for b in range(PASSES_2):
-                for i in tiles:
-                    wt_code[b, i] = tile[:, b, P * (i - tiles.start) : P * (i - tiles.start + 1)]
+            nc.sync.dma_start(out=wt_code[u][:].bitcast(I32), in_=words[:, :, BANK * u : BANK * (u + 1)])
 
-        load_wt(range(0, 2))
+        load_wt(0)
         wt_scale = keep.tile([P, PASSES_2, H], U8, name="wt_scale", align_bytes=64)
         load_scale_rows(wt_scale, wt_scales)
-        load_wt(range(2, ROW_TILES))
+        load_wt(1)
         nc.sync.dma_start(pos2_sb[:], pos2)
 
         acc = {}
@@ -215,7 +213,7 @@ def tile_list_fugue_imitation_gate_kernel(
             keep_rows(i, 0)
         last_first = [
             keep.tile([P, HALF], F32, name="lead6_first"),
-            laid.tile([P, HALF], F32, name="lead7_first", offset=3072, align_bytes=64),
+            laid.tile([P, HALF], F32, name="lead7_first", offset=2048, align_bytes=64),
         ]
         for i in range(ROW_TILES):
             if i >= EARLY:
@@ -240,9 +238,9 @@ def tile_list_fugue_imitation_gate_kernel(
 
         x_grouped = [
             laid.tile([P, PASSES_2, 4 * HALF], BF16, name="x_grouped0", offset=26624, align_bytes=64),
-            keep.tile([P, PASSES_2, 4 * HALF], BF16, name="x_grouped1", align_bytes=64),
+            laid.tile([P, PASSES_2, 4 * HALF], BF16, name="x_grouped1", offset=44544, align_bytes=64),
         ]
-        x_code = {0: keep.tile([P, PASSES_2, HALF], U32, name="x_code0", align_bytes=64)}
+        x_code = [keep.tile([P, PASSES_2, HALF], U32, name=f"x_code{hf}", align_bytes=64) for hf in range(2)]
         x_scale = [keep.tile([P, PASSES_2, HALF], U8, name=f"x_scale{hf}", align_bytes=64) for hf in range(2)]
 
         def quantize_x(hf):
@@ -295,7 +293,7 @@ def tile_list_fugue_imitation_gate_kernel(
             if j % 2 == 0:
                 act = keep.tile([P, 2, HALF], F32, name=f"act{j}", tag="v_code21", align_bytes=64)
             else:
-                act = laid.tile([P, 2, HALF], F32, name=f"act{j}", offset=3584, align_bytes=64)
+                act = laid.tile([P, 2, HALF], F32, name=f"act{j}", offset=2560, align_bytes=64)
             if j < 3:
                 nc.scalar.activation(act[:], lead[2 * j, "pair", 1], ACT.Gelu_apprx_tanh)
             else:
@@ -323,20 +321,89 @@ def tile_list_fugue_imitation_gate_kernel(
                 ps[:].rearrange("p u (m e) -> p m u e", e=2),
             )
 
+        follow = {}
+
+        def plain_followers(tiles, hf, offset):
+            tile = laid.tile([P, len(tiles), HALF], F32, name=f"follow{tiles[0]}{hf}", offset=offset, align_bytes=64)
+            for g, i in enumerate(tiles):
+                nc.vector.tensor_copy(tile[:, g, :], h[i][:].indirect(pos2_sb[:, 16 * hf : 16 * (hf + 1)]))
+                follow[i] = tile[:, g, :]
+
+        turned = {}
+
+        def turned_product(k, name, n, code, scale, factor):
+            hf, first = TURNED[k]
+            cols = slice(P * (first % 4), P * (first % 4 + 2))
+            ps = bank(n, f"{name}{k}_sum", [P, BANK])
+            for b in range(PASSES_2):
+                for mb in range(2):
+                    nc.tensor.matmul_mx(
+                        out=ps[:, HALF * mb : HALF * (mb + 1)],
+                        lhsT=x_code[hf][:, b, P * mb : P * (mb + 1)].bitcast(FP8X4),
+                        lhsT_scale=x_scale[hf][:, b, P * mb : P * (mb + 1)],
+                        rhs=code(first // 4, b)[:, cols].bitcast(FP8X4),
+                        rhs_scale=scale(first // 4, b)[:, cols],
+                        start=(b == 0 and mb == 0),
+                        stop=(b == PASSES_2 - 1 and mb == 1),
+                    )
+            turned[name, k] = keep.tile([P, 2, 2, P], F32, name=f"{name}{k}")
+            nc.scalar.activation(turned[name, k][:].rearrange("m mb g p -> m (mb g p)"), ps[:], ACT.Tanh, scale=factor)
+
+        both_at = {0: 22528}
+
+        def turned_terms(k, n):
+            hf, first = TURNED[k]
+            if k in both_at:
+                both = laid.tile([P, 2, 2, P], F32, name=f"both{k}", offset=both_at[k], align_bytes=64)
+            else:
+                both = keep.tile([P, 2, 2, P], F32, name=f"both{k}")
+            nc.gpsimd.tensor_tensor(both[:], turned["gate", k][:], turned["minus_answer", k][:], ALU.mult)
+            turned["both", k] = both
+            ps = bank(n, f"follow_turned{k}", [P, 2, 2, P])
+            for g in range(2):
+                for mb in range(2):
+                    nc.tensor.transpose(ps[:, mb, g, :], follow[first + g][:, P * mb : P * (mb + 1)], ident[:])
+            kept = keep.tile([P, 2, 2, P], F32, name=f"kept{k}")
+            nc.vector.scalar_tensor_tensor(
+                kept[:].rearrange("m mb g p -> m (mb g p)"),
+                turned["gate", k][:].rearrange("m mb g p -> m (mb g p)"),
+                -1.0,
+                ps[:].rearrange("m mb g p -> m (mb g p)"),
+                ALU.add,
+                ALU.mult,
+            )
+            turned["kept", k] = kept
+
+        def turned_finish(k, n):
+            hf, first = TURNED[k]
+            ps = bank(n, f"out_sum{k}", [P, 2, 2, P])
+            for g in range(2):
+                for mb in range(2):
+                    for j, name in enumerate(("minus_answer", "both", "kept")):
+                        nc.tensor.matmul(
+                            ps[:, g, mb, :], lhsT=turned[name, k][:, mb, g, :], rhs=ident[:],
+                            start=(j == 0), stop=(j == 2), is_transpose=True,
+                        )
+            res = keep.tile([P, BANK], F32, name=f"res_turned{k}")
+            nc.scalar.activation(res[:], ps[:].rearrange("p g mb m -> p (g mb m)"), ACT.Copy, scale=-0.5)
+            rows = out[P * first : P * (first + 2), HALF * hf : HALF * (hf + 1)].rearrange("(g p) m -> p g m", p=P)
+            nc.scalar.dma_start(out=rows, in_=res[:].rearrange("p (g m) -> p g m", m=HALF))
+
         answer = {}
         half_gate = {}
         diff = {}
         step = {}
 
         def product(k, name, n, code, scale):
-            first, hf = UNITS[k]
+            hf, first = PLAIN[k]
             ps = bank(n, f"{name}{k}", [P, BANK])
             for b in range(PASSES_2):
                 for g in range(2):
+                    i = first + g
                     nc.tensor.matmul_mx(
                         out=ps[:, HALF * g : HALF * (g + 1)],
-                        lhsT=code(b, first + g).bitcast(FP8X4),
-                        lhsT_scale=scale(b, first + g),
+                        lhsT=code(i // 4, b)[:, P * (i % 4) : P * (i % 4 + 1)].bitcast(FP8X4),
+                        lhsT_scale=scale(i // 4, b)[:, P * (i % 4) : P * (i % 4 + 1)],
                         rhs=x_code[hf][:, b, :].bitcast(FP8X4),
                         rhs_scale=x_scale[hf][:, b, :],
                         start=(b == 0 and g == 0),
@@ -344,31 +411,23 @@ def tile_list_fugue_imitation_gate_kernel(
                     )
             return ps
 
+        wt_operand = (lambda u, b: wt_code[u][:, b, :], lambda u, b: wt_scale[:, b, BANK * u : BANK * (u + 1)])
+        wg_operand = (lambda u, b: wg_code[u][:, b, :], lambda u, b: wg_scale[u][:, b, :])
+
         def propose(k, n):
-            ps = product(
-                k, "answer_sum", n,
-                lambda b, i: wt_code[b, i],
-                lambda b, i: wt_scale[:, b, P * i : P * (i + 1)],
-            )
-            answer[k] = ring.tile([P, BANK], F32, name="answer", bufs=8)
+            ps = product(k, "answer_sum", n, *wt_operand)
+            answer[k] = laid.tile([P, BANK], F32, name=f"answer{k}", offset=32768 + 2048 * [0, 3, 1, 2][k], align_bytes=64)
             nc.scalar.activation(answer[k][:], ps[:], ACT.Tanh)
 
         def weigh(k, n):
-            ps = product(
-                k, "gate_sum", n,
-                lambda b, i: wg_code[i // 4][:, b, P * (i % 4) : P * (i % 4 + 1)],
-                lambda b, i: wg_scale[i // 4][:, b, P * (i % 4) : P * (i % 4 + 1)],
-            )
-            if k == 0:
-                half_gate[k] = keep.tile([P, BANK], F32, name="first_gate", tag="first_gate", align_bytes=64)
-            else:
-                half_gate[k] = ring.tile([P, BANK], F32, name="half_gate", bufs=4)
+            ps = product(k, "gate_sum", n, *wg_operand)
+            half_gate[k] = keep.tile([P, BANK], F32, name=f"half_gate{k}")
             nc.scalar.activation(half_gate[k][:], ps[:], ACT.Tanh, scale=-0.5)
 
         def follower(k, g):
-            first, hf = UNITS[k]
+            hf, first = PLAIN[k]
             if g == 0:
-                diff[k] = laid.tile([P, BANK], F32, name=f"diff{k}", offset=16384 + 2048 * (k % 4), align_bytes=64)
+                diff[k] = laid.tile([P, BANK], F32, name=f"diff{k}", offset=12288 + 2048 * (k % 2), align_bytes=64)
             nc.vector.tensor_tensor(
                 diff[k][:, HALF * g : HALF * (g + 1)],
                 h[first + g][:].indirect(pos2_sb[:, 16 * hf : 16 * (hf + 1)]),
@@ -376,38 +435,22 @@ def tile_list_fugue_imitation_gate_kernel(
                 ALU.subtract,
             )
 
-        def pieces(k):
-            return [LOW, HIGH] if k == len(UNITS) - 1 else [slice(0, BANK)]
-
         LOW, HIGH = slice(0, HALF), slice(HALF, BANK)
 
+        def pieces(k):
+            return [LOW, HIGH] if k == 3 else [slice(0, BANK)]
+
         def gated(k):
-            step[k] = ring.tile([P, BANK], F32, name="step", bufs=3)
+            step[k] = laid.tile([P, BANK], F32, name=f"step{k}", offset=8192 + 2048 * (k % 2), align_bytes=64)
             for piece in pieces(k):
                 nc.vector.scalar_tensor_tensor(
                     step[k][:, piece], half_gate[k][:, piece], 1.0, diff[k][:, piece], ALU.add, ALU.mult
                 )
 
         def finish(k):
-            res = ring.tile([P, BANK], F32, name="res", bufs=len(UNITS))
-            first, hf = UNITS[k]
+            res = keep.tile([P, BANK], F32, name=f"res{k}")
+            hf, first = PLAIN[k]
             rows = out[P * first : P * (first + 2), HALF * hf : HALF * (hf + 1)].rearrange("(g p) m -> p g m", p=P)
-            if k in sum_banks:
-                blocks = [slice(P * j, P * (j + 1)) for j in range(4)]
-                ps = bank(sum_banks[k][0], f"twice_out{k}", [P, BANK])
-                for block in blocks:
-                    for n, term in enumerate((step[k], answer[k], answer[k])):
-                        nc.tensor.matmul(
-                            ps[:, block], lhsT=term[:, block], rhs=ident[:], start=(n == 0), stop=(n == 2), is_transpose=True
-                        )
-                twice = ring.tile([P, BANK], F32, name="twice", bufs=2)
-                nc.scalar.copy(twice[:], ps[:])
-                ps = bank(sum_banks[k][1], f"twice_back{k}", [P, BANK])
-                for block in blocks:
-                    nc.tensor.transpose(ps[:, block], twice[:, block], ident[:])
-                nc.scalar.activation(res[:], ps[:], ACT.Copy, scale=0.5)
-                nc.sync.dma_start(out=rows, in_=res[:].rearrange("p (g m) -> p g m", m=HALF))
-                return
             for piece in pieces(k):
                 nc.vector.scalar_tensor_tensor(res[:, piece], step[k][:, piece], 0.5, answer[k][:, piece], ALU.mult, ALU.add)
                 nc.sync.dma_start(
@@ -415,40 +458,37 @@ def tile_list_fugue_imitation_gate_kernel(
                     in_=res[:, piece].rearrange("p (g m) -> p g m", m=HALF),
                 )
 
-        answer_bank = [2, 0, 1, 3, 7, 0, 1, 3]
-        gate_bank = [4, 5, 2, 6, 4, 5, 2, 6]
-        sum_banks = {0: (5, 1), 4: (7, 4)}
-        propose(0, answer_bank[0])
+        def turned_pair(k, banks):
+            turned_product(k, "minus_answer", banks[0], *wt_operand, -1.0)
+            turned_product(k, "gate", banks[1], *wg_operand, 0.5)
+
+        turned_pair(0, (2, 3))
         second_out(0, 7)
         second_out(1, 6)
-        for k in range(len(UNITS) + 1):
-            if k == 0:
-                second_back(0, 7)
-            if k == 1:
-                second_out(2, 6)
-            if k == 2:
-                second_out(3, 7)
-            if k + 1 < len(UNITS) and k != 3:
-                propose(k + 1, answer_bank[k + 1])
-            if k == 2:
-                second_back(1, 6)
-            if k < len(UNITS):
-                weigh(k, gate_bank[k])
+        second_back(0, 7)
+        plain_followers((0, 1), 0, 16384)
+        plain_followers((2, 3), 0, 18432)
+        plain_followers((4, 5), 0, 20480)
+        second_out(2, 6)
+        second_out(3, 7)
+        second_back(1, 6)
+        quantize_x(1)
+        plain_followers((6, 7), 0, 44544)
+        turned_pair(1, (4, 5))
+        turned_pair(2, (0, 1))
+        turned_pair(3, (2, 3))
+        for k, n in enumerate((7, 6, 4, 5)):
+            turned_terms(k, n)
+        for k in range(5):
+            if k < 4:
+                propose(k, 2 * (k % 2))
+                weigh(k, 2 * (k % 2) + 1)
                 follower(k, 0)
-            if k >= 1 and k not in (3, 4):
+            if k >= 1:
                 gated(k - 1)
-            if k < len(UNITS):
+            if k < 4:
                 follower(k, 1)
-            if k == 3:
-                x_code[1] = keep.tile([P, PASSES_2, HALF], U32, name="x_code1", tag="first_gate", align_bytes=64)
-                quantize_x(1)
-                propose(4, answer_bank[4])
-                for last_step in (gated, finish):
-                    last_step(2)
-                    last_step(3)
-            if k == len(UNITS) - 1:
-                finish(4)
-            if k == 2:
-                finish(0)
-            if k >= 2 and k not in (3, 4, 5):
+            if k >= 1:
                 finish(k - 1)
+        for k, n in enumerate((7, 6, 4, 5)):
+            turned_finish(k, n)

@@ -349,7 +349,7 @@ def tile_list_fugue_imitation_gate_kernel(
             turned[name, k] = keep.tile([P, 2, 2, P], F32, name=f"{name}{k}")
             nc.scalar.activation(turned[name, k][:].rearrange("m mb g p -> m (mb g p)"), ps[:], ACT.Tanh, scale=factor)
 
-        both_at = {0: 22528}
+        both_at = {0: 22528, 1: 46592}
 
         def turned_terms(k, n):
             hf, first = TURNED[k]

@@ -139,7 +139,8 @@ def tile_list_fugue_imitation_gate_kernel(
                 wg_pair[u][:, b, :, :], raw[:].rearrange("p j n -> p n j"), 1.0, 0.0, ALU.mult, ALU.add
             )
 
-        gain_word = keep.tile([P, PASSES_2, 4], F32, name="gain_word")
+        gain_word = laid.tile([P, PASSES_2, 4], F32, name="gain_word", offset=4608, align_bytes=64)
+        gain_last = laid.tile([P, 32], F32, name="gain_last", offset=28672 - 64, align_bytes=64)
         load_and_cast_wg(0, 0, "big0")
         load_w1("w1_last", range(0, 3), range(EARLY, ROW_TILES))
         load_scale_rows(w1_scale[1], w1_scales[:, :, BANK:H])
@@ -237,7 +238,7 @@ def tile_list_fugue_imitation_gate_kernel(
                 first_out((2, 3), 1)
 
         x_grouped = [
-            laid.tile([P, PASSES_2, 4 * HALF], BF16, name="x_grouped0", offset=26624, align_bytes=64),
+            keep.tile([P, PASSES_2, 4 * HALF], BF16, name="x_grouped0", align_bytes=64),
             laid.tile([P, PASSES_2, 4 * HALF], BF16, name="x_grouped1", offset=44544, align_bytes=64),
         ]
         x_code = [keep.tile([P, PASSES_2, HALF], U32, name=f"x_code{hf}", align_bytes=64) for hf in range(2)]
@@ -250,6 +251,15 @@ def tile_list_fugue_imitation_gate_kernel(
                 in_=x_grouped[hf][:].rearrange("p b m -> p (b m)"),
             )
 
+        nc.scalar.copy(gain_last[:, 0:4], gain_word[:, 1, :])
+        follow = {}
+
+        def plain_followers(tiles, hf, offset):
+            tile = laid.tile([P, len(tiles), HALF], F32, name=f"follow{tiles[0]}{hf}", offset=offset, align_bytes=64)
+            for g, i in enumerate(tiles):
+                nc.vector.tensor_copy(tile[:, g, :], h[i][:].indirect(pos2_sb[:, 16 * hf : 16 * (hf + 1)]))
+                follow[i] = tile[:, g, :]
+
         for tiles, n in (((4, 5), 2), ((6,), 3), ((7,), 7)):
             first_out(tiles, n)
         for b in range(PASSES_2):
@@ -261,9 +271,10 @@ def tile_list_fugue_imitation_gate_kernel(
                 nc.vector.tensor_tensor(
                     x_grouped[0][:, b, BANK * mb : BANK * (mb + 1)].rearrange("p (m e t) -> p m t e", e=2, t=4),
                     ps[:].rearrange("p t (m e) -> p m t e", e=2),
-                    gain_word[:, b, :].unsqueeze(1).unsqueeze(3).to_broadcast([P, P // 2, 4, 2]),
+                    (gain_last[:, 0:4] if (b, mb) == (1, 1) else gain_word[:, b, :]).unsqueeze(1).unsqueeze(3).to_broadcast([P, P // 2, 4, 2]),
                     ALU.mult,
                 )
+        plain_followers((0,), 0, 4608)
         quantize_x(0)
 
         last_second = [
@@ -320,14 +331,6 @@ def tile_list_fugue_imitation_gate_kernel(
                 x_grouped[1][:, b, :].bitcast(F32).rearrange("p (m e u) -> p m u e", e=2, u=2),
                 ps[:].rearrange("p u (m e) -> p m u e", e=2),
             )
-
-        follow = {}
-
-        def plain_followers(tiles, hf, offset):
-            tile = laid.tile([P, len(tiles), HALF], F32, name=f"follow{tiles[0]}{hf}", offset=offset, align_bytes=64)
-            for g, i in enumerate(tiles):
-                nc.vector.tensor_copy(tile[:, g, :], h[i][:].indirect(pos2_sb[:, 16 * hf : 16 * (hf + 1)]))
-                follow[i] = tile[:, g, :]
 
         turned = {}
 
@@ -427,7 +430,7 @@ def tile_list_fugue_imitation_gate_kernel(
         def follower(k, g):
             hf, first = PLAIN[k]
             if g == 0:
-                diff[k] = laid.tile([P, BANK], F32, name=f"diff{k}", offset=12288 + 2048 * (k % 2), align_bytes=64)
+                diff[k] = laid.tile([P, BANK], F32, name=f"diff{k}", offset=16384 + 2048 * (k % 2), align_bytes=64)
             nc.vector.tensor_tensor(
                 diff[k][:, HALF * g : HALF * (g + 1)],
                 h[first + g][:].indirect(pos2_sb[:, 16 * hf : 16 * (hf + 1)]),
@@ -441,7 +444,7 @@ def tile_list_fugue_imitation_gate_kernel(
             return [LOW, HIGH] if k == 3 else [slice(0, BANK)]
 
         def gated(k):
-            step[k] = laid.tile([P, BANK], F32, name=f"step{k}", offset=8192 + 2048 * (k % 2), align_bytes=64)
+            step[k] = laid.tile([P, BANK], F32, name=f"step{k}", offset=14336 + 6144 * (k % 2), align_bytes=64)
             for piece in pieces(k):
                 nc.vector.scalar_tensor_tensor(
                     step[k][:, piece], half_gate[k][:, piece], 1.0, diff[k][:, piece], ALU.add, ALU.mult
@@ -466,9 +469,7 @@ def tile_list_fugue_imitation_gate_kernel(
         second_out(0, 7)
         second_out(1, 6)
         second_back(0, 7)
-        plain_followers((0, 1), 0, 16384)
-        plain_followers((2, 3), 0, 18432)
-        plain_followers((4, 5), 0, 20480)
+        plain_followers((1, 2, 3, 4, 5), 0, 8192)
         second_out(2, 6)
         second_out(3, 7)
         second_back(1, 6)

@@ -53,17 +53,30 @@ def tile_list_fugue_imitation_gate_kernel(
         ident_bf16 = keep.tile([P, P], BF16, name="ident_bf16")
 
         nc.gpsimd.memset(tab_scale[0:112, :].bitcast(I32), 0)
-        gain_rows = keep.tile([P, P], F32, name="gain_rows")
+        gain_rows = keep.tile([P, BANK], F32, name="gain_rows")
         gain_col = keep.tile([P, ROW_TILES], F32, name="gain_col")
+        gain_word = laid.tile([P, PASSES_2, 4], F32, name="gain_word", offset=4608, align_bytes=64)
+        gain_last = laid.tile([P, 32], F32, name="gain_last", offset=28672 - 64, align_bytes=64)
         nc.vector.memset(zero_col[:], 0.0)
         nc.scalar.activation(zero_bias[:], zero_col[:], ACT.Gelu_apprx_tanh)
         nc.vector.memset(gain_rows[:], 0.0)
-        nc.scalar.dma_start(out=gain_rows[24:32, :], in_=gain.rearrange("(i p) -> i p", p=P))
+        nc.scalar.dma_start(out=gain_rows[24:26, :], in_=gain.rearrange("(b c) -> b c", b=PASSES_2))
         make_identity(nc, ident[:])
         make_identity(nc, ident_bf16[:])
-        ps = bank(7, "gain_turned", [P, P])
-        nc.tensor.transpose(ps[:], gain_rows[:], ident[:])
-        nc.scalar.activation(gain_col[:], ps[:, 24:32], ACT.Identity, bias=zero_bias[:])
+        ps = bank(7, "gain_turned", [P, 4, P])
+        for j in range(4):
+            nc.tensor.transpose(ps[:, j, :], gain_rows[:, P * j : P * (j + 1)], ident[:])
+        nc.scalar.activation(
+            gain_col[:].rearrange("p (b j) -> p b j", b=PASSES_2),
+            ps[:, :, 24:26].rearrange("p j b -> p b j"),
+            ACT.Identity,
+            bias=zero_bias[:],
+        )
+        ps = bank(6, "gain_dealt", [P, 4, P])
+        for t in range(4):
+            nc.tensor.transpose(ps[:, t, :], gain_rows[:, t:BANK:4], ident[:])
+        nc.scalar.copy(gain_word[:], ps[:, :, 24:26].rearrange("p t b -> p b t"))
+        nc.scalar.copy(gain_last[:, 0:4], ps[:, :, 25])
 
         w1_i32 = w1_words.bitcast(I32)
         tab_rows = tab_scales.bitcast(I32)
@@ -139,13 +152,10 @@ def tile_list_fugue_imitation_gate_kernel(
                 wg_pair[u][:, b, :, :], raw[:].rearrange("p j n -> p n j"), 1.0, 0.0, ALU.mult, ALU.add
             )
 
-        gain_word = laid.tile([P, PASSES_2, 4], F32, name="gain_word", offset=4608, align_bytes=64)
-        gain_last = laid.tile([P, 32], F32, name="gain_last", offset=28672 - 64, align_bytes=64)
         load_and_cast_wg(0, 0, "big0")
         load_w1("w1_last", range(0, 3), range(EARLY, ROW_TILES))
         load_scale_rows(w1_scale[1], w1_scales[:, :, BANK:H])
         load_and_cast_wg(0, 1, "big1")
-        nc.gpsimd.dma_start(out=gain_word[:], in_=gain.rearrange("(b p t) -> p b t", b=PASSES_2, t=4))
         load_and_cast_wg(1, 0, "big2")
         load_and_cast_wg(1, 1, "big0")
         wt_code = {}
@@ -179,7 +189,7 @@ def tile_list_fugue_imitation_gate_kernel(
             )
 
         def keep_rows(i, u):
-            if u == 0 and i in (1, 3):
+            if u == 0 and i in (1, 2, 3):
                 nc.vector.tensor_copy(h[i][:, BANK * u : BANK * (u + 1)], acc[i, u][:])
             else:
                 nc.scalar.copy(h[i][:, BANK * u : BANK * (u + 1)], acc[i, u][:])
@@ -251,7 +261,6 @@ def tile_list_fugue_imitation_gate_kernel(
                 in_=x_grouped[hf][:].rearrange("p b m -> p (b m)"),
             )
 
-        nc.scalar.copy(gain_last[:, 0:4], gain_word[:, 1, :])
         follow = {}
 
         def plain_followers(tiles, hf, offset):

@@ -324,7 +324,11 @@ def tile_list_fugue_imitation_gate_kernel(
             rows = ring.tile([P, 2, HALF], BF16, name="x_rows", bufs=2)
             ps = bank(n, f"out1{j}", [P, 2, 2 * P], BF16)
             for k in range(2):
-                nc.scalar.activation(rows[:, k, :], act[:, k, :], ACT.Copy, scale=gain_col[:, 2 * j + k : 2 * j + k + 1])
+                factor = gain_col[:, 2 * j + k : 2 * j + k + 1]
+                if j == 0:
+                    nc.gpsimd.tensor_scalar(rows[:, k, :], act[:, k, :], factor, 0.0, ALU.mult, ALU.add)
+                else:
+                    nc.scalar.activation(rows[:, k, :], act[:, k, :], ACT.Copy, scale=factor)
                 for mb in range(2):
                     nc.tensor.transpose(ps[:, mb, P * k : P * (k + 1)], rows[:, k, P * mb : P * (mb + 1)], ident_bf16[:])
             dst = x_turned[b][:, :, 2 * P * (j % 2) : 2 * P * (j % 2 + 1)]
@@ -478,12 +482,12 @@ def tile_list_fugue_imitation_gate_kernel(
         second_out(0, 7)
         second_out(1, 6)
         second_back(0, 7)
-        plain_followers((1, 2, 3, 4, 5), 0, 8192)
+        plain_followers((1, 2, 3, 4), 0, 8192)
         second_out(2, 6)
         second_out(3, 7)
         second_back(1, 6)
         quantize_x(1)
-        plain_followers((6, 7), 0, 44544)
+        plain_followers((5, 6, 7), 0, 43520)
         turned_pair(1, (4, 5))
         turned_pair(2, (0, 1))
         turned_pair(3, (2, 3))

@@ -149,7 +149,12 @@ def tile_list_fugue_imitation_gate_kernel(
             raw = keep.tile([P, 4, BANK], F32, name=f"wg_raw{u}{b}", tag=tag, align_bytes=64)
             nc.sync.dma_start(out=raw[:], in_=rows[:, :, BANK * u : BANK * (u + 1)])
             nc.gpsimd.tensor_scalar(
-                wg_pair[u][:, b, :, :], raw[:].rearrange("p j n -> p n j"), 1.0, 0.0, ALU.mult, ALU.add
+                wg_pair[u][:, b, :, :].rearrange("p (c e) j -> p c j e", e=2),
+                raw[:].rearrange("p j (c e) -> p c j e", e=2),
+                1.0,
+                0.0,
+                ALU.mult,
+                ALU.add,
             )
 
         load_and_cast_wg(0, 0, "big0")
@@ -326,7 +331,7 @@ def tile_list_fugue_imitation_gate_kernel(
             for k in range(2):
                 factor = gain_col[:, 2 * j + k : 2 * j + k + 1]
                 if j == 0:
-                    nc.gpsimd.tensor_scalar(rows[:, k, :], act[:, k, :], factor, 0.0, ALU.mult, ALU.add)
+                    nc.gpsimd.tensor_scalar(rows[:, k, :], act[:, k, :], factor, zero_col[:], ALU.mult, ALU.add)
                 else:
                     nc.scalar.activation(rows[:, k, :], act[:, k, :], ACT.Copy, scale=factor)
                 for mb in range(2):

from contextlib import ExitStack

import concourse.mybir as mybir
from concourse.masks import make_identity

K, H, T, S, M = 1536, 1024, 2048, 1024, 512
P = 128
BANK = 512
HALF = M // 2
PASSES_1 = K // 512
PASSES_2 = H // 512
ROW_TILES = H // P
FLOPS = 2 * K * H * S + 2 * 2 * H * H * M

F32 = mybir.dt.float32
BF16 = mybir.dt.bfloat16
I32 = mybir.dt.int32
U32 = mybir.dt.uint32
U16 = mybir.dt.uint16
U8 = mybir.dt.uint8
FP8X4 = mybir.dt.float8_e4m3fn_x4
FP4X4 = mybir.dt.float4_e2m1fn_x4
ACT = mybir.ActivationFunctionType
ALU = mybir.AluOpType

EARLY = 4
TURNED = [(0, 0), (0, 2), (0, 4), (0, 6)]
PLAIN = [(1, 0), (1, 2), (1, 4), (1, 6)]


def tile_list_fugue_imitation_gate_kernel(
    tc, tab_words, tab_scales, offs, pos1, pos2, w1_words, w1_scales, gain, wg, wt_words, wt_scales, out
):
    nc = tc.nc
    with ExitStack() as ctx:
        keep = ctx.enter_context(tc.tile_pool(name="keep", bufs=1))
        laid = ctx.enter_context(tc.tile_pool(name="laid", bufs=1))
        ring = ctx.enter_context(tc.tile_pool(name="ring", bufs=3))
        psum = ctx.enter_context(tc.psum_pool(name="psum", bufs=1))

        def bank(n, name, shape, dtype=F32):
            return psum.tile(shape, dtype, name=name, offset=2048 * n)

        offs_sb = keep.tile([P, S // 16], U16, name="offs_sb")
        pos1_sb = keep.tile([P, M // 16], U16, name="pos1_sb")
        pos2_sb = keep.tile([P, M // 16], U16, name="pos2_sb")
        tab_scale = keep.tile([P, T], U8, name="tab_scale", align_bytes=64)
        w1_scale = [keep.tile([P, PASSES_1, BANK], U8, name=f"w1_scale{g}", align_bytes=64) for g in range(2)]
        v_scale = [keep.tile([P, S], U8, name=f"v_scale{a}", align_bytes=64) for a in range(PASSES_1)]
        zero_col = keep.tile([P, 1], F32, name="zero_col")
        zero_bias = keep.tile([P, 1], F32, name="zero_bias")
        ident = keep.tile([P, P], F32, name="ident")
        ident_bf16 = keep.tile([P, P], BF16, name="ident_bf16")

        nc.gpsimd.memset(tab_scale[0:112, :].bitcast(I32), 0)
        gain_rows = keep.tile([P, BANK], F32, name="gain_rows")
        gain_col = keep.tile([P, ROW_TILES], F32, name="gain_col")
        gain_word = laid.tile([P, PASSES_2, 4], F32, name="gain_word", offset=4608, align_bytes=64)
        gain_last = laid.tile([P, 32], F32, name="gain_last", offset=28672 - 64, align_bytes=64)
        nc.vector.memset(zero_col[:], 0.0)
        nc.scalar.activation(zero_bias[:], zero_col[:], ACT.Gelu_apprx_tanh)
        nc.vector.memset(gain_rows[:], 0.0)
        nc.scalar.dma_start(out=gain_rows[24:26, :], in_=gain.rearrange("(b c) -> b c", b=PASSES_2))
        make_identity(nc, ident[:])
        make_identity(nc, ident_bf16[:])
        ps = bank(7, "gain_turned", [P, 4, P])
        for j in range(4):
            nc.tensor.transpose(ps[:, j, :], gain_rows[:, P * j : P * (j + 1)], ident[:])
        nc.scalar.activation(
            gain_col[:].rearrange("p (b j) -> p b j", b=PASSES_2),
            ps[:, :, 24:26].rearrange("p j b -> p b j"),
            ACT.Identity,
            bias=zero_bias[:],
        )
        ps = bank(6, "gain_dealt", [P, 4, P])
        for t in range(4):
            nc.tensor.transpose(ps[:, t, :], gain_rows[:, t:BANK:4], ident[:])
        nc.scalar.copy(gain_word[:], ps[:, :, 24:26].rearrange("p t b -> p b t"))
        nc.scalar.copy(gain_last[:, 0:4], ps[:, :, 25])

        w1_i32 = w1_words.bitcast(I32)
        tab_rows = tab_scales.bitcast(I32)
        tab_code = {}

        def load_tab(a):
            tab_code[a] = keep.tile([P, T], U32, name=f"tab_code{a}", tag=f"big{a}", align_bytes=64)
            nc.sync.dma_start(
                out=tab_code[a][:].bitcast(I32),
                in_=tab_words[a].rearrange("p t i -> p (t i)").bitcast(I32),
            )

        def load_w1(name, passes, tiles):
            tile = keep.tile([P, len(passes), 256 * len(tiles)], U8, name=name, align_bytes=64)
            nc.sync.dma_start(
                out=tile[:].bitcast(I32),
                in_=w1_i32[passes.start : passes.stop, :, 64 * tiles.start : 64 * tiles.stop].rearrange("a p c -> p a c"),
            )
            for a in passes:
                for i in tiles:
                    w1_code[a, i] = tile[:, a - passes.start, 256 * (i - tiles.start) : 256 * (i - tiles.start + 1)]

        def load_scale_rows(plane, rows):
            for r in range(4):
                nc.sync.dma_start(
                    out=plane[r:P:32, :, :].bitcast(I32),
                    in_=rows.bitcast(I32)[:, r:16:4, :].rearrange("a q c -> q a c"),
                )

        def move_scale_rows(a):
            for r in range(4):
                rows = slice(4 + r, P, 32) if a == 1 else slice(112 + r, P, 4)
                nc.sync.dma_start(out=v_scale[a][r:P:32, :].bitcast(I32), in_=v_scale[0][rows, :].bitcast(I32))

        w1_code = {}
        nc.sync.dma_start(offs_sb[:], offs)
        nc.sync.dma_start(out=tab_scale[112:128, :].bitcast(I32), in_=tab_rows[2])
        for q in (0, 2, 1, 3):
            nc.sync.dma_start(
                out=tab_scale[32 * q : 32 * q + 8, :].bitcast(I32), in_=tab_rows[0:2, 4 * q : 4 * q + 4, :]
            )
        load_tab(0)
        load_scale_rows(w1_scale[0], w1_scales[:, :, 0:BANK])
        load_w1("w1_first", range(0, 2), range(0, EARLY))
        load_tab(1)
        nc.vector.tensor_copy(v_scale[0][:], tab_scale[:].indirect(offs_sb[:]))
        move_scale_rows(1)
        load_tab(2)
        move_scale_rows(2)
        load_w1("w1_next", range(2, 3), range(0, EARLY))
        nc.sync.dma_start(pos1_sb[:], pos1)

        def column_pieces(a, u):
            return [slice(0, HALF), slice(HALF, BANK)] if (a, u) == (0, 0) else [slice(0, BANK)]

        v_code = {}
        for a in range(PASSES_1):
            for u in range(2):
                v_code[a, u] = keep.tile([P, BANK], U32, name=f"v_code{a}{u}", tag=f"v_code{a}{u}", align_bytes=64)
                for cols in column_pieces(a, u):
                    nc.vector.tensor_copy(
                        v_code[a, u][:, cols],
                        tab_code[a][:].indirect(offs_sb[:, 32 * u + cols.start // 16 : 32 * u + cols.stop // 16]),
                    )

        wg_pair = [laid.tile([P, PASSES_2, BANK, 4], BF16, name=f"wg_pair{u}", offset=8192 * (u + 1), align_bytes=64) for u in range(2)]

        def load_and_cast_wg(u, b, tag):
            rows = wg[512 * b : 512 * (b + 1), :].rearrange("(p j) n -> p j n", j=4)
            raw = keep.tile([P, 4, BANK], F32, name=f"wg_raw{u}{b}", tag=tag, align_bytes=64)
            nc.sync.dma_start(out=raw[:], in_=rows[:, :, BANK * u : BANK * (u + 1)])
            nc.gpsimd.tensor_scalar(
                wg_pair[u][:, b, :, :].rearrange("p (c e) j -> p c j e", e=2),
                raw[:].rearrange("p j (c e) -> p c j e", e=2),
                1.0,
                0.0,
                ALU.mult,
                ALU.add,
            )

        load_and_cast_wg(0, 0, "big0")
        load_w1("w1_last", range(0, 3), range(EARLY, ROW_TILES))
        load_scale_rows(w1_scale[1], w1_scales[:, :, BANK:H])
        load_and_cast_wg(0, 1, "big1")
        load_and_cast_wg(1, 0, "big2")
        load_and_cast_wg(1, 1, "big0")
        wt_code = {}

        def load_wt(u):
            wt_code[u] = keep.tile([P, PASSES_2, BANK], U32, name=f"wt_code{u}", align_bytes=64)
            words = wt_words.rearrange("a p c i -> p a (c i)").bitcast(I32)
            nc.sync.dma_start(out=wt_code[u][:].bitcast(I32), in_=words[:, :, BANK * u : BANK * (u + 1)])

        load_wt(0)
        wt_scale = keep.tile([P, PASSES_2, H], U8, name="wt_scale", align_bytes=64)
        load_scale_rows(wt_scale, wt_scales)
        load_wt(1)
        nc.sync.dma_start(pos2_sb[:], pos2)

        acc = {}
        h = [keep.tile([P, S], F32, name=f"h{i}") for i in range(ROW_TILES)]
        lead = {}

        def stage1_pass(i, u, a, cols=slice(0, BANK)):
            if a == 0 and cols.start == 0:
                acc[i, u] = bank((2 * i + u) % 8, f"acc{i}{u}", [P, BANK])
            nc.tensor.matmul_mx(
                out=acc[i, u][:, cols],
                lhsT=w1_code[a, i].bitcast(FP4X4),
                lhsT_scale=w1_scale[i // EARLY][:, a, P * (i % EARLY) : P * (i % EARLY + 1)],
                rhs=v_code[a, u][:, cols].bitcast(FP8X4),
                rhs_scale=v_scale[a][:, BANK * u + cols.start : BANK * u + cols.stop],
                start=(a == 0 and cols.start == 0),
                stop=(a == PASSES_1 - 1),
            )

        def keep_rows(i, u):
            if u == 0 and i in (1, 2, 3):
                nc.vector.tensor_copy(h[i][:, BANK * u : BANK * (u + 1)], acc[i, u][:])
            else:
                nc.scalar.copy(h[i][:, BANK * u : BANK * (u + 1)], acc[i, u][:])

        def leader(dst, i, halves):
            nc.vector.tensor_copy(dst, h[i][:].indirect(pos1_sb[:, 16 * halves[0] : 16 * (halves[-1] + 1)]))

        act_turned = [keep.tile([P, 2, 4, P], F32, name=f"act_turned{b}", align_bytes=64) for b in range(PASSES_2)]

        def first_out(tiles, n):
            ps = bank(n, f"out0{tiles[0]}", [P, 2, len(tiles) * P])
            for k, i in enumerate(tiles):
                for mb in range(2):
                    nc.tensor.transpose(ps[:, mb, P * k : P * (k + 1)], lead[i, 0][:, P * mb : P * (mb + 1)], ident[:])
            nc.scalar.activation(
                act_turned[tiles[0] // 4][:, :, :, 32 * (tiles[0] % 4) : 32 * (tiles[-1] % 4 + 1)].rearrange(
                    "m mb t p -> m mb p t"
                ),
                ps[:].rearrange("m mb (p t) -> m mb p t", t=4),
                ACT.Gelu_apprx_tanh,
            )

        for cols in column_pieces(0, 0):
            for i in range(EARLY):
                stage1_pass(i, 0, 0, cols)
        for a in range(PASSES_1):
            for u in range(2):
                for i in range(EARLY):
                    if (a, u) != (0, 0):
                        stage1_pass(i, u, a)
        for i in range(EARLY):
            keep_rows(i, 0)
        last_first = [
            keep.tile([P, HALF], F32, name="lead6_first"),
            laid.tile([P, HALF], F32, name="lead7_first", offset=2048, align_bytes=64),
        ]
        for i in range(ROW_TILES):
            if i >= EARLY:
                for u in range(2):
                    for a in range(PASSES_1):
                        stage1_pass(i, u, a)
                keep_rows(i, 0)
            keep_rows(i, 1)
            if i < 6:
                if i % 2 == 0:
                    pair = keep.tile([P, 2, M], F32, name=f"lead{i}")
                leader(pair[:, i % 2, :], i, [0, 1])
                for hf in range(2):
                    lead[i, hf] = pair[:, i % 2, HALF * hf : HALF * (hf + 1)]
                    lead[i - i % 2, "pair", hf] = pair[:, :, HALF * hf : HALF * (hf + 1)]
            else:
                leader(last_first[i - 6][:], i, [0])
                lead[i, 0] = last_first[i - 6][:]
            if i == 6:
                first_out((0, 1), 0)
                first_out((2, 3), 1)

        x_grouped = [
            keep.tile([P, PASSES_2, 4 * HALF], BF16, name="x_grouped0", align_bytes=64),
            laid.tile([P, PASSES_2, 4 * HALF], BF16, name="x_grouped1", offset=44544, align_bytes=64),
        ]
        x_code = [keep.tile([P, PASSES_2, HALF], U32, name=f"x_code{hf}", align_bytes=64) for hf in range(2)]
        x_scale = [keep.tile([P, PASSES_2, HALF], U8, name=f"x_scale{hf}", align_bytes=64) for hf in range(2)]

        def quantize_x(hf):
            nc.vector.quantize_mx(
                out=x_code[hf][:].rearrange("p b m -> p (b m)").bitcast(FP8X4),
                scales=x_scale[hf][:].rearrange("p b m -> p (b m)"),
                in_=x_grouped[hf][:].rearrange("p b m -> p (b m)"),
            )

        follow = {}

        def plain_followers(tiles, hf, offset):
            tile = laid.tile([P, len(tiles), HALF], F32, name=f"follow{tiles[0]}{hf}", offset=offset, align_bytes=64)
            for g, i in enumerate(tiles):
                nc.vector.tensor_copy(tile[:, g, :], h[i][:].indirect(pos2_sb[:, 16 * hf : 16 * (hf + 1)]))
                follow[i] = tile[:, g, :]

        for tiles, n in (((4, 5), 2), ((6,), 3), ((7,), 7)):
            first_out(tiles, n)
        for b in range(PASSES_2):
            act = act_turned[b]
            for mb in range(2):
                ps = bank([[4, 5], [0, 1]][b][mb], f"back0{b}{mb}", [P, 4, P])
                for t in range(4):
                    nc.tensor.transpose(ps[:, t, :], act[:, mb, t, :], ident[:])
                nc.vector.tensor_tensor(
                    x_grouped[0][:, b, BANK * mb : BANK * (mb + 1)].rearrange("p (m e t) -> p m t e", e=2, t=4),
                    ps[:].rearrange("p t (m e) -> p m t e", e=2),
                    (gain_last[:, 0:4] if (b, mb) == (1, 1) else gain_word[:, b, :]).unsqueeze(1).unsqueeze(3).to_broadcast([P, P // 2, 4, 2]),
                    ALU.mult,
                )
        plain_followers((0,), 0, 4608)
        quantize_x(0)

        last_second = [
            keep.tile([P, HALF], F32, name="lead6_second"),
            keep.tile([P, HALF], F32, name="lead7_second"),
        ]
        for i in (7, 6):
            leader(last_second[i - 6][:], i, [1])
            lead[i, 1] = last_second[i - 6][:]

        wg_code = [
            laid.tile([P, PASSES_2, BANK], U32, name=f"wg_code{u}", offset=24576 + 4096 * u, align_bytes=64)
            for u in range(2)
        ]
        wg_scale = [keep.tile([P, PASSES_2, BANK], U8, name=f"wg_scale{u}", align_bytes=64) for u in range(2)]
        for u in range(2):
            nc.vector.quantize_mx(
                out=wg_code[u][:].rearrange("p b n -> p (b n)").bitcast(FP8X4),
                scales=wg_scale[u][:].rearrange("p b n -> p (b n)"),
                in_=wg_pair[u][:].rearrange("p b n j -> p (b n j)"),
            )

        x_turned = {}

        def second_out(j, n):
            b = j // 2
            if j % 2 == 0:
                act = keep.tile([P, 2, HALF], F32, name=f"act{j}", tag="v_code21", align_bytes=64)
            else:
                act = laid.tile([P, 2, HALF], F32, name=f"act{j}", offset=2560, align_bytes=64)
            if j < 3:
                nc.scalar.activation(act[:], lead[2 * j, "pair", 1], ACT.Gelu_apprx_tanh)
            else:
                for k in range(2):
                    nc.scalar.activation(act[:, k, :], lead[2 * j + k, 1], ACT.Gelu_apprx_tanh)
            if j % 2 == 0:
                x_turned[b] = keep.tile([P, 2, BANK], BF16, name=f"x_turned{b}", align_bytes=64)
            rows = ring.tile([P, 2, HALF], BF16, name="x_rows", bufs=2)
            ps = bank(n, f"out1{j}", [P, 2, 2 * P], BF16)
            for k in range(2):
                factor = gain_col[:, 2 * j + k : 2 * j + k + 1]
                if j == 0:
                    nc.gpsimd.tensor_scalar(rows[:, k, :], act[:, k, :], factor, zero_col[:], ALU.mult, ALU.add)
                else:
                    nc.scalar.activation(rows[:, k, :], act[:, k, :], ACT.Copy, scale=factor)
                for mb in range(2):
                    nc.tensor.transpose(ps[:, mb, P * k : P * (k + 1)], rows[:, k, P * mb : P * (mb + 1)], ident_bf16[:])
            dst = x_turned[b][:, :, 2 * P * (j % 2) : 2 * P * (j % 2 + 1)]
            nc.scalar.copy(dst.bitcast(F32), ps[:].bitcast(F32))

        def second_back(b, n):
            words = x_turned[b][:].rearrange("p mb r -> p (mb r)").bitcast(F32)
            ps = bank(n, f"back1{b}", [P, 2, 2 * P])
            for mb in range(2):
                for u in range(2):
                    nc.tensor.transpose(ps[:, u, P * mb : P * (mb + 1)], words[:, 256 * mb + u : 256 * (mb + 1) : 2], ident[:])
            nc.scalar.copy(
                x_grouped[1][:, b, :].bitcast(F32).rearrange("p (m e u) -> p m u e", e=2, u=2),
                ps[:].rearrange("p u (m e) -> p m u e", e=2),
            )

        turned = {}

        def turned_product(k, name, n, code, scale, factor):
            hf, first = TURNED[k]
            cols = slice(P * (first % 4), P * (first % 4 + 2))
            ps = bank(n, f"{name}{k}_sum", [P, BANK])
            for b in range(PASSES_2):
                for mb in range(2):
                    nc.tensor.matmul_mx(
                        out=ps[:, HALF * mb : HALF * (mb + 1)],
                        lhsT=x_code[hf][:, b, P * mb : P * (mb + 1)].bitcast(FP8X4),
                        lhsT_scale=x_scale[hf][:, b, P * mb : P * (mb + 1)],
                        rhs=code(first // 4, b)[:, cols].bitcast(FP8X4),
                        rhs_scale=scale(first // 4, b)[:, cols],
                        start=(b == 0 and mb == 0),
                        stop=(b == PASSES_2 - 1 and mb == 1),
                    )
            turned[name, k] = keep.tile([P, 2, 2, P], F32, name=f"{name}{k}")
            nc.scalar.activation(turned[name, k][:].rearrange("m mb g p -> m (mb g p)"), ps[:], ACT.Tanh, scale=factor)

        both_at = {0: 22528, 1: 46592}

        def turned_terms(k, n):
            hf, first = TURNED[k]
            if k in both_at:
                both = laid.tile([P, 2, 2, P], F32, name=f"both{k}", offset=both_at[k], align_bytes=64)
            else:
                both = keep.tile([P, 2, 2, P], F32, name=f"both{k}")
            nc.gpsimd.tensor_tensor(both[:], turned["gate", k][:], turned["minus_answer", k][:], ALU.mult)
            turned["both", k] = both
            ps = bank(n, f"follow_turned{k}", [P, 2, 2, P])
            for g in range(2):
                for mb in range(2):
                    nc.tensor.transpose(ps[:, mb, g, :], follow[first + g][:, P * mb : P * (mb + 1)], ident[:])
            kept = keep.tile([P, 2, 2, P], F32, name=f"kept{k}")
            nc.vector.scalar_tensor_tensor(
                kept[:].rearrange("m mb g p -> m (mb g p)"),
                turned["gate", k][:].rearrange("m mb g p -> m (mb g p)"),
                -1.0,
                ps[:].rearrange("m mb g p -> m (mb g p)"),
                ALU.add,
                ALU.mult,
            )
            turned["kept", k] = kept

        def turned_finish(k, n):
            hf, first = TURNED[k]
            ps = bank(n, f"out_sum{k}", [P, 2, 2, P])
            for g in range(2):
                for mb in range(2):
                    for j, name in enumerate(("minus_answer", "both", "kept")):
                        nc.tensor.matmul(
                            ps[:, g, mb, :], lhsT=turned[name, k][:, mb, g, :], rhs=ident[:],
                            start=(j == 0), stop=(j == 2), is_transpose=True,
                        )
            res = keep.tile([P, BANK], F32, name=f"res_turned{k}")
            nc.scalar.activation(res[:], ps[:].rearrange("p g mb m -> p (g mb m)"), ACT.Copy, scale=-0.5)
            rows = out[P * first : P * (first + 2), HALF * hf : HALF * (hf + 1)].rearrange("(g p) m -> p g m", p=P)
            nc.scalar.dma_start(out=rows, in_=res[:].rearrange("p (g m) -> p g m", m=HALF))

        answer = {}
        half_gate = {}
        diff = {}
        step = {}

        def product(k, name, n, code, scale):
            hf, first = PLAIN[k]
            ps = bank(n, f"{name}{k}", [P, BANK])
            for b in range(PASSES_2):
                for g in range(2):
                    i = first + g
                    nc.tensor.matmul_mx(
                        out=ps[:, HALF * g : HALF * (g + 1)],
                        lhsT=code(i // 4, b)[:, P * (i % 4) : P * (i % 4 + 1)].bitcast(FP8X4),
                        lhsT_scale=scale(i // 4, b)[:, P * (i % 4) : P * (i % 4 + 1)],
                        rhs=x_code[hf][:, b, :].bitcast(FP8X4),
                        rhs_scale=x_scale[hf][:, b, :],
                        start=(b == 0 and g == 0),
                        stop=(b == PASSES_2 - 1 and g == 1),
                    )
            return ps

        wt_operand = (lambda u, b: wt_code[u][:, b, :], lambda u, b: wt_scale[:, b, BANK * u : BANK * (u + 1)])
        wg_operand = (lambda u, b: wg_code[u][:, b, :], lambda u, b: wg_scale[u][:, b, :])

        def propose(k, n):
            ps = product(k, "answer_sum", n, *wt_operand)
            answer[k] = laid.tile([P, BANK], F32, name=f"answer{k}", offset=32768 + 2048 * [0, 3, 1, 2][k], align_bytes=64)
            nc.scalar.activation(answer[k][:], ps[:], ACT.Tanh)

        def weigh(k, n):
            ps = product(k, "gate_sum", n, *wg_operand)
            half_gate[k] = keep.tile([P, BANK], F32, name=f"half_gate{k}")
            nc.scalar.activation(half_gate[k][:], ps[:], ACT.Tanh, scale=-0.5)

        def follower(k, g):
            hf, first = PLAIN[k]
            if g == 0:
                diff[k] = laid.tile([P, BANK], F32, name=f"diff{k}", offset=16384 + 2048 * (k % 2), align_bytes=64)
            nc.vector.tensor_tensor(
                diff[k][:, HALF * g : HALF * (g + 1)],
                h[first + g][:].indirect(pos2_sb[:, 16 * hf : 16 * (hf + 1)]),
                answer[k][:, HALF * g : HALF * (g + 1)],
                ALU.subtract,
            )

        LOW, HIGH = slice(0, HALF), slice(HALF, BANK)

        def pieces(k):
            return [LOW, HIGH] if k == 3 else [slice(0, BANK)]

        def gated(k):
            step[k] = laid.tile([P, BANK], F32, name=f"step{k}", offset=14336 + 6144 * (k % 2), align_bytes=64)
            for piece in pieces(k):
                nc.vector.scalar_tensor_tensor(
                    step[k][:, piece], half_gate[k][:, piece], 1.0, diff[k][:, piece], ALU.add, ALU.mult
                )

        def finish(k):
            res = keep.tile([P, BANK], F32, name=f"res{k}")
            hf, first = PLAIN[k]
            rows = out[P * first : P * (first + 2), HALF * hf : HALF * (hf + 1)].rearrange("(g p) m -> p g m", p=P)
            for piece in pieces(k):
                nc.vector.scalar_tensor_tensor(res[:, piece], step[k][:, piece], 0.5, answer[k][:, piece], ALU.mult, ALU.add)
                nc.sync.dma_start(
                    out=rows[:, piece.start // HALF : piece.stop // HALF, :],
                    in_=res[:, piece].rearrange("p (g m) -> p g m", m=HALF),
                )

        def turned_pair(k, banks):
            turned_product(k, "minus_answer", banks[0], *wt_operand, -1.0)
            turned_product(k, "gate", banks[1], *wg_operand, 0.5)

        turned_pair(0, (2, 3))
        second_out(0, 7)
        second_out(1, 6)
        second_back(0, 7)
        plain_followers((1, 2, 3, 4), 0, 8192)
        second_out(2, 6)
        second_out(3, 7)
        second_back(1, 6)
        quantize_x(1)
        plain_followers((5, 6, 7), 0, 43520)
        turned_pair(1, (4, 5))
        turned_pair(2, (0, 1))
        turned_pair(3, (2, 3))
        for k, n in enumerate((7, 6, 4, 5)):
            turned_terms(k, n)
        for k in range(5):
            if k < 4:
                propose(k, 2 * (k % 2))
                weigh(k, 2 * (k % 2) + 1)
                follower(k, 0)
            if k >= 1:
                gated(k - 1)
            if k < 4:
                follower(k, 1)
            if k >= 1:
                finish(k - 1)
        for k, n in enumerate((7, 6, 4, 5)):
            turned_finish(k, n)
